import numpy as np, ml_dtypes
CORES = [1,5,17,21,33,37,49,53]
N = 8
import mx_ref
BF = ml_dtypes.bfloat16
def gentries(a):
    return np.ascontiguousarray(a.reshape(8, 16, -1).transpose(0, 2, 1)).reshape(8, -1)
def gtable(e):
    e = np.asarray(e); return np.ascontiguousarray(e.reshape(8, -1, 16).transpose(0, 2, 1)).reshape(128, -1).astype(np.int32)
def gcols(t, e):
    v = np.concatenate([t.reshape(8, 16, -1, 4), np.zeros((8, 16, 1, 4), BF)], axis=2)
    return np.ascontiguousarray(np.stack([v[g][:, e[g]] for g in range(8)])).reshape(128, -1)
def tile(rs):
    return np.stack(rs, axis=2).reshape(128, -1).astype(BF)
def pick(q, e):
    c = np.concatenate([q[0].reshape(128, -1, 4), np.zeros((128, 1, 4), np.uint8)], axis=1); s = np.concatenate([q[1], np.ones((16, 1), np.uint8)], axis=1)
    return (np.ascontiguousarray(c[:, e].reshape(128, -1)), np.ascontiguousarray(s[:, e]))
def join(*qs):
    return (np.concatenate([q[0] for q in qs], axis=1), np.concatenate([q[1] for q in qs], axis=1))
def put(q, e, v):
    c, s = q[0].reshape(128, -1, 4).copy(), q[1].copy(); c[:, e] = v[0].reshape(128, -1, 4); s[:, e] = v[1]
    return (c.reshape(128, -1), s)
def pk(c, s):
    return (np.ascontiguousarray(c), mx_ref.live(s))
def emit(q):
    return q[0], q[1]
def packed(v, rng):
    q = [mx_ref.quantize(np.ascontiguousarray(v[r])) for r in range(N)]
    return np.stack([a for a, b in q]), np.stack([mx_ref.plane(b, rng) for a, b in q])
def values_of_codes():
    e, c = np.zeros((128, 128, 4), np.float32), np.zeros((128, 2, 4), np.uint8)
    e[np.arange(128), np.arange(128), 0] = 1
    c[:127, :, 0] = np.arange(256).reshape(2, 128).T[:127]
    return mx_ref.matmul(mx_ref.quantize(e.reshape(128, 512).astype(BF)), (c.reshape(128, 8), np.full((16, 2), 127, np.uint8))).T.reshape(-1).astype(np.float64)
CODE_VALUE, SCALE_VALUE = values_of_codes(), 2.0 ** (np.arange(256) - 127.0)
def decode(q):
    return (CODE_VALUE[q[0]].reshape(16, 8, -1, 4) * SCALE_VALUE[q[1]][:, None, :, None] + 0.0).reshape(128, -1).astype(np.float32)
def f(rng, *shape):
    return mx_ref.flush((rng.standard_normal(shape, dtype=np.float32) * np.exp2(rng.integers(-2, 3, shape[:-1] + (1,)))).astype(BF))
def wide(rng, *shape, cols=0):
    v = rng.standard_normal(shape, dtype=np.float32) * np.exp2(rng.integers(-12, 13, shape)).astype(np.float32)
    if cols: v *= np.repeat(np.exp2(rng.integers(-cols, cols + 1, shape[:-2] + (1, shape[-1] // 4))) * (rng.random(shape[:-2] + (1, shape[-1] // 4)) > 0.0625), 4, axis=-1).astype(np.float32)
    return mx_ref.flush(v.astype(BF))
C, T = 256, 96
STEPS = [1, 2, 4]
def big(v):
    v = v.astype(np.float32)
    v[np.abs(v) < np.float32(2.0 ** -16)] = 0
    return v.astype(BF)
def numbers_of(rng):
    return {"x": big(f(rng, N, 128, 4 * C)), "u": np.array(f(rng, N, 128, 512)), "v": np.array(f(rng, N, 128, 512))}
def lists(rng, a=None):
    if a is None: a = np.argsort(rng.random((N, 8, C // 8, 8)), axis=3)
    a = (a + 8 * np.arange(C // 8)[:, None]).reshape(N, 8, C)
    c = np.argsort(rng.random((N, 8, C)), axis=2)
    return {"p": np.stack([gtable(a[r]) for r in range(N)]), "h": np.stack([gtable(c[r]) for r in range(N)])}
def weights(rng, w):
    c, s = packed(np.ascontiguousarray(w).reshape(N, 128, 2048), rng)
    return {"wc": c, "ws": s}
def layers(rng, still=[]):
    w = big(f(rng, N, 128, 2048)).reshape(N, 8, 16, 4, 8, 16, 4)
    for i in still:
        w[:, :, i] = 0
        w[:, :, :, :, :, i] = 0
    return weights(rng, w)
def setup_inputs(rng):
    return {**numbers_of(rng), **lists(rng), **layers(rng)}
def setup_inputs_ties(rng):
    d = numbers_of(rng)
    x = d["x"].astype(np.float32).reshape(N, 8, 16, C, 4)
    x[:, :, 0] = 0
    x[:, :, 0, :, 0] = rng.integers(-2, 3, (N, 8, C))
    z = np.exp2(rng.integers(-14, -7, (N, 8, C, 32))) * (1 + (2 * rng.integers(0, 64, (N, 8, C, 32)) + 1) / 128) * rng.choice([-1.0, 1.0], (N, 8, C, 32))
    np.put_along_axis(z, rng.integers(0, 32, (N, 8, C, 1)), 1.96875 * rng.choice([-1.0, 1.0], (N, 8, C, 1)), axis=3)
    z = z * np.exp2(rng.integers(-2, 3, (N, 8, C, 1)))
    x[:, :, 8:] = z.reshape(N, 8, C, 8, 4).transpose(0, 1, 3, 2, 4)
    u = d["u"].reshape(N, 128, 128, 4)
    u[:, :, ::16] = 0
    o = rng.permutation(N)
    for r in range(N):
        for i in range(0, 128, 16): u[r, i, i, 0] = 0.0 if r == o[0] else -1.0 if r == o[1] else 1.0
    return {"x": x.reshape(N, 128, 4 * C).astype(BF), "u": u.reshape(N, 128, 512), "v": d["v"], **lists(rng), **layers(rng, [0, 8, 9, 10, 11, 12, 13, 14, 15])}
def setup_inputs_near(rng):
    d = numbers_of(rng)
    x = d["x"].astype(np.float32).reshape(N, 8, 16, C, 4)
    u = d["u"].reshape(N, 128, 128, 4)
    x[:, :, 0] = 0
    x[:, :, 8:] = 0
    u[:, :, ::16] = 0
    s = rng.integers(0, 16, (N, 8, C))
    k = rng.permutation(8) % 4
    for g in range(8):
        i = 16 * g
        if k[g] < 2:
            x[:, g, 0, :, 0] = 1
            x[:, g, 8] = ((s[:, g, :, None] >> np.arange(4)) & 1) * np.exp2(np.arange(4) - 23.0)
            x[:, g, 11, :, 0] = 2.0 ** -10
            c = 1.0 if k[g] == 0 else -2.0 ** -30
            u[:, i, i, 0] = c
            u[:, i + 8, i] = c
            u[:, i + 11, i, 0] = c
        else:
            x[:, g, 10, :, 0] = (1 + s[:, g] % 8 * 0.125) * 2.0 ** -30
            u[:, i + 10, i, 0] = 2.0 ** -30 if k[g] == 2 else -2.0 ** -30
            if k[g] == 3: x[np.arange(N), g, 10, rng.integers(0, C, N), 0] = 2.0 ** 30
    return {"x": x.reshape(N, 128, 4 * C).astype(BF), "u": u.reshape(N, 128, 512), "v": d["v"], **lists(rng), **layers(rng, [0, 8, 9, 10, 11, 12, 13, 14, 15])}
def setup_inputs_huge(rng):
    d = numbers_of(rng)
    o = rng.permutation(N)
    x = 0.6 + 0.4 * rng.random((N, 8, 16, C, 4))
    x[o == 0] = 0.875 + 0.25 * (x[o == 0] - 0.5)
    c = rng.choice([-1.0, 1.0], (N, 1, 1, C, 1))
    c[o % 2 == 0] = -1
    u = d["u"].reshape(N, 128, 128, 4)
    a = 1 - 0.1 * rng.random((N, 128, 8, 4))
    a[o == 0] = 1
    a = 2.0 ** 30 * a * (rng.permutation(8) % 2 * 2.0 - 1.0)[:, None]
    u[:, :, ::16] = a.astype(np.float32).astype(BF)
    w = np.zeros((N, 128, 4, 128, 4), np.float32)
    i = np.arange(128)
    for b in range(4): w[:, i, b, i, b] = -1
    return {"x": (2.0 ** 30 * x * c).astype(np.float32).reshape(N, 128, 4 * C).astype(BF), "u": u.reshape(N, 128, 512), "v": d["v"], **lists(rng), **weights(rng, w.astype(BF))}
def setup_inputs_caps(rng):
    d = numbers_of(rng)
    u = d["u"].reshape(N, 128, 128, 4)
    u[:, :, ::16] = 0
    n, t = C // 8, T // 8
    back = {8: [[1], [6, 7]], 4: [[1, 2], [0, 2, 3]]}[N]
    size = rng.permutation(np.array([[t, t], [t, t], [t + 1, t - 1], [t - 1, t + 1], [n, 0], [0, n], [t, n - t], [n - t, t]]))
    a = np.zeros((N, 8, n, 8), int) + np.arange(8)
    for g in range(8):
        o = rng.permutation(n)
        i, j = int(size[g, 0]), int(size[g, 0] + size[g, 1])
        for r in back[0]: a[r, g, o[:i]] = np.arange(7, -1, -1)
        for r in back[1]: a[r, g, o[i:j]] = np.arange(7, -1, -1)
        for r in range(N): a[r, g, o[j:]] = np.array([7, 5, 6, 3, 4, 1, 2, 0] if r % 2 else [1, 0, 3, 2, 5, 4, 7, 6])
    return {"x": d["x"], "u": u.reshape(N, 128, 512), "v": d["v"], **lists(rng, a), **layers(rng)}
def setup_inputs_spread(rng):
    d = setup_inputs(rng)
    d["x"] = big(wide(rng, N, 128, 4 * C, cols=6))
    return d
def check_inputs(d):
    b = []
    for k in ("x", "u", "v"):
        a = np.abs(d[k].astype(np.float32))
        if not (np.isfinite(a).all() and ((a == 0) | (a >= 2.0 ** -30) & (a <= 2.0 ** 30)).all()): b.append("a value of " + k)
    none, least, most = [emit(mx_ref.quantize(np.full((128, 16), k, np.float32).astype(BF)))[1][0, 0] for k in (0.0, 2.0 ** -30, 2.0 ** 30)]
    for r in range(N):
        if (np.sort(gentries(d["p"][r]).reshape(8, -1, 8), axis=2).reshape(8, C) != np.arange(C)).any(): b.append("p: a block that doesn't hold its letters")
        if (np.sort(gentries(d["h"][r]), axis=1) != np.arange(C)).any(): b.append("h: a group that doesn't name every column once")
        if ((d["wc"][r] == 0x7F) | (d["wc"][r] == 0xFF)).any(): b.append("wc: a code that is no number")
        s = mx_ref.live(d["ws"][r])
        if ((s != none) & ((s < least) | (s > most))).any(): b.append("ws: a scale out of range")
    return b
def meet(a, b):
    a, b = a.reshape(8, -1, 8), np.argsort(b.reshape(8, -1, 8), axis=2)
    up = np.arange(8)[:, None] < np.arange(8)
    k = up & ((a[:, :, :, None] > a[:, :, None, :]) | (b[:, :, :, None] < b[:, :, None, :]))
    for i in range(8): k = k | (k[:, :, :, i:i + 1] & k[:, :, i:i + 1, :])
    return (np.sum(k, axis=2) + np.sum(up & ~k, axis=3)).reshape(8, C) + np.arange(C) // 8 * 8
def reference(x, u, v, p, h, wc, ws):
    qu = [mx_ref.quantize(u[r]) for r in range(N)]
    lay = [pk(wc[r], ws[r]) for r in range(N)]
    now = [x[r] for r in range(N)]
    word = [gentries(p[r]) for r in range(N)]
    home = [gentries(h[r]) for r in range(N)]
    for step in STEPS:
        for r in range(N):
            s = mx_ref.matmul(qu[r], mx_ref.quantize(now[r]))[::16] + np.float32(0.0)
            s = np.take_along_axis(s, np.take_along_axis(home[r], word[r], axis=1), axis=1).reshape(8, -1, 2)
            a = word[r].reshape(8, -1, 2)
            word[r] = np.where(s[:, :, :1] < s[:, :, 1:], a[:, :, ::-1], a).reshape(8, C)
        m = [None] * N
        for r in range(N):
            e = r ^ step
            if r < e:
                pos = meet(word[r], word[e])
                m[r] = m[e] = np.argsort(pos, axis=1)
                word[r], word[e] = np.take_along_axis(word[r], m[r], axis=1), np.take_along_axis(pos, word[e], axis=1)
        made, slot, sent = [], [], []
        for r in range(N):
            z = gcols(now[r], np.take_along_axis(home[r], word[r], axis=1))
            q = mx_ref.quantize(z)
            made.append(tile([mx_ref.matmul(pick(lay[r], np.arange(128 * b, 128 * b + 128)), q) * np.float32(0.03125) + z[:, b::4].astype(np.float32) for b in range(4)]))
            moved = m[r] != np.arange(C)
            o = np.argsort(~moved, axis=1, kind="stable")[:, :T]
            e = np.where(np.take_along_axis(moved, o, axis=1), o, -1)
            k = np.full((8, C + 1), -1)
            np.put_along_axis(k, np.where(e < 0, C, e), np.zeros((8, 1), int) + np.arange(T), axis=1)
            slot.append(k[:, :C])
            sent.append(mx_ref.quantize(gcols(made[r], e)))
        for r in range(N):
            came = gcols(decode(sent[r ^ step]).astype(BF), slot[r]).astype(np.float32)
            own = made[r].astype(np.float32)
            met = np.repeat(np.repeat(slot[r] >= 0, 16, axis=0), 4, axis=1)
            now[r] = np.where(met, (own + came) * np.float32(0.5), own).astype(BF)
    y, op = np.zeros((N, 128, C), np.float32), np.zeros((N, 8, C), np.float32)
    oc, osc = np.zeros((N, 128, 4 * C), np.uint8), np.zeros((N, 16, C), np.uint8)
    for r in range(N):
        q = mx_ref.quantize(now[r])
        y[r] = mx_ref.matmul(mx_ref.quantize(v[r]), q)
        op[r] = word[r]
        oc[r], osc[r] = emit(q)
    return {"y": y, "op": op, "oc": oc, "osc": osc}

@@ -1,0 +1,627 @@
+from concourse.mybir import dt, AluOpType, AxisListType, ActivationFunctionType
+
+F32, BF, I32, U16, U8, X4 = "float32", "bfloat16", "int32", "uint16", "uint8", "float8_e4m3fn_x4"
+STEPS = [1, 2, 4]
+NT = 96
+YS = 256 + NT
+OPT = {"gp": 14, "vp": 16, "s1": 22}
+
+D1 = [(2, 3), (1, 3), (0, 3), (1, 2), (0, 2), (0, 3), (0, 1), (0, 0)]
+D0 = [(0, 0), (1, 2), (0, 1), (0, 0), (0, 1), (2, 3), (0, 0), (0, 0)]
+A_SLOT = [7, 6, 4, 2, 5, 7, 3, 1, 7, 0, 7]
+A_FROM = [0, 1, 2, 3, 3, 1, 2, 3, 2, 3, 3]
+ENDS = [4, 7, 9, 10]
+STARTS = [0, 5, 8, 10, 11, 13]
+B_FROM = [3, 2, 1, 0, 0, 2, 1, 0, 1, 0, 0, 0, 0, 0, 0, 0]
+B_SLOT = [7, 0, 1, 2, 5, 7, 3, 4, 7, 6, 7, 7, 7, 7, 7, 7]
+INTRA = [[(6, -1), (4, -1), (12, -1)], [(6, 1), (1, -1), (13, -1)], [(4, 1), (0, -1), (13, 1)], [(1, 1), (0, 1), (12, 1)]]
+SHIFTS = [(0, 255), (8, 15), (12, 15), (16, 15), (20, 15)]
+
+
+def pos_term(e, t):
+    h, x = e // 4, e % 4
+    if t < 4:
+        return (160 + 16 * x + ENDS[3 - t], -1) if h == 0 else (160 + 16 * t + ENDS[3 - x], 1)
+    if t < 6:
+        return (8 * h + INTRA[x][t - 4][0], INTRA[x][t - 4][1])
+    if t == 6:
+        return (32 + 16 * h + INTRA[x][2][0], INTRA[x][2][1])
+    return (7, 7 - e)
+
+
+def tables():
+    R = range(16)
+    pos = [[pos_term(2 * c + r // 8, r % 8)[0] for r in R] for c in range(4)]
+    f = [[pos[0], [r // 4 for r in R], [4 + r % 4 for r in R], B_FROM, A_SLOT + [2, 5, 3, 7, 7]],
+         [pos[1], [D1[r % 8][0] + 4 * (r // 8) for r in R], [D1[r % 8][1] + 4 * (r // 8) for r in R],
+          [1 if r % 8 in (4, 5, 7) else 4 for r in R], A_SLOT + [10, 13, 11, 7, 7]],
+         [pos[2], [D0[r % 8][0] + 4 * (r // 8) for r in R], [D0[r % 8][1] + 4 * (r // 8) for r in R],
+          [6 * (r % 2) + 2 * (r // 2) if r < 6 else 0 for r in R], [1] * 11 + [0] * 5],
+         [pos[3], A_FROM + [8] * 5, [0] * 16, [0] * 16, [8 + s for s in B_SLOT]]]
+    out = [sum(f[k][t][r] << SHIFTS[t][0] for t in range(5)) for k in range(4) for r in R]
+    row = ENDS + [0 if r in STARTS else 1 for r in R] + [pos_term(j // 8, j % 8)[1] + 8 for j in range(64)] + [0]
+    return out + [sum(row[5 * k + t] << SHIFTS[t][0] for t in range(5)) for k in range(17)]
+
+
+PACKS = tables()
+NP = len(PACKS)
+TABS = {}
+_at = [0]
+for _n, _w in (("rj", 6), ("ri", 6), ("ai", 8), ("ag", 8), ("bi", 8), ("bg", 8), ("pp", 8), ("p1e", 8), ("p2", 8), ("pe", 2),
+               ("p32", 2), ("p1", 8), ("p3", 8), ("pr", 4), ("pl", 2), ("rep", 8), ("pu", 8)):
+    TABS[_n] = (_at[0], _w)
+    _at[0] += _w
+NTF = TABS["pe"][0] + 1
+
+_B = {
+    "x0": (1024, BF), "xs": (1024, BF), "xp": (1024, BF), "zt": (1024, BF), "z32": (1024, BF), "yw": (4 * YS, BF),
+    "ft": (512, BF), "f16": (4 * NT, BF), "ut": (512, BF), "vt": (512, BF), "et": (2048, BF), "k16": (512, BF),
+    "qa": (3 * NT + 256, X4), "sa": (3 * NT + 256, U8), "qx": (256, X4), "sx": (256, U8), "qz": (256, X4), "sz": (256, U8),
+    "qf": (384, X4), "sf": (384, U8), "qu": (128, X4), "su": (128, U8), "qu2": (128, X4), "su2": (128, U8),
+    "qv": (128, X4), "sv": (128, U8), "qw": (512, X4), "sw": (512, U8), "qe": (512, X4), "se": (512, U8),
+    "ssb": (256, F32), "ysb": (256, F32), "g1": (128, F32), "fr": (128, BF), "fl": (144, BF),
+    "phi": (64, I32), "phf": (64, F32), "pht": (64, F32), "wh": (32, BF), "absb": (32, BF), "dd": (32, BF), "dx": (32, F32),
+    "bx": (96, F32), "px": (32, F32), "wp": (96, BF), "vs": (48, BF), "wl": (48, BF), "w0": (32, F32), "vb": (32, F32),
+    "dh": (128, BF), "dw": (128, BF),
+    "dt_": (128, BF), "nq": (128, BF), "hs": (144, BF), "ls": (144, BF), "pq": (144, BF), "pr": (128, BF), "eq": (128, BF),
+    "eb": (128, BF), "e4": (64, BF), "p4": (64, BF), "s4": (64, BF), "bs": (144, BF), "ks": (128, BF),
+    "go": (96, BF), "ow": (96, BF), "ob": (96, F32), "oa": (96, F32), "gp": (96, F32), "kk": (112, BF), "frc": (96, BF),
+    "cw": (288, BF), "ga": (128, BF), "gb": (128, BF), "pa": (128, BF), "pw": (128, BF), "ra": (128, BF), "r8": (128, BF),
+    "mv": (16, F32), "um": (16, F32), "loc": (16, F32), "t1": (16, F32), "t2": (16, F32), "t3": (16, F32),
+    "cm": (32, F32), "ct": (32, F32), "pre": (1, F32), "m32": (32, F32), "ma": (64, F32), "cu": (16, F32),
+    "sg": (16, F32), "xd": (32, F32), "xt": (32, F32), "er": (816, BF), "e2": (192, BF), "opf": (16, F32),
+    "uz": (16, U16), "ue": (8, U16), "uo": (8, U16), "us": (16, U16), "uf": (16, U16), "ux": (16, U16), "tab": (_at[0], U16),
+    "tf": (NTF, F32), "pi": (4, I32), "ci": (8, I32), "col": (24, F32), "rows": (48, F32), "jr": (256, BF), "kr": (128, BF),
+    "lr": (128, BF), "mi": (32, I32), "c16": (48, F32), "cr": (128, BF), "pk": (NP, F32), "pki": (21, I32),
+    "rwi": (105, I32), "rw": (105, F32), "dg": (256, F32), "z1": (1, F32),
+}
+SCRATCH = {n: ("sbuf", [128, w], d) for n, (w, d) in _B.items()}
+for _i in range(8):
+    SCRATCH["ps%d" % _i] = ("psum", [128, 512], F32)
+POOL = {"v": 54, "s": 36, "t": 16, "g": 12, "d": 22}
+SEMAPHORES = ([k + str(i) for k, n in POOL.items() for i in range(n)] + ["sent", "base"] + ["w%d_" % i for i in range(3)]
+              + ["f%d_" % i for i in range(3)])
+
+
+def emit(g, T, ops):
+    qs = {"v": g.vector, "s": g.scalar, "t": g.tensor, "g": g, "y": g.sync}
+    masks = {}
+
+    def mask(a):
+        if a not in masks:
+            masks[a] = sum(1 << c for c in range(a[1], a[2], a[3]))
+        return masks[a]
+    seen, known, at, waits, signals = {}, {k: 0 for k in qs}, [], [], set()
+    for n, o in enumerate(ops):
+        deps = set(o["after"])
+        acc = [(a, False) for a in o["r"]] + [(a, True) for a in o["w"]]
+        for a, wr in acc:
+            ps = a[0][:2] == "ps"
+            for m, mk, w2, q2 in seen.get(a[0], []):
+                if (ps and (wr or w2 or q2 != o["q"])) or (not ps and (wr or w2) and mk & mask(a)):
+                    deps.add(m)
+        for a, wr in acc:
+            seen.setdefault(a[0], []).append((n, mask(a), wr, o["q"]))
+        ws = []
+        if o["q"] is not None:
+            for m in sorted(deps, reverse=True):
+                if not known[o["q"]] >> m & 1:
+                    ws.append(m)
+                    signals.add(m)
+                    known[o["q"]] |= at[m] | 1 << m
+        at.append(known[o["q"]] if o["q"] is not None else 0)
+        waits.append(ws)
+    used, holder, sem = {k: 0 for k in POOL}, {}, {}
+    for n, o in enumerate(ops):
+        if o["q"] is None:
+            sem[n] = o["sem"]
+            continue
+        ws = list(waits[n])
+        if n in signals:
+            k = "d" if o["dma"] else o["q"]
+            name = k + str(used[k] % POOL[k])
+            step = 16 if o["dma"] else 1
+            sem[n] = (name, step * (used[k] // POOL[k] + 1), step)
+            used[k] += 1
+            if name in holder and not at[n] >> holder[name] & 1:
+                ws.append(holder[name])
+            holder[name] = n
+        for m in ws:
+            qs[o["q"]].wait_ge(T.sem[sem[m][0]], sem[m][1])
+        if o["fn"] is not None:
+            i = o["fn"](qs[o["q"]])
+            if n in signals:
+                i.then_inc(T.sem[sem[n][0]], sem[n][2])
+
+
+def rank_program(g, core, T, topo):
+    rank = T.rank_of(core)
+    if rank is None:
+        return
+    Op, Act = AluOpType, ActivationFunctionType
+    ops = []
+
+    def A(n, lo=0, hi=None, st=1):
+        if hi is None:
+            hi = SCRATCH[n][1][1]
+        return (n, lo, hi, st)
+
+    def tab(n, a=0, b=None, st=1, buf="tab"):
+        return A(buf, TABS[n][0] + a, TABS[n][0] + (TABS[n][1] if b is None else b), st)
+
+    def tf(n, a=0, b=None, st=1):
+        return tab(n, a, b, st, "tf")
+
+    def G(win, off):
+        return ("*", win, off)
+
+    def col(k):
+        return A("col", k, k + 1)
+
+    def one(n, k):
+        return A(n, k, k + 1)
+
+    def ap(a):
+        if not isinstance(a, tuple):
+            return a
+        if a[0] == "*":
+            return ap(a[1]).indirect(ap(a[2]))
+        return T[a[0]][:, a[1]:a[2]:a[3]] if a[3] != 1 else T[a[0]][:, a[1]:a[2]]
+
+    def rec(q, fn, outs, ins, dma=False, after=(), sem=None):
+        r, w = [], []
+        for a in ins:
+            if isinstance(a, tuple):
+                r += [a[1], a[2]] if a[0] == "*" else [a]
+        for a in outs:
+            if a[0] == "*":
+                w.append(a[1])
+                r.append(a[2])
+            else:
+                w.append(a)
+        ops.append({"q": q, "fn": fn, "r": r, "w": w, "dma": dma, "after": list(after), "sem": sem})
+        return len(ops) - 1
+
+    def tt(o, a, b, op):
+        rec("v", lambda e: e.tensor_tensor(ap(o), ap(a), ap(b), op), [o], [a, b])
+
+    def ts(o, a, s1, op0, s2=None, op1=None):
+        if op1 is None:
+            rec("v", lambda e: e.tensor_scalar(ap(o), ap(a), ap(s1), None, op0), [o], [a, s1])
+        else:
+            rec("v", lambda e: e.tensor_scalar(ap(o), ap(a), ap(s1), ap(s2), op0, op1), [o], [a, s1, s2])
+
+    def cp(o, a, q="v", scale=None):
+        if q == "s":
+            if scale is None:
+                rec("s", lambda e: e.activation(ap(o), ap(a), Act.Copy), [o], [a])
+            else:
+                rec("s", lambda e: e.activation(ap(o), ap(a), Act.Copy, scale=scale), [o], [a])
+        elif scale is None:
+            rec("v", lambda e: e.tensor_copy(ap(o), ap(a)), [o], [a])
+        else:
+            ts(o, a, scale, Op.mult)
+
+    def af(o, a, scale=1.0, bias=0.0, func=None):
+        f = Act.Identity if func is None else func
+        rec("s", lambda e: e.activation(ap(o), ap(a), f, bias=ap(bias), scale=ap(scale)), [o], [a, scale, bias])
+
+    def ms(o, c):
+        rec("v", lambda e: e.memset(ap(o), c), [o], [])
+
+    def scan(o, d0, d1, op0, op1):
+        rec("v", lambda e: e.tensor_tensor_scan(ap(o), ap(d0), ap(d1), 0.0, op0, op1), [o], [d0, d1])
+
+    def tr(o, a):
+        rec("v", lambda e: e.transpose(ap(o), ap(a)), [o], [a])
+
+    def iota(o, pat, base, cm):
+        if SCRATCH[o[0]][2] == I32:
+            rec("g", lambda e: e.iota(ap(o), pat, base, cm), [o], [])
+        else:
+            rec("g", lambda e: e.iota(ap(o), pat, base, cm, allow_small_or_imprecise_dtypes=True), [o], [])
+
+    def quant(q, s, lo, n, a):
+        o1, o2 = A(q, lo, lo + n), A(s, lo, lo + n)
+        rec("v", lambda e: e.quantize_mx(ap(o1), ap(o2), ap(a)), [o1, o2], [a])
+
+    def mm(ps, wq, ws_, wlo, xq, xs_, xlo, n):
+        o = A(ps, 0, n)
+        a = [A(wq, wlo, wlo + 128), A(ws_, wlo, wlo + 128), A(xq, xlo, xlo + n), A(xs_, xlo, xlo + n)]
+        rec("t", lambda e: e.matmul_mx(ap(o), ap(a[0]), ap(a[1]), ap(a[2]), ap(a[3]), True, True), [o], a)
+
+    def load(q, o, src, codes=False):
+        rec(q, lambda e: e.dma_start(ap(o).bitcast(dt.uint8) if codes else ap(o), src), [o], [], dma=True)
+
+    stores = []
+
+    def store(q, dst, src, a):
+        stores.append(rec(q, lambda e: e.dma_start(dst, src), [], [a], dma=True))
+
+    sent = [0]
+
+    def send(peer, dst, src, sem, codes=False):
+        rid, pid = topo.addr(peer)[0], topo.addr(peer)[1]
+        m = topo.mask(core, peer)
+        view = (lambda a: ap(a).bitcast(dt.uint8)) if codes else ap
+        rec("g", lambda e: e.remote_dma(view(dst), view(src), T.sem[sem], T.sem.sent, pid, rid, m), [], [src])
+        sent[0] += len(topo.engines(core, peer))
+
+    def arrive(peer, outs, sem, writes):
+        rec(None, None, outs, [], sem=(sem, writes * len(topo.engines(peer, core))))
+
+    left = [rank < rank ^ s for s in STEPS]
+
+    load("y", A("phi", 0, 16), T.p[:])
+    load("s", A("phi", 16, 32), T.p[:])
+    load("y", A("phi", 32, 48), T.h[:])
+    load("s", A("phi", 48, 64), T.h[:])
+    load("y", A("ut"), T.u[:])
+    load("s", A("x0", 0, 512), T.x[:, 0:512])
+    load("y", A("x0", 512, 1024), T.x[:, 512:1024])
+    load("y", A("qw"), T.wc[:], codes=True)
+    load("y", A("sw"), T.ws[:])
+    load("y", A("vt"), T.v[:])
+
+    cols = [(0, 0, 15), (0, 0, 7), (0, 3, 1), (0, 0, 31), (2, 0, 255), (1, 0, 112), (2, 0, 48)]
+
+    def packs_s(k0, k1):
+        for k in range(k0, k1):
+            af(one("pk", k), A("z1"), 0.0, float(PACKS[k]))
+
+    nv, ng = OPT["vp"], OPT["gp"]
+    s1 = nv + ng + OPT["s1"]
+    a8, a16, a64, j16 = A("rows", 0, 16, 2), A("rows", 16, 24), A("rows", 24, 32), A("jr", 0, 256, 16)
+    iota(A("pi", 0, 1), [[0, 1]], 0, 1)
+    iota(A("mi", 0, 16), [[1, 16]], 128, -1)
+    iota(A("pi", 2, 3), [[0, 1]], 0, 16)
+    iota(A("pi", 1, 2), [[0, 1]], 0, 8)
+    iota(A("rows", 0, 16), [[8, 2], [0, 8]], 0, 0)
+    iota(A("jr"), [[1, 256]], 0, 0)
+    iota(A("lr"), [[0, 16], [1, 8]], 0, 0)
+    if not left[0]:
+        iota(A("kr"), [[0, 2], [1, 8], [0, 8]], 0, 0)
+    for k in range(nv, nv + ng):
+        iota(one("pk", k), [[0, 1]], PACKS[k], 0)
+    ms(A("z1"), 0.0)
+    for k in range(nv - 6):
+        ms(one("pk", k), float(PACKS[k]))
+    packs_s(nv + ng, s1)
+    ts(A("mi", 16, 32), A("mi", 0, 16), 15, Op.bitwise_and)
+    for k, (src, sh, an) in enumerate(cols):
+        if sh:
+            ts(one("ci", k), one("pi", src), sh, Op.logical_shift_right, an, Op.bitwise_and)
+        else:
+            ts(one("ci", k), one("pi", src), an, Op.bitwise_and)
+    ts(A("c16", 16, 32), A("mi", 16, 32), 0.0, Op.is_equal, 32.0, Op.mult)
+    ts(A("c16", 32, 48), A("mi", 16, 32), 1.0, Op.is_equal, -16.0, Op.mult)
+    cp(A("col", 0, 7), A("ci", 0, 7))
+    ms(A("absb", 16, 32), 0.0)
+    tt(A("c16", 0, 16), A("c16", 16, 32), A("c16", 32, 48), Op.add)
+    ts(col(13), col(0), 15.0, Op.not_equal, 16.0, Op.mult)
+    ts(A("absb", 0, 16), A("rows", 0, 16), col(4), Op.add)
+    ts(tab("p32"), A("jr", 0, 64, 32), col(3), Op.add)
+    ts(tab("rep"), A("jr", 0, 8), 0.0, Op.mult, col(0), Op.add)
+    cp(tab("pu"), A("jr", 0, 128, 16))
+    ts(tab("p1"), a8, col(1), Op.add)
+    ts(tab("p3"), A("jr", 0, 16, 2), col(2), Op.add)
+    cp(A("phf"), A("phi"))
+    tt(col(10), col(3), col(0), Op.subtract)
+    tr(A("pht"), A("phf"))
+    for k in range(nv - 6, nv - 4):
+        ms(one("pk", k), float(PACKS[k]))
+    af(a64, a8, 8.0)
+    af(col(15), col(13), -1.0)
+    af(A("r8"), A("lr"), func=Act.Sign)
+    af(A("ks", 0, 128, 2), A("lr", 0, 128, 2), 1.0, col(13))
+    af(A("ks", 1, 128, 2), A("lr", 1, 128, 2), 1.0, col(15))
+    cp(A("cr"), G(A("c16", 0, 16), tab("rep")), "s")
+
+    def lists_of_pairs():
+        cp(A("uo"), A("hs", 16, 129, 16))
+        cp(A("ue"), A("hs", 8, 129, 16))
+
+    def prepare(rd, lo, hi):
+        o = 32 * rd
+        tt(A("dx", lo, hi, 2), A("wh", lo + 1, hi, 2), A("wh", lo, hi, 2), Op.subtract)
+        tt(A("dx", lo + 1, hi, 2), A("wh", lo, hi, 2), A("wh", lo + 1, hi, 2), Op.subtract)
+        ts(A("xd", lo, hi), A("dx", lo, hi), col(13), Op.mult)
+        tt(A("bx", o + lo, o + hi), A("xd", lo, hi), A("wh", lo, hi), Op.add)
+
+    def prepare_right():
+        tt(A("eq"), G(A("wh", 0, 16), tab("p1")), A("kr"), Op.is_equal)
+        tt(A("pr"), A("eq"), A("ks"), Op.mult)
+        tt(A("e4"), A("eq", 0, 128, 2), A("eq", 1, 128, 2), Op.subtract)
+        scan(A("bs", 1, 129), A("r8"), A("pr"), Op.mult, Op.add)
+
+    peer0 = T.cores[rank ^ STEPS[0]]
+    tt(A("wh"), G(A("pht"), tab("p32")), A("absb"), Op.subtract)
+    for k in range(nv - 4, nv - 2):
+        ms(one("pk", k), float(PACKS[k]))
+    tt(A("dd", 16, 31), A("wh", 16, 31), A("wh", 17, 32), Op.subtract)
+    if left[0]:
+        prepare(0, 0, 16)
+        send(peer0, A("w0", 0, 16), A("bx", 0, 16), "base")
+    else:
+        tt(A("eq"), G(A("wh", 0, 16), tab("p1")), A("kr"), Op.is_equal)
+    cp(A("dd", 23, 32, 8), A("wh", 23, 32, 8))
+    cp(A("dt_"), G(A("dd", 16, 32), tab("p1")), "s")
+    if not left[0]:
+        tt(A("pr"), A("eq"), A("ks"), Op.mult)
+    quant("qu", "su", 0, 128, A("ut"))
+    cp(A("su2"), G(A("su"), tab("pu")), "s")
+    if not left[0]:
+        scan(A("bs", 1, 129), A("r8"), A("pr"), Op.mult, Op.add)
+        tt(A("e4"), A("eq", 0, 128, 2), A("eq", 1, 128, 2), Op.subtract)
+        cp(A("vb", 0, 16), A("bs", 8, 129, 8))
+        send(peer0, A("w0", 0, 16), A("vb", 0, 16), "base")
+    rec("v", lambda e: e.tensor_copy(T.qu2[:, 0:128].bitcast(dt.uint32), T.qu[:, 0:128].bitcast(dt.uint32).indirect(ap(tab("pu")))),
+        [A("qu2")], [A("qu"), tab("pu")])
+    quant("qa", "sa", 3 * NT, 256, A("x0"))
+    tt(A("nq"), G(A("wh", 0, 16), tab("p3")), A("lr"), Op.not_equal)
+    if left[0]:
+        ts(tab("pl"), A("rows", 0, 2), col(5), Op.add, 16.0, Op.add)
+    else:
+        ts(tab("pr"), A("rows", 24, 32, 2), col(6), Op.add, 16.0, Op.add)
+    scan(A("hs", 1, 129), A("nq"), A("dt_"), Op.mult, Op.add)
+    for k in range(nv - 2, nv):
+        ms(one("pk", k), float(PACKS[k]))
+    lists_of_pairs()
+    packs_s(s1, NP)
+    af(A("dg", 0, 64), A("cr", 0, 64), 0.03125, func=Act.Relu)
+    af(A("frc"), A("jr", 0, 96), 0.0)
+    af(A("dg", 64, 128), A("dg", 0, 64), -1.0, 1.0)
+    af(A("frc", 39, 64, 8), A("jr", 0, 4), 0.0, 100.0)
+    af(a16, a8, 2.0)
+    af(A("rows", 40, 48), a64, 1.0, 8.0)
+    af(col(11), col(2), 8.0)
+    af(col(12), col(1), 8.0)
+    af(col(9), col(10), 0.0625)
+    af(col(14), col(10), 1.0, -1.0)
+    af(tf("p2"), A("jr", 8, 136, 16), 1.0, col(11))
+    af(tf("p1e"), A("rows", 40, 48), 1.0, col(12))
+    af(A("cu"), A("jr", 0, 16), 1.0, col(4))
+
+    def closure_tables():
+        tt(A("dg", 128, 192), A("pk", 0, 64), A("dg", 0, 64), Op.mult)
+        cp(A("pki", 4, 21), A("pk", 64, NP))
+        scan(A("dg", 192, 256), A("dg", 64, 128), A("dg", 128, 192), Op.mult, Op.add)
+        ms(A("kk", 32, 48), 1.0)
+        cp(A("pki", 0, 4), A("dg", 207, 256, 16))
+        for t in range(5):
+            ts(A("rwi", t, 105, 5), A("pki"), SHIFTS[t][0], Op.logical_shift_right, SHIFTS[t][1], Op.bitwise_and)
+        cp(A("rw"), A("rwi"))
+        for n, c0 in (("rj", 2), ("ri", 1)):
+            cp(tab(n, 0, 6, 2), A("rw", c0, 15, 5))
+            ts(tab(n, 1, 6, 2), A("rw", c0, 15, 5), 8.0, Op.add)
+        af(A("col", 16, 19), A("rw", 3, 15, 5), 16.0)
+        af(col(19), one("rw", 16), 4.0)
+        for k in range(2):
+            af(tf("ai", k, 8, 2), A("rows", 16, 24, 2), 1.0, one("rw", 4 + 5 * k))
+        af(tf("bg"), a16, 1.0, one("rw", 19))
+        af(tf("pp", 0, 4), A("rw", 0, 20, 5))
+        af(tf("bi", 0, 4), A("rw", 20, 24), 1.0, col(16))
+        af(tf("ag"), A("rows", 32, 40), one("rw", 14), col(19))
+        af(tf("pp", 4, 8), A("rw", 0, 20, 5), 1.0, col(17))
+        af(tf("pe", 0, 1), col(18), 1.0, col(10))
+        af(tf("bi", 4, 8), tf("bi", 0, 4), 1.0, 64.0)
+        cp(A("ra"), G(A("rw", 24, 40), tab("rep")), "s")
+        af(A("pw", 0, 64), A("rw", 40, 104), 1.0, -8.0)
+        af(A("pw", 64, 128), A("rw", 40, 104), 1.0, -8.0)
+
+    for rd, step in enumerate(STEPS):
+        peer = T.cores[rank ^ step]
+        xt_ = "x0" if rd == 0 else "xs"
+        if rd == 0:
+            mm("ps0", "qu2", "su2", 0, "qa", "sa", 3 * NT, 256)
+            cp(A("ssb"), A("ps0", 0, 256))
+            cp(A("g1"), G(A("ssb"), A("uo")))
+            if left[0]:
+                cp(A("wh", 16, 32), A("hs", 8, 129, 8))
+        else:
+            cp(A("g1", 64, 128), G(A("ssb"), A("uo", 4, 8)), "s")
+            cp(A("g1", 0, 64), G(A("ssb"), A("uo", 0, 4)))
+        tt(A("fr"), G(A("ssb"), A("ue")), A("g1"), Op.is_lt)
+        scan(A("fl", 1, 129), A("cr"), A("fr"), Op.add, Op.min)
+        lo = 32 * rd
+        nw = 32 if left[rd] else 16
+        word = A("wp", lo, lo + 16)
+        land = A("wl", 16 * rd, 16 * rd + 16) if rd else A("w0", 16, 32)
+        mine = word if left[rd] else A("vs", 16 * rd, 16 * rd + 16)
+        if not left[rd]:
+            tt(A("p4"), G(A("fl"), tab("pr")), A("e4"), Op.mult)
+            scan(A("s4"), A("r8", 0, 128, 2), A("p4"), Op.mult, Op.add)
+            if rd == 0:
+                cp(A("vb", 16, 32), A("s4", 3, 64, 4))
+                send(peer, land, A("vb", 16, 32), "w0_")
+            tt(mine, A("s4", 3, 64, 4), A("bs", 8, 129, 8), Op.add)
+            if rd:
+                send(peer, land, mine, "w%d_" % rd)
+        if rd == 0:
+            if left[0]:
+                tt(A("vb", 16, 32), G(A("fl"), tab("pl", 0, 1)), A("dx", 0, 16), Op.mult)
+                send(peer, land, A("vb", 16, 32), "w0_")
+                iota(A("rows", 32, 40), [[16, 2], [1, 4]], 0, 0)
+                iota(A("kr"), [[0, 2], [1, 8], [0, 8]], 0, 0)
+                closure_tables()
+                prepare(0, 16, 32)
+            else:
+                iota(A("rows", 32, 40), [[16, 2], [1, 4]], 0, 0)
+                closure_tables()
+                ts(tab("pl"), A("rows", 0, 2), col(5), Op.add, 16.0, Op.add)
+                prepare(0, 0, 16)
+            iota(A("k16"), [[0, 512]], 16, 0)
+            for b in range(4):
+                o = A("et", 512 * b, 512 * b + 512)
+                rec("g", lambda e, o=o, b=b: e.affine_select(ap(o), T.k16[:], [[-1, 512]], Op.is_equal, 0.0, b, 4), [o], [A("k16")])
+        tt(A("px", 0, nw), G(A("fl"), tab("pl", 0, nw // 16)), A("dx", 0, nw), Op.mult)
+        tt(A("wp", lo, lo + nw), A("px", 0, nw), A("bx", lo, lo + nw), Op.add)
+        if left[rd] and rd:
+            send(peer, land, mine, "w%d_" % rd)
+        if rd:
+            for b in range(4):
+                cp(A("xp", 256 * b, 256 * b + 256), A(xt_, b, 1024, 4), "s")
+        tt(A("go"), G(mine, tab("rj")), A("frc"), Op.subtract if left[rd] else Op.add)
+        if left[rd]:
+            tt(A("dd", 0, 31), A("wp", lo, lo + 31), A("wp", lo + 1, lo + 32), Op.subtract)
+        else:
+            tt(A("eb"), G(word, tab("p3")), A("lr"), Op.is_equal)
+        tt(A("ow"), G(mine, tab("ri")), A("go"), Op.is_gt if left[rd] else Op.is_lt)
+        if left[rd]:
+            cp(A("dd", 7, 32, 8), A("wp", lo + 7, lo + 32, 8))
+        if rd == 0:
+            cp(A("tab", 12, NTF), A("tf", 12, NTF))
+        ts(A("ob"), A("ow"), 100.0, Op.mult)
+        if rd == 0:
+            arrive(peer, [A("w0", 0, 16)], "base", 1)
+            ts(A("ma", 0, 32), A("jr", 0, 32), col(3), Op.is_gt)
+            tt(A("oa"), G(A("w0", 0, 16), tab("ri" if left[0] else "rj")), A("ob"), Op.subtract)
+            ts(A("ma", 32, 64), A("jr", 0, 32), 15.5, Op.is_gt, col(9), Op.is_equal)
+            tt(A("ob"), G(A("w0", 0, 16), tab("rj" if left[0] else "ri")), A("oa"), Op.subtract)
+            tt(A("m32"), A("ma", 0, 32), A("ma", 32, 64), Op.mult)
+        arrive(peer, [land], "w%d_" % rd, 1)
+        cmp_ = Op.is_lt if left[rd] else Op.is_gt
+        tt(A("gp"), G(land, tab("rj")), A("ob"), Op.add if left[rd] else Op.subtract)
+        tt(A("kk", 0, 32), G(land, tab("ri", 0, 2)), A("gp", 0, 32), cmp_)
+        tt(A("kk", 48, 112), G(land, tab("ri", 2, 6)), A("gp", 32, 96), cmp_)
+        cp(A("ga"), G(A("kk", 0, 48), tab("ag")), "s")
+        scan(A("cw", 0, 32), A("kk", 80, 112), A("kk", 48, 80), Op.min, Op.max)
+        cp(A("gb"), G(A("cw", 0, 32), tab("bg")), "s")
+        if left[rd]:
+            cp(A("dh"), G(A("dd", 16, 32), tab("p1")), "s")
+        if rd == 0:
+            for b in range(4):
+                cp(A("xp", 256 * b, 256 * b + 256), A(xt_, b, 1024, 4), "s")
+            af(A("cu"), A("cu"), 1.0, 273.0)
+            af(A("er", 0, 112), A("jr", 0, 112), 0.0)
+        tt(A("pa"), G(A("cw", 0, 32), tab("ai")), A("ga"), Op.min)
+        scan(A("cw", 32, 160), A("ra"), A("pa"), Op.mult, Op.max)
+        tt(A("pa"), G(A("cw", 32, 160), tab("bi")), A("gb"), Op.min)
+        scan(A("cw", 160, 288), A("ra"), A("pa"), Op.mult, Op.max)
+        tt(A("pa"), G(A("cw"), tab("pp")), A("pw"), Op.mult)
+        scan(A("pq", 1, 129), A("r8"), A("pa"), Op.mult, Op.add)
+        pos = A("pq", 8, 129, 8)
+        if left[rd]:
+            tt(A("nq"), G(A("pq"), tab("p1e")), A("kr"), Op.not_equal)
+            tt(A("mv"), pos, A("lr", 0, 16), Op.not_equal)
+            scan(A("hs", 1, 129), A("nq"), A("dh"), Op.mult, Op.add)
+            scan(A("loc"), A("kk", 32, 48), A("mv"), Op.mult, Op.add)
+            cp(A("uz"), A("hs", 8, 129, 8))
+            tt(A("um"), pos, A("lr", 0, 16), Op.is_equal)
+            ts(A("cm"), A("m32"), A("loc", 15, 16), Op.mult)
+        else:
+            tt(A("pr"), G(A("pq"), tab("p1e")), A("eb"), Op.mult)
+            tt(A("mv"), pos, A("lr", 0, 16), Op.not_equal)
+            scan(A("ls", 1, 129), A("r8"), A("pr"), Op.mult, Op.add)
+            scan(A("loc"), A("kk", 32, 48), A("mv"), Op.mult, Op.add)
+            tt(A("nq"), G(A("ls"), tab("p2")), A("lr"), Op.not_equal)
+            tt(A("um"), pos, A("lr", 0, 16), Op.is_equal)
+            scan(A("hs", 1, 129), A("nq"), A("dt_"), Op.mult, Op.add)
+            ts(A("cm"), A("m32"), A("loc", 15, 16), Op.mult)
+            cp(A("uz"), A("hs", 8, 129, 8))
+        for h in range(2):
+            for b in range(4):
+                cp(A("zt", 512 * h + b, 512 * h + 512, 4), G(A("xp", 256 * b, 256 * b + 256), A("uz", 8 * h, 8 * h + 8)), "s")
+        tt(A("t1"), A("um"), A("cu"), Op.mult)
+        tr(A("ct"), A("cm"))
+        tt(A("t2"), A("t1"), A("loc"), Op.add)
+        rec("v", lambda e: e.tensor_reduce(ap(A("pre")), ap(A("ct")), AxisListType.X, Op.add), [A("pre")], [A("ct")])
+        if rd == 0:
+            ms(A("ft", 4 * NT, 512), 0.0)
+        ts(A("us"), A("t2"), A("pre"), Op.add, col(14), Op.add)
+        cp(G(A("er"), A("us")), A("jr"))
+
+        def z32(b, h, q):
+            cp(A("z32", 256 * b + 128 * h, 256 * b + 128 * h + 128), A("zt", 512 * h + b, 512 * h + 512, 4), q, 32.0)
+
+        def ysum(b, h):
+            o = 128 * h
+            tt(A("yw", YS * b + o, YS * b + o + 128), A("ps%d" % (4 * h + b), 0, 128), A("z32", 256 * b + o, 256 * b + o + 128), Op.add)
+        quant("qz", "sz", 0, 128, A("zt", 0, 512))
+        for b in range(4):
+            mm("ps%d" % b, "qw", "sw", 128 * b, "qz", "sz", 0, 128)
+        for b in range(4):
+            z32(b, 0, "v")
+        tr(A("e2", 0, 96), A("er", 0, 96))
+        tr(A("e2", 96, 192), A("er", 16, 112))
+        ysum(0, 0)
+        quant("qz", "sz", 128, 128, A("zt", 512, 1024))
+        for b in range(4):
+            mm("ps%d" % (4 + b), "qw", "sw", 128 * b, "qz", "sz", 128, 128)
+        for b in range(4):
+            z32(b, 1, "s")
+        cp(A("uf"), G(A("e2"), tab("pe", 0, 1)))
+        for b in range(1, 4):
+            ysum(b, 0)
+        for b in range(4):
+            ysum(b, 1)
+        for b in range(4):
+            cp(A("ft", b, 4 * NT, 4), G(A("yw", YS * b, YS * b + 256), A("uf", 0, 6)), "s" if b < 3 else "v", 0.03125)
+        quant("qf", "sf", 128 * rd, 128, A("ft"))
+        at_ = NT * (2 - rd)
+        send(peer, A("qa", at_, at_ + NT), A("qf", 128 * rd, 128 * rd + NT), "f%d_" % rd, codes=True)
+        send(peer, A("sa", at_, at_ + NT), A("sf", 128 * rd, 128 * rd + NT), "f%d_" % rd)
+        for b in range(4):
+            cp(A("f16", NT * b, NT * b + NT), A("ft", b, 4 * NT, 4), "s", 16.0)
+        if left[rd]:
+            cp(A("dw"), G(A("dd", 0, 16), tab("p1")), "s")
+        if rd == 0:
+            quant("qe", "se", 0, 512, A("et"))
+            ts(A("sg"), j16, col(0), Op.add)
+            if left[0]:
+                ts(tab("pr"), A("rows", 24, 32, 2), col(6), Op.add, 16.0, Op.add)
+        ts(A("t1"), A("loc"), A("pre"), Op.add, NT + 0.5, Op.is_lt)
+        ts(A("t2"), A("loc"), A("pre"), Op.add, 255.0, Op.add)
+        tt(A("t1"), A("t1"), A("mv"), Op.mult)
+        tt(A("t2"), A("t2"), A("sg"), Op.subtract)
+        if rd < 2:
+            lists_of_pairs()
+        tt(A("t3"), A("t1"), A("t2"), Op.mult)
+        if left[rd]:
+            scan(A("ls", 1, 129), A("nq"), A("dw"), Op.mult, Op.add)
+        tt(A("xd", 0, 16), A("t3"), A("sg"), Op.add)
+        tt(A("xd", 16, 32), A("t3"), A("sg"), Op.add)
+        if rd < 2:
+            cp(A("wh", 16, 32), A("hs", 8, 129, 8))
+            cp(A("wh", 0, 16), A("ls", 8, 129, 8))
+        tr(A("xt"), A("xd"))
+        cp(A("ux"), G(A("xt"), tab("p32", 0, 1)))
+        if rd < 2:
+            if not left[rd + 1]:
+                prepare_right()
+            prepare(rd + 1, 0, 32 if left[rd + 1] else 16)
+        else:
+            tt(A("opf"), A("ls", 8, 129, 8), A("absb", 0, 16), Op.add)
+            store("y", T.op[:], T.opf[:], A("opf"))
+        if rd == 1:
+            quant("qv", "sv", 0, 128, A("vt"))
+        arrive(peer, [A("qa", at_, at_ + NT), A("sa", at_, at_ + NT)], "f%d_" % rd, 2)
+        for b in range(4):
+            mm("ps%d" % (2 + b), "qe", "se", 128 * b, "qa", "sa", at_, 128)
+        for b in range(4):
+            tt(A("yw", YS * b + 256, YS * b + YS), A("ps%d" % (2 + b), 0, NT), A("f16", NT * b, NT * b + NT), Op.add)
+
+        def part(b, h, q):
+            cp(A("xs", 512 * h + b, 512 * h + 512, 4), G(A("yw", YS * b, YS * b + YS), A("ux", 8 * h, 8 * h + 8)), q, 0.03125)
+        wq, wsc, res = ("qu2", "su2", "ssb") if rd < 2 else ("qv", "sv", "ysb")
+        for b, h, q in ((0, 0, "s"), (1, 0, "s"), (2, 0, "v"), (3, 0, "v")):
+            part(b, h, q)
+        quant("qx", "sx", 0, 128, A("xs", 0, 512))
+        mm("ps0", wq, wsc, 0, "qx", "sx", 0, 128)
+        if rd == 2:
+            store("y", T.oc[:, 0:512], T.qx[:, 0:128].bitcast(dt.uint8), A("qx", 0, 128))
+        for b, h, q in ((0, 1, "s"), (1, 1, "s"), (2, 1, "s"), (3, 1, "v")):
+            part(b, h, q)
+        cp(A(res, 0, 128), A("ps0", 0, 128), "s")
+        quant("qx", "sx", 128, 128, A("xs", 512, 1024))
+        mm("ps1", wq, wsc, 0, "qx", "sx", 128, 128)
+        cp(A(res, 128, 256), A("ps1", 0, 128))
+
+    store("s", T.y[:, 0:128], T.ysb[:, 0:128], A("ysb", 0, 128))
+    store("y", T.oc[:, 512:1024], T.qx[:, 128:256].bitcast(dt.uint8), A("qx", 128, 256))
+    for k in range(4):
+        store("y" if k < 1 else "s", T.osc[4 * k:4 * k + 4, :], T.sx[32 * k:32 * k + 4, :], A("sx"))
+    store("y", T.y[:, 128:256], T.ysb[:, 128:256], A("ysb", 128, 256))
+    rec("y", None, [], [], after=stores)
+    emit(g, T, ops)
+    g.wait_ge(T.sem.sent, sent[0])

@@ -4,7 +4,8 @@ F32, BF, I32, U16, U8, X4 = "float32", "bfloat16", "int32", "uint16", "uint8", "
 STEPS = [1, 2, 4]
 NT = 96
 YS = 256 + NT
-OPT = {"gp": 14, "vp": 16, "s1": 22}
+OPT = {"gp": 14, "vp": 16}
+WAKE, FAR, ISSUE, EARLY = 200.0, 2500.0, 400.0, 3000.0
 
 D1 = [(2, 3), (1, 3), (0, 3), (1, 2), (0, 2), (0, 3), (0, 1), (0, 0)]
 D0 = [(0, 0), (1, 2), (0, 1), (0, 0), (0, 1), (2, 3), (0, 0), (0, 0)]
@@ -83,7 +84,7 @@ SEMAPHORES = ([k + str(i) for k, n in POOL.items() for i in range(n)] + ["sent",
               + ["f%d_" % i for i in range(3)])
 
 
-def emit(g, T, ops):
+def emit(g, T, ops, free):
     qs = {"v": g.vector, "s": g.scalar, "t": g.tensor, "g": g, "y": g.sync}
     masks = {}
 
@@ -91,7 +92,7 @@ def emit(g, T, ops):
         if a not in masks:
             masks[a] = sum(1 << c for c in range(a[1], a[2], a[3]))
         return masks[a]
-    seen, known, at, waits, signals = {}, {k: 0 for k in qs}, [], [], set()
+    seen, before = {}, []
     for n, o in enumerate(ops):
         deps = set(o["after"])
         acc = [(a, False) for a in o["r"]] + [(a, True) for a in o["w"]]
@@ -102,9 +103,44 @@ def emit(g, T, ops):
                     deps.add(m)
         for a, wr in acc:
             seen.setdefault(a[0], []).append((n, mask(a), wr, o["q"]))
+        before.append(deps)
+    prev, loose = {}, {}
+    for n, o in enumerate(ops):
+        if n >= free:
+            q = o["q"]
+            o["hint"] += prev.get(q, [])
+            if o["loose"]:
+                loose.setdefault(q, []).append(n)
+            else:
+                o["hint"] += loose.pop(q, [])
+                prev[q] = [n]
+    rest = [0.0] * len(ops)
+    for n in range(len(ops) - 1, -1, -1):
+        rest[n] += ops[n]["busy"] + ops[n]["lag"]
+        for m in before[n] | set(ops[n]["hint"]):
+            rest[m] = max(rest[m], rest[n] + WAKE)
+    start, taken = {}, {k: [] for k in qs}
+    for n in sorted(range(len(ops)), key=lambda k: (-rest[k], k)):
+        o = ops[n]
+        t = max([0.0] + [start[m] + ops[m]["busy"] + ops[m]["lag"] + (WAKE if m in before[n] or o["q"] is None else 0.0)
+                         for m in before[n] | set(o["hint"])])
+        if o["q"] is not None:
+            for a, b in taken[o["q"]]:
+                if t + o["busy"] <= a:
+                    break
+                t = max(t, b)
+            taken[o["q"]].append((t, t + o["busy"]))
+            taken[o["q"]].sort()
+        start[n] = t
+    order = sorted(range(len(ops)), key=lambda k: (start[k], k))
+    place = {m: i for i, m in enumerate(order)}
+    before = [[place[m] for m in before[n]] for n in order]
+    ops = [ops[n] for n in order]
+    known, at, waits, signals = {k: 0 for k in qs}, [], [], set()
+    for n, o in enumerate(ops):
         ws = []
         if o["q"] is not None:
-            for m in sorted(deps, reverse=True):
+            for m in sorted(before[n], reverse=True):
                 if not known[o["q"]] >> m & 1:
                     ws.append(m)
                     signals.add(m)
@@ -139,7 +175,7 @@ def rank_program(g, core, T, topo):
     if rank is None:
         return
     Op, Act = AluOpType, ActivationFunctionType
-    ops = []
+    ops, free, mode = [], [], [False]
 
     def A(n, lo=0, hi=None, st=1):
         if hi is None:
@@ -168,7 +204,7 @@ def rank_program(g, core, T, topo):
             return ap(a[1]).indirect(ap(a[2]))
         return T[a[0]][:, a[1]:a[2]:a[3]] if a[3] != 1 else T[a[0]][:, a[1]:a[2]]
 
-    def rec(q, fn, outs, ins, dma=False, after=(), sem=None):
+    def rec(q, fn, outs, ins, dma=False, after=(), sem=None, hint=(), per=0):
         r, w = [], []
         for a in ins:
             if isinstance(a, tuple):
@@ -179,7 +215,32 @@ def rank_program(g, core, T, topo):
                 r.append(a[2])
             else:
                 w.append(a)
-        ops.append({"q": q, "fn": fn, "r": r, "w": w, "dma": dma, "after": list(after), "sem": sem})
+        wide = lambda a: 16 * (a[2][2] - a[2][1]) if a[0] == "*" else len(range(a[1], a[2], a[3]))
+        n = wide(outs[0]) if outs else 0
+        full = [a for a in ins if isinstance(a, tuple) and (a[0] == "*" or wide(a) == n)]
+        lag = 0.0
+        if q is None or fn is None:
+            busy = 0.0
+        elif dma:
+            busy, lag = 100.0, 2000.0 + 2.0 * (n if outs else wide(ins[0]))
+        elif q == "g":
+            busy = 130.0 + 2.0 * n if outs else ISSUE
+        elif q == "t":
+            busy = 0.6 * n + 10.0
+        elif outs[0][0] == "*":
+            busy = 50.0 + 3.8 * n
+        elif [a for a in full if a[0] == "*"]:
+            busy = 55.0 + 1.5 * n
+        elif len(outs) == 2:
+            busy = 12.0 + n
+        elif q == "s":
+            busy = 65.0 + n
+        else:
+            two = not [a for a in full + outs if SCRATCH[a[0]][2] != BF]
+            both = len(full) == 2 and per == 0 and not [a for a in full if a[0][:2] == "ps"]
+            busy = max(64.0, n * (2.0 if both else 0.5 if two else 1.0))
+        ops.append({"q": q, "fn": fn, "r": r, "w": w, "dma": dma, "after": list(after), "sem": sem, "busy": busy, "lag": lag,
+                    "hint": list(hint), "loose": mode[0]})
         return len(ops) - 1
 
     def tt(o, a, b, op):
@@ -210,7 +271,7 @@ def rank_program(g, core, T, topo):
         rec("v", lambda e: e.memset(ap(o), c), [o], [])
 
     def scan(o, d0, d1, op0, op1):
-        rec("v", lambda e: e.tensor_tensor_scan(ap(o), ap(d0), ap(d1), 0.0, op0, op1), [o], [d0, d1])
+        rec("v", lambda e: e.tensor_tensor_scan(ap(o), ap(d0), ap(d1), 0.0, op0, op1), [o], [d0, d1], per=1)
 
     def tr(o, a):
         rec("v", lambda e: e.transpose(ap(o), ap(a)), [o], [a])
@@ -238,17 +299,23 @@ def rank_program(g, core, T, topo):
     def store(q, dst, src, a):
         stores.append(rec(q, lambda e: e.dma_start(dst, src), [], [a], dma=True))
 
-    sent = [0]
+    sent, last = [0], {}
 
     def send(peer, dst, src, sem, codes=False):
         rid, pid = topo.addr(peer)[0], topo.addr(peer)[1]
         m = topo.mask(core, peer)
         view = (lambda a: ap(a).bitcast(dt.uint8)) if codes else ap
-        rec("g", lambda e: e.remote_dma(view(dst), view(src), T.sem[sem], T.sem.sent, pid, rid, m), [], [src])
+        last[sem] = rec("g", lambda e: e.remote_dma(view(dst), view(src), T.sem[sem], T.sem.sent, pid, rid, m), [], [src],
+                        hint=[last[sem]] if sem in last else [])
+        ops[-1]["lag"] = FAR
+        if sem == "base":
+            ops[-1]["busy"], ops[-1]["lag"] = EARLY, 0.0
+        if sem == "w0_":
+            ops[-1]["hint"].append(last["base"])
         sent[0] += len(topo.engines(core, peer))
 
     def arrive(peer, outs, sem, writes):
-        rec(None, None, outs, [], sem=(sem, writes * len(topo.engines(peer, core))))
+        rec(None, None, outs, [], sem=(sem, writes * len(topo.engines(peer, core))), hint=[last[sem]])
 
     left = [rank < rank ^ s for s in STEPS]
 
@@ -264,13 +331,7 @@ def rank_program(g, core, T, topo):
     load("y", A("vt"), T.v[:])
 
     cols = [(0, 0, 15), (0, 0, 7), (0, 3, 1), (0, 0, 31), (2, 0, 255), (1, 0, 112), (2, 0, 48)]
-
-    def packs_s(k0, k1):
-        for k in range(k0, k1):
-            af(one("pk", k), A("z1"), 0.0, float(PACKS[k]))
-
     nv, ng = OPT["vp"], OPT["gp"]
-    s1 = nv + ng + OPT["s1"]
     a8, a16, a64, j16 = A("rows", 0, 16, 2), A("rows", 16, 24), A("rows", 24, 32), A("jr", 0, 256, 16)
     iota(A("pi", 0, 1), [[0, 1]], 0, 1)
     iota(A("mi", 0, 16), [[1, 16]], 128, -1)
@@ -284,9 +345,10 @@ def rank_program(g, core, T, topo):
     for k in range(nv, nv + ng):
         iota(one("pk", k), [[0, 1]], PACKS[k], 0)
     ms(A("z1"), 0.0)
-    for k in range(nv - 6):
+    for k in range(nv):
         ms(one("pk", k), float(PACKS[k]))
-    packs_s(nv + ng, s1)
+    for k in range(nv + ng, NP):
+        af(one("pk", k), A("z1"), 0.0, float(PACKS[k]))
     ts(A("mi", 16, 32), A("mi", 0, 16), 15, Op.bitwise_and)
     for k, (src, sh, an) in enumerate(cols):
         if sh:
@@ -308,8 +370,6 @@ def rank_program(g, core, T, topo):
     cp(A("phf"), A("phi"))
     tt(col(10), col(3), col(0), Op.subtract)
     tr(A("pht"), A("phf"))
-    for k in range(nv - 6, nv - 4):
-        ms(one("pk", k), float(PACKS[k]))
     af(a64, a8, 8.0)
     af(col(15), col(13), -1.0)
     af(A("r8"), A("lr"), func=Act.Sign)
@@ -325,8 +385,8 @@ def rank_program(g, core, T, topo):
         o = 32 * rd
         tt(A("dx", lo, hi, 2), A("wh", lo + 1, hi, 2), A("wh", lo, hi, 2), Op.subtract)
         tt(A("dx", lo + 1, hi, 2), A("wh", lo, hi, 2), A("wh", lo + 1, hi, 2), Op.subtract)
-        ts(A("xd", lo, hi), A("dx", lo, hi), col(13), Op.mult)
-        tt(A("bx", o + lo, o + hi), A("xd", lo, hi), A("wh", lo, hi), Op.add)
+        ts(A("ct", lo, hi), A("dx", lo, hi), col(13), Op.mult)
+        tt(A("bx", o + lo, o + hi), A("ct", lo, hi), A("wh", lo, hi), Op.add)
 
     def prepare_right():
         tt(A("eq"), G(A("wh", 0, 16), tab("p1")), A("kr"), Op.is_equal)
@@ -336,27 +396,20 @@ def rank_program(g, core, T, topo):
 
     peer0 = T.cores[rank ^ STEPS[0]]
     tt(A("wh"), G(A("pht"), tab("p32")), A("absb"), Op.subtract)
-    for k in range(nv - 4, nv - 2):
-        ms(one("pk", k), float(PACKS[k]))
     tt(A("dd", 16, 31), A("wh", 16, 31), A("wh", 17, 32), Op.subtract)
     if left[0]:
         prepare(0, 0, 16)
         send(peer0, A("w0", 0, 16), A("bx", 0, 16), "base")
     else:
-        tt(A("eq"), G(A("wh", 0, 16), tab("p1")), A("kr"), Op.is_equal)
-    cp(A("dd", 23, 32, 8), A("wh", 23, 32, 8))
-    cp(A("dt_"), G(A("dd", 16, 32), tab("p1")), "s")
-    if not left[0]:
-        tt(A("pr"), A("eq"), A("ks"), Op.mult)
-    quant("qu", "su", 0, 128, A("ut"))
-    cp(A("su2"), G(A("su"), tab("pu")), "s")
-    if not left[0]:
-        scan(A("bs", 1, 129), A("r8"), A("pr"), Op.mult, Op.add)
-        tt(A("e4"), A("eq", 0, 128, 2), A("eq", 1, 128, 2), Op.subtract)
+        prepare_right()
         cp(A("vb", 0, 16), A("bs", 8, 129, 8))
         send(peer0, A("w0", 0, 16), A("vb", 0, 16), "base")
+    cp(A("dd", 23, 32, 8), A("wh", 23, 32, 8))
+    cp(A("dt_"), G(A("dd", 16, 32), tab("p1")), "s")
+    quant("qu", "su", 0, 128, A("ut"))
+    cp(A("su2"), G(A("su"), tab("pu")), "s")
     rec("v", lambda e: e.tensor_copy(T.qu2[:, 0:128].bitcast(dt.uint32), T.qu[:, 0:128].bitcast(dt.uint32).indirect(ap(tab("pu")))),
-        [A("qu2")], [A("qu"), tab("pu")])
+        [A("qu2")], [G(A("qu"), tab("pu"))])
     quant("qa", "sa", 3 * NT, 256, A("x0"))
     tt(A("nq"), G(A("wh", 0, 16), tab("p3")), A("lr"), Op.not_equal)
     if left[0]:
@@ -364,10 +417,7 @@ def rank_program(g, core, T, topo):
     else:
         ts(tab("pr"), A("rows", 24, 32, 2), col(6), Op.add, 16.0, Op.add)
     scan(A("hs", 1, 129), A("nq"), A("dt_"), Op.mult, Op.add)
-    for k in range(nv - 2, nv):
-        ms(one("pk", k), float(PACKS[k]))
     lists_of_pairs()
-    packs_s(s1, NP)
     af(A("dg", 0, 64), A("cr", 0, 64), 0.03125, func=Act.Relu)
     af(A("frc"), A("jr", 0, 96), 0.0)
     af(A("dg", 64, 128), A("dg", 0, 64), -1.0, 1.0)
@@ -451,6 +501,7 @@ def rank_program(g, core, T, topo):
                 ts(tab("pl"), A("rows", 0, 2), col(5), Op.add, 16.0, Op.add)
                 prepare(0, 0, 16)
             iota(A("k16"), [[0, 512]], 16, 0)
+            ops[-1]["hint"].append(last["w0_"])
             for b in range(4):
                 o = A("et", 512 * b, 512 * b + 512)
                 rec("g", lambda e, o=o, b=b: e.affine_select(ap(o), T.k16[:], [[-1, 512]], Op.is_equal, 0.0, b, 4), [o], [A("k16")])
@@ -461,6 +512,7 @@ def rank_program(g, core, T, topo):
         if rd:
             for b in range(4):
                 cp(A("xp", 256 * b, 256 * b + 256), A(xt_, b, 1024, 4), "s")
+        mode[0] = True
         tt(A("go"), G(mine, tab("rj")), A("frc"), Op.subtract if left[rd] else Op.add)
         if left[rd]:
             tt(A("dd", 0, 31), A("wp", lo, lo + 31), A("wp", lo + 1, lo + 32), Op.subtract)
@@ -479,23 +531,29 @@ def rank_program(g, core, T, topo):
             ts(A("ma", 32, 64), A("jr", 0, 32), 15.5, Op.is_gt, col(9), Op.is_equal)
             tt(A("ob"), G(A("w0", 0, 16), tab("rj" if left[0] else "ri")), A("oa"), Op.subtract)
             tt(A("m32"), A("ma", 0, 32), A("ma", 32, 64), Op.mult)
+            free.append(len(ops))
+        mode[0] = False
         arrive(peer, [land], "w%d_" % rd, 1)
         cmp_ = Op.is_lt if left[rd] else Op.is_gt
-        tt(A("gp"), G(land, tab("rj")), A("ob"), Op.add if left[rd] else Op.subtract)
+        tt(A("gp", 0, 32), G(land, tab("rj", 0, 2)), A("ob", 0, 32), Op.add if left[rd] else Op.subtract)
+        tt(A("gp", 32, 96), G(land, tab("rj", 2, 6)), A("ob", 32, 96), Op.add if left[rd] else Op.subtract)
         tt(A("kk", 0, 32), G(land, tab("ri", 0, 2)), A("gp", 0, 32), cmp_)
         tt(A("kk", 48, 112), G(land, tab("ri", 2, 6)), A("gp", 32, 96), cmp_)
         cp(A("ga"), G(A("kk", 0, 48), tab("ag")), "s")
         scan(A("cw", 0, 32), A("kk", 80, 112), A("kk", 48, 80), Op.min, Op.max)
         cp(A("gb"), G(A("cw", 0, 32), tab("bg")), "s")
+        if rd == 0:
+            af(A("cu"), A("cu"), 1.0, 273.0)
         if left[rd]:
             cp(A("dh"), G(A("dd", 16, 32), tab("p1")), "s")
         if rd == 0:
             for b in range(4):
                 cp(A("xp", 256 * b, 256 * b + 256), A(xt_, b, 1024, 4), "s")
-            af(A("cu"), A("cu"), 1.0, 273.0)
             af(A("er", 0, 112), A("jr", 0, 112), 0.0)
         tt(A("pa"), G(A("cw", 0, 32), tab("ai")), A("ga"), Op.min)
         scan(A("cw", 32, 160), A("ra"), A("pa"), Op.mult, Op.max)
+        if rd == 0:
+            ms(A("ft", 4 * NT, 512), 0.0)
         tt(A("pa"), G(A("cw", 32, 160), tab("bi")), A("gb"), Op.min)
         scan(A("cw", 160, 288), A("ra"), A("pa"), Op.mult, Op.max)
         tt(A("pa"), G(A("cw"), tab("pp")), A("pw"), Op.mult)
@@ -504,32 +562,30 @@ def rank_program(g, core, T, topo):
         if left[rd]:
             tt(A("nq"), G(A("pq"), tab("p1e")), A("kr"), Op.not_equal)
             tt(A("mv"), pos, A("lr", 0, 16), Op.not_equal)
+            tt(A("um"), pos, A("lr", 0, 16), Op.is_equal)
             scan(A("hs", 1, 129), A("nq"), A("dh"), Op.mult, Op.add)
             scan(A("loc"), A("kk", 32, 48), A("mv"), Op.mult, Op.add)
+            tt(A("t1"), A("um"), A("cu"), Op.mult)
             cp(A("uz"), A("hs", 8, 129, 8))
-            tt(A("um"), pos, A("lr", 0, 16), Op.is_equal)
             ts(A("cm"), A("m32"), A("loc", 15, 16), Op.mult)
+            tt(A("t2"), A("t1"), A("loc"), Op.add)
+            tr(A("ct"), A("cm"))
         else:
             tt(A("pr"), G(A("pq"), tab("p1e")), A("eb"), Op.mult)
             tt(A("mv"), pos, A("lr", 0, 16), Op.not_equal)
+            tt(A("um"), pos, A("lr", 0, 16), Op.is_equal)
             scan(A("ls", 1, 129), A("r8"), A("pr"), Op.mult, Op.add)
             scan(A("loc"), A("kk", 32, 48), A("mv"), Op.mult, Op.add)
+            tt(A("t1"), A("um"), A("cu"), Op.mult)
             tt(A("nq"), G(A("ls"), tab("p2")), A("lr"), Op.not_equal)
-            tt(A("um"), pos, A("lr", 0, 16), Op.is_equal)
-            scan(A("hs", 1, 129), A("nq"), A("dt_"), Op.mult, Op.add)
             ts(A("cm"), A("m32"), A("loc", 15, 16), Op.mult)
+            tt(A("t2"), A("t1"), A("loc"), Op.add)
+            scan(A("hs", 1, 129), A("nq"), A("dt_"), Op.mult, Op.add)
+            tr(A("ct"), A("cm"))
             cp(A("uz"), A("hs", 8, 129, 8))
-        for h in range(2):
-            for b in range(4):
-                cp(A("zt", 512 * h + b, 512 * h + 512, 4), G(A("xp", 256 * b, 256 * b + 256), A("uz", 8 * h, 8 * h + 8)), "s")
-        tt(A("t1"), A("um"), A("cu"), Op.mult)
-        tr(A("ct"), A("cm"))
-        tt(A("t2"), A("t1"), A("loc"), Op.add)
-        rec("v", lambda e: e.tensor_reduce(ap(A("pre")), ap(A("ct")), AxisListType.X, Op.add), [A("pre")], [A("ct")])
-        if rd == 0:
-            ms(A("ft", 4 * NT, 512), 0.0)
-        ts(A("us"), A("t2"), A("pre"), Op.add, col(14), Op.add)
-        cp(G(A("er"), A("us")), A("jr"))
+
+        def zpart(b, h, q):
+            cp(A("zt", 512 * h + b, 512 * h + 512, 4), G(A("xp", 256 * b, 256 * b + 256), A("uz", 8 * h, 8 * h + 8)), q)
 
         def z32(b, h, q):
             cp(A("z32", 256 * b + 128 * h, 256 * b + 128 * h + 128), A("zt", 512 * h + b, 512 * h + 512, 4), q, 32.0)
@@ -537,6 +593,12 @@ def rank_program(g, core, T, topo):
         def ysum(b, h):
             o = 128 * h
             tt(A("yw", YS * b + o, YS * b + o + 128), A("ps%d" % (4 * h + b), 0, 128), A("z32", 256 * b + o, 256 * b + o + 128), Op.add)
+        for k in range(7):
+            zpart(k % 4, k // 4, "s")
+        rec("v", lambda e: e.tensor_reduce(ap(A("pre")), ap(A("ct")), AxisListType.X, Op.add), [A("pre")], [A("ct")])
+        zpart(3, 1, "v")
+        ts(A("us"), A("t2"), A("pre"), Op.add, col(14), Op.add)
+        cp(G(A("er"), A("us")), A("jr"))
         quant("qz", "sz", 0, 128, A("zt", 0, 512))
         for b in range(4):
             mm("ps%d" % b, "qw", "sw", 128 * b, "qz", "sz", 0, 128)
@@ -544,34 +606,33 @@ def rank_program(g, core, T, topo):
             z32(b, 0, "v")
         tr(A("e2", 0, 96), A("er", 0, 96))
         tr(A("e2", 96, 192), A("er", 16, 112))
-        ysum(0, 0)
         quant("qz", "sz", 128, 128, A("zt", 512, 1024))
         for b in range(4):
             mm("ps%d" % (4 + b), "qw", "sw", 128 * b, "qz", "sz", 128, 128)
         for b in range(4):
             z32(b, 1, "s")
         cp(A("uf"), G(A("e2"), tab("pe", 0, 1)))
-        for b in range(1, 4):
-            ysum(b, 0)
-        for b in range(4):
-            ysum(b, 1)
+        for h in range(2):
+            for b in range(4):
+                ysum(b, h)
         for b in range(4):
             cp(A("ft", b, 4 * NT, 4), G(A("yw", YS * b, YS * b + 256), A("uf", 0, 6)), "s" if b < 3 else "v", 0.03125)
         quant("qf", "sf", 128 * rd, 128, A("ft"))
         at_ = NT * (2 - rd)
         send(peer, A("qa", at_, at_ + NT), A("qf", 128 * rd, 128 * rd + NT), "f%d_" % rd, codes=True)
         send(peer, A("sa", at_, at_ + NT), A("sf", 128 * rd, 128 * rd + NT), "f%d_" % rd)
+        mode[0] = True
         for b in range(4):
             cp(A("f16", NT * b, NT * b + NT), A("ft", b, 4 * NT, 4), "s", 16.0)
         if left[rd]:
             cp(A("dw"), G(A("dd", 0, 16), tab("p1")), "s")
-        if rd == 0:
-            quant("qe", "se", 0, 512, A("et"))
-            ts(A("sg"), j16, col(0), Op.add)
-            if left[0]:
-                ts(tab("pr"), A("rows", 24, 32, 2), col(6), Op.add, 16.0, Op.add)
         ts(A("t1"), A("loc"), A("pre"), Op.add, NT + 0.5, Op.is_lt)
         ts(A("t2"), A("loc"), A("pre"), Op.add, 255.0, Op.add)
+        if rd == 0:
+            ts(A("sg"), j16, col(0), Op.add)
+            quant("qe", "se", 0, 512, A("et"))
+            if left[0]:
+                ts(tab("pr"), A("rows", 24, 32, 2), col(6), Op.add, 16.0, Op.add)
         tt(A("t1"), A("t1"), A("mv"), Op.mult)
         tt(A("t2"), A("t2"), A("sg"), Op.subtract)
         if rd < 2:
@@ -585,33 +646,31 @@ def rank_program(g, core, T, topo):
             cp(A("wh", 16, 32), A("hs", 8, 129, 8))
             cp(A("wh", 0, 16), A("ls", 8, 129, 8))
         tr(A("xt"), A("xd"))
+        if rd < 2 and not left[rd + 1]:
+            prepare_right()
         cp(A("ux"), G(A("xt"), tab("p32", 0, 1)))
         if rd < 2:
-            if not left[rd + 1]:
-                prepare_right()
             prepare(rd + 1, 0, 32 if left[rd + 1] else 16)
         else:
             tt(A("opf"), A("ls", 8, 129, 8), A("absb", 0, 16), Op.add)
             store("y", T.op[:], T.opf[:], A("opf"))
         if rd == 1:
             quant("qv", "sv", 0, 128, A("vt"))
+        mode[0] = False
         arrive(peer, [A("qa", at_, at_ + NT), A("sa", at_, at_ + NT)], "f%d_" % rd, 2)
-        for b in range(4):
+        for b in (0, 2, 1, 3):
             mm("ps%d" % (2 + b), "qe", "se", 128 * b, "qa", "sa", at_, 128)
-        for b in range(4):
+        for b in (0, 2, 1, 3):
             tt(A("yw", YS * b + 256, YS * b + YS), A("ps%d" % (2 + b), 0, NT), A("f16", NT * b, NT * b + NT), Op.add)
-
-        def part(b, h, q):
-            cp(A("xs", 512 * h + b, 512 * h + 512, 4), G(A("yw", YS * b, YS * b + YS), A("ux", 8 * h, 8 * h + 8)), q, 0.03125)
+        for h in range(2):
+            for b in range(4):
+                cp(A("xs", 512 * h + b, 512 * h + 512, 4), G(A("yw", YS * b, YS * b + YS), A("ux", 8 * h, 8 * h + 8)),
+                   "s" if b < 2 else "v", 0.03125)
         wq, wsc, res = ("qu2", "su2", "ssb") if rd < 2 else ("qv", "sv", "ysb")
-        for b, h, q in ((0, 0, "s"), (1, 0, "s"), (2, 0, "v"), (3, 0, "v")):
-            part(b, h, q)
         quant("qx", "sx", 0, 128, A("xs", 0, 512))
         mm("ps0", wq, wsc, 0, "qx", "sx", 0, 128)
         if rd == 2:
             store("y", T.oc[:, 0:512], T.qx[:, 0:128].bitcast(dt.uint8), A("qx", 0, 128))
-        for b, h, q in ((0, 1, "s"), (1, 1, "s"), (2, 1, "s"), (3, 1, "v")):
-            part(b, h, q)
         cp(A(res, 0, 128), A("ps0", 0, 128), "s")
         quant("qx", "sx", 128, 128, A("xs", 512, 1024))
         mm("ps1", wq, wsc, 0, "qx", "sx", 128, 128)
@@ -623,5 +682,5 @@ def rank_program(g, core, T, topo):
         store("y" if k < 1 else "s", T.osc[4 * k:4 * k + 4, :], T.sx[32 * k:32 * k + 4, :], A("sx"))
     store("y", T.y[:, 128:256], T.ysb[:, 128:256], A("ysb", 128, 256))
     rec("y", None, [], [], after=stores)
-    emit(g, T, ops)
+    emit(g, T, ops, free[0])
     g.wait_ge(T.sem.sent, sent[0])

@@ -4,8 +4,11 @@ F32, BF, I32, U16, U8, X4 = "float32", "bfloat16", "int32", "uint16", "uint8", "
 STEPS = [1, 2, 4]
 NT = 96
 YS = 256 + NT
-OPT = {"gp": 14, "vp": 16}
-WAKE, FAR, ISSUE, EARLY = 200.0, 2500.0, 400.0, 3000.0
+UNIT = 0.0625
+FARBELOW = -2.0 ** 90
+OPT = {"vp": 24, "wake": 170.0, "far": 1500.0, "issue": 300.0, "early": 2000.0, "late": 3500.0, "load": 1900.0,
+       "z": "ssssssss", "z32": "vvvvssss", "f": "sssv", "x": "ssvvssvv", "seed": 1, "tries": 2, "passes": 3,
+       "noise": 1.0, "cut": 1}
 
 D1 = [(2, 3), (1, 3), (0, 3), (1, 2), (0, 2), (0, 3), (0, 1), (0, 0)]
 D0 = [(0, 0), (1, 2), (0, 1), (0, 0), (0, 1), (2, 3), (0, 0), (0, 0)]
@@ -17,16 +20,17 @@ B_FROM = [3, 2, 1, 0, 0, 2, 1, 0, 1, 0, 0, 0, 0, 0, 0, 0]
 B_SLOT = [7, 0, 1, 2, 5, 7, 3, 4, 7, 6, 7, 7, 7, 7, 7, 7]
 INTRA = [[(6, -1), (4, -1), (12, -1)], [(6, 1), (1, -1), (13, -1)], [(4, 1), (0, -1), (13, 1)], [(1, 1), (0, 1), (12, 1)]]
 SHIFTS = [(0, 255), (8, 15), (12, 15), (16, 15), (20, 15)]
+CW = 144
 
 
 def pos_term(e, t):
     h, x = e // 4, e % 4
     if t < 4:
-        return (160 + 16 * x + ENDS[3 - t], -1) if h == 0 else (160 + 16 * t + ENDS[3 - x], 1)
+        return (80 + 16 * x + ENDS[3 - t], -1) if h == 0 else (80 + 16 * t + ENDS[3 - x], 1)
     if t < 6:
         return (8 * h + INTRA[x][t - 4][0], INTRA[x][t - 4][1])
     if t == 6:
-        return (32 + 16 * h + INTRA[x][2][0], INTRA[x][2][1])
+        return (16 + 16 * h + INTRA[x][2][0], INTRA[x][2][1])
     return (7, 7 - e)
 
 
@@ -35,21 +39,21 @@ def tables():
     pos = [[pos_term(2 * c + r // 8, r % 8)[0] for r in R] for c in range(4)]
     f = [[pos[0], [r // 4 for r in R], [4 + r % 4 for r in R], B_FROM, A_SLOT + [2, 5, 3, 7, 7]],
          [pos[1], [D1[r % 8][0] + 4 * (r // 8) for r in R], [D1[r % 8][1] + 4 * (r // 8) for r in R],
-          [1 if r % 8 in (4, 5, 7) else 4 for r in R], A_SLOT + [10, 13, 11, 7, 7]],
+          [0] * 16, A_SLOT + [10, 13, 11, 7, 7]],
          [pos[2], [D0[r % 8][0] + 4 * (r // 8) for r in R], [D0[r % 8][1] + 4 * (r // 8) for r in R],
           [6 * (r % 2) + 2 * (r // 2) if r < 6 else 0 for r in R], [1] * 11 + [0] * 5],
-         [pos[3], A_FROM + [8] * 5, [0] * 16, [0] * 16, [8 + s for s in B_SLOT]]]
+         [pos[3], A_FROM + [12] * 5, [0] * 16, [0] * 16, [8 + s for s in B_SLOT]]]
     out = [sum(f[k][t][r] << SHIFTS[t][0] for t in range(5)) for k in range(4) for r in R]
-    row = ENDS + [0 if r in STARTS else 1 for r in R] + [pos_term(j // 8, j % 8)[1] + 8 for j in range(64)] + [0]
-    return out + [sum(row[5 * k + t] << SHIFTS[t][0] for t in range(5)) for k in range(17)]
+    row = ENDS + [0 if r in STARTS else 1 for r in R] + [pos_term(j // 8, j % 8)[1] + 8 for j in range(64)] + [0] * 6
+    return out + [sum(row[5 * k + t] << SHIFTS[t][0] for t in range(5)) for k in range(18)]
 
 
 PACKS = tables()
 NP = len(PACKS)
 TABS = {}
 _at = [0]
-for _n, _w in (("rj", 6), ("ri", 6), ("ai", 8), ("ag", 8), ("bi", 8), ("bg", 8), ("pp", 8), ("p1e", 8), ("p2", 8), ("pe", 2),
-               ("p32", 2), ("p1", 8), ("p3", 8), ("pr", 4), ("pl", 2), ("rep", 8), ("pu", 8)):
+for _n, _w in (("p32", 2), ("pu", 8), ("p1", 8), ("p3", 8), ("pl", 2), ("rep", 4), ("pr", 4), ("p1o", 8), ("hx", 64), ("rj", 8),
+               ("ri", 8), ("rj0", 8), ("ri0", 8), ("ai", 4), ("ag", 4), ("bi", 4), ("bg", 4), ("pp", 4), ("p1e", 4), ("p2", 8), ("pe", 2)):
     TABS[_n] = (_at[0], _w)
     _at[0] += _w
 NTF = TABS["pe"][0] + 1
@@ -60,33 +64,42 @@ _B = {
     "qa": (3 * NT + 256, X4), "sa": (3 * NT + 256, U8), "qx": (256, X4), "sx": (256, U8), "qz": (256, X4), "sz": (256, U8),
     "qf": (384, X4), "sf": (384, U8), "qu": (128, X4), "su": (128, U8), "qu2": (128, X4), "su2": (128, U8),
     "qv": (128, X4), "sv": (128, U8), "qw": (512, X4), "sw": (512, U8), "qe": (512, X4), "se": (512, U8),
-    "ssb": (256, F32), "ysb": (256, F32), "g1": (128, F32), "fr": (128, BF), "fl": (144, BF),
-    "phi": (64, I32), "phf": (64, F32), "pht": (64, F32), "wh": (32, BF), "absb": (32, BF), "dd": (32, BF), "dx": (32, F32),
-    "bx": (96, F32), "px": (32, F32), "wp": (96, BF), "vs": (48, BF), "wl": (48, BF), "w0": (32, F32), "vb": (32, F32),
-    "dh": (128, BF), "dw": (128, BF),
-    "dt_": (128, BF), "nq": (128, BF), "hs": (144, BF), "ls": (144, BF), "pq": (144, BF), "pr": (128, BF), "eq": (128, BF),
-    "eb": (128, BF), "e4": (64, BF), "p4": (64, BF), "s4": (64, BF), "bs": (144, BF), "ks": (128, BF),
-    "go": (96, BF), "ow": (96, BF), "ob": (96, F32), "oa": (96, F32), "gp": (96, F32), "kk": (112, BF), "frc": (96, BF),
-    "cw": (288, BF), "ga": (128, BF), "gb": (128, BF), "pa": (128, BF), "pw": (128, BF), "ra": (128, BF), "r8": (128, BF),
-    "mv": (16, F32), "um": (16, F32), "loc": (16, F32), "t1": (16, F32), "t2": (16, F32), "t3": (16, F32),
+    "ssb": (256, F32), "ysb": (256, F32), "g1": (128, F32), "fr": (128, BF), "fl": (128, BF),
+    "phi": (64, I32), "pf": (32, BF), "pt": (32, BF), "hf": (32, BF), "ht": (32, BF), "hb": (32, BF),
+    "wh": (48, BF), "absb": (16, BF), "dd": (16, BF), "dx": (16, BF), "px": (16, BF), "wp": (16, BF), "vs": (48, BF),
+    "wl": (48, BF), "b0": (32, BF), "bl": (48, BF), "bv": (48, BF), "vv": (16, BF), "dw": (128, BF), "dt_": (128, BF),
+    "nq": (128, BF), "n2": (128, BF), "ni": (128, BF), "hs": (128, BF), "ls": (128, BF), "pq": (128, BF), "sl": (128, BF),
+    "eb": (128, BF), "e4": (128, BF), "p4": (64, BF), "s4": (64, BF), "bs": (128, BF), "bp": (128, BF), "np_": (128, BF),
+    "go": (96, BF), "ow": (96, BF), "ob": (96, F32), "tb": (96, F32), "bd": (96, F32), "gp": (96, F32), "kk": (128, BF),
+    "frc": (48, BF), "cw": (2 * CW, BF), "ga": (128, BF), "gb": (128, BF), "pa": (128, BF), "pb": (128, BF), "pc": (128, BF),
+    "pw": (64, BF), "ra": (64, BF), "r8": (128, BF), "r16": (128, BF), "dc": (128, BF), "cr": (64, BF), "ka": (128, BF),
+    "mv": (16, F32), "um": (16, F32), "loc": (16, F32), "t1": (16, F32), "t2": (16, F32), "t3": (48, F32),
     "cm": (32, F32), "ct": (32, F32), "pre": (1, F32), "m32": (32, F32), "ma": (64, F32), "cu": (16, F32),
     "sg": (16, F32), "xd": (32, F32), "xt": (32, F32), "er": (816, BF), "e2": (192, BF), "opf": (16, F32),
     "uz": (16, U16), "ue": (8, U16), "uo": (8, U16), "us": (16, U16), "uf": (16, U16), "ux": (16, U16), "tab": (_at[0], U16),
-    "tf": (NTF, F32), "pi": (4, I32), "ci": (8, I32), "col": (24, F32), "rows": (48, F32), "jr": (256, BF), "kr": (128, BF),
-    "lr": (128, BF), "mi": (32, I32), "c16": (48, F32), "cr": (128, BF), "pk": (NP, F32), "pki": (21, I32),
-    "rwi": (105, I32), "rw": (105, F32), "dg": (256, F32), "z1": (1, F32),
+    "tf": (NTF, F32), "pi": (1, I32), "ci": (8, I32), "col": (24, F32), "rows": (32, F32), "jr": (256, BF), "kr": (256, BF),
+    "lr": (256, BF), "q16": (64, BF), "pk": (NP, F32), "pki": (22, I32), "rwi": (110, I32), "rw": (110, F32),
+    "dg": (192, F32), "z1": (2, F32),
 }
-SCRATCH = {n: ("sbuf", [128, w], d) for n, (w, d) in _B.items()}
+PLACE = {n: (n, 0) for n in _B}
+for _h, _d, _l in (("slots", F32, "mv um loc t1 t2 t3 cm ct xd xt pre"), ("words", BF, "dd dx px wp vv")):
+    _w = 0
+    for _n in _l.split():
+        PLACE[_n] = (_h, _w)
+        _w += -(-_B[_n][0] // 16) * 16
+    _B[_h], PLACE[_h] = (_w, _d), (_h, 0)
+SCRATCH = {n: ("sbuf", [128, w], d) for n, (w, d) in _B.items() if PLACE[n][0] == n}
 for _i in range(8):
     SCRATCH["ps%d" % _i] = ("psum", [128, 512], F32)
-POOL = {"v": 54, "s": 36, "t": 16, "g": 12, "d": 22}
-SEMAPHORES = ([k + str(i) for k, n in POOL.items() for i in range(n)] + ["sent", "base"] + ["w%d_" % i for i in range(3)]
-              + ["f%d_" % i for i in range(3)])
+POOL = {"v": 56, "s": 34, "t": 16, "g": 12, "d": 22}
+SEMAPHORES = ([k + str(i) for k, n in POOL.items() for i in range(n)] + ["sent"]
+              + ["%s%d_" % (k, i) for k in "bwf" for i in range(3)])
 
 
-def emit(g, T, ops, free):
+def emit(g, T, ops):
     qs = {"v": g.vector, "s": g.scalar, "t": g.tensor, "g": g, "y": g.sync}
     masks = {}
+    wake = OPT["wake"]
 
     def mask(a):
         if a not in masks:
@@ -104,34 +117,41 @@ def emit(g, T, ops, free):
         for a, wr in acc:
             seen.setdefault(a[0], []).append((n, mask(a), wr, o["q"]))
         before.append(deps)
-    prev, loose = {}, {}
+    N = len(ops)
+    up, down = [[] for o in ops], [[] for o in ops]
     for n, o in enumerate(ops):
-        if n >= free:
-            q = o["q"]
-            o["hint"] += prev.get(q, [])
-            if o["loose"]:
-                loose.setdefault(q, []).append(n)
-            else:
-                o["hint"] += loose.pop(q, [])
-                prev[q] = [n]
-    rest = [0.0] * len(ops)
-    for n in range(len(ops) - 1, -1, -1):
-        rest[n] += ops[n]["busy"] + ops[n]["lag"]
-        for m in before[n] | set(ops[n]["hint"]):
-            rest[m] = max(rest[m], rest[n] + WAKE)
-    start, taken = {}, {k: [] for k in qs}
-    for n in sorted(range(len(ops)), key=lambda k: (-rest[k], k)):
-        o = ops[n]
-        t = max([0.0] + [start[m] + ops[m]["busy"] + ops[m]["lag"] + (WAKE if m in before[n] or o["q"] is None else 0.0)
-                         for m in before[n] | set(o["hint"])])
-        if o["q"] is not None:
-            for a, b in taken[o["q"]]:
-                if t + o["busy"] <= a:
-                    break
-                t = max(t, b)
-            taken[o["q"]].append((t, t + o["busy"]))
-            taken[o["q"]].sort()
-        start[n] = t
+        for m in before[n] | set(o["hint"]):
+            d = o["far"] + (ops[m]["lag"] + wake if m in before[n] or o["q"] is None else 0.0)
+            up[n].append((m, d))
+            down[m].append((n, d))
+
+    def lay(order, edges):
+        end, taken = {}, {k: [] for k in qs}
+        for n in order:
+            o = ops[n]
+            t = max([0.0] + [end[m] + d for m, d in edges[n]])
+            if o["q"] is not None:
+                l = taken[o["q"]]
+                i = 0
+                while i < len(l) and t + o["busy"] > l[i][0]:
+                    t = max(t, l[i][1])
+                    i += 1
+                l.insert(i, (t, t + o["busy"]))
+            end[n] = t + o["busy"]
+        return end
+    best, seed = None, OPT["seed"]
+    for trial in range(OPT["tries"]):
+        rest = [0.0] * N
+        for n in range(N - 1, -1, -1):
+            seed = (seed * 1103515245 + 12345) % 2147483648
+            more = OPT["noise"] * seed / 2147483648.0 if trial else 0.0
+            rest[n] = ops[n]["busy"] * (1.0 + more) + max([0.0] + [rest[m] + d for m, d in down[n]])
+        for k in range(OPT["passes"]):
+            end = lay(sorted(range(N), key=lambda n: (-rest[n], n)), up)
+            if best is None or end[N - 1] < best[N - 1]:
+                best = end
+            rest = lay(sorted(range(N), key=lambda n: (-end[n], -n)), down)
+    start = {n: best[n] - ops[n]["busy"] for n in range(N)}
     order = sorted(range(len(ops)), key=lambda k: (start[k], k))
     place = {m: i for i, m in enumerate(order)}
     before = [[place[m] for m in before[n]] for n in order]
@@ -175,12 +195,13 @@ def rank_program(g, core, T, topo):
     if rank is None:
         return
     Op, Act = AluOpType, ActivationFunctionType
-    ops, free, mode = [], [], [False]
+    ops = []
 
     def A(n, lo=0, hi=None, st=1):
-        if hi is None:
-            hi = SCRATCH[n][1][1]
-        return (n, lo, hi, st)
+        if n[:2] == "ps":
+            return (n, lo, hi, st)
+        buf, at = PLACE[n]
+        return (buf, at + lo, at + (_B[n][0] if hi is None else hi), st)
 
     def tab(n, a=0, b=None, st=1, buf="tab"):
         return A(buf, TABS[n][0] + a, TABS[n][0] + (TABS[n][1] if b is None else b), st)
@@ -204,7 +225,7 @@ def rank_program(g, core, T, topo):
             return ap(a[1]).indirect(ap(a[2]))
         return T[a[0]][:, a[1]:a[2]:a[3]] if a[3] != 1 else T[a[0]][:, a[1]:a[2]]
 
-    def rec(q, fn, outs, ins, dma=False, after=(), sem=None, hint=(), per=0):
+    def rec(q, fn, outs, ins, dma=False, after=(), sem=None, hint=(), per=0, far=0.0):
         r, w = [], []
         for a in ins:
             if isinstance(a, tuple):
@@ -222,25 +243,25 @@ def rank_program(g, core, T, topo):
         if q is None or fn is None:
             busy = 0.0
         elif dma:
-            busy, lag = 100.0, 2000.0 + 2.0 * (n if outs else wide(ins[0]))
+            busy, lag = 60.0, OPT["load"] + 1.0 * (n if outs else wide(ins[0]))
         elif q == "g":
-            busy = 130.0 + 2.0 * n if outs else ISSUE
+            busy = 140.0 + 1.7 * n if outs else OPT["issue"]
         elif q == "t":
             busy = 0.6 * n + 10.0
         elif outs[0][0] == "*":
-            busy = 50.0 + 3.8 * n
+            busy = 50.0 + 3.2 * n
         elif [a for a in full if a[0] == "*"]:
-            busy = 55.0 + 1.5 * n
+            busy = (65.0 if q == "s" else 50.0) + 1.3 * n
         elif len(outs) == 2:
-            busy = 12.0 + n
+            busy = 12.0 + 0.88 * n
         elif q == "s":
-            busy = 65.0 + n
+            busy = 50.0 + 0.83 * n
         else:
-            two = not [a for a in full + outs if SCRATCH[a[0]][2] != BF]
+            two = not [a for a in full + outs if SCRATCH[a[0]][2] not in (BF, U16)]
             both = len(full) == 2 and per == 0 and not [a for a in full if a[0][:2] == "ps"]
-            busy = max(64.0, n * (2.0 if both else 0.5 if two else 1.0))
+            busy = 0.83 * max(64.0, n * (2.0 if both else 0.5 if two else 1.0))
         ops.append({"q": q, "fn": fn, "r": r, "w": w, "dma": dma, "after": list(after), "sem": sem, "busy": busy, "lag": lag,
-                    "hint": list(hint), "loose": mode[0]})
+                    "hint": list(hint), "far": far})
         return len(ops) - 1
 
     def tt(o, a, b, op):
@@ -248,9 +269,9 @@ def rank_program(g, core, T, topo):
 
     def ts(o, a, s1, op0, s2=None, op1=None):
         if op1 is None:
-            rec("v", lambda e: e.tensor_scalar(ap(o), ap(a), ap(s1), None, op0), [o], [a, s1])
+            rec("v", lambda e: e.tensor_scalar(ap(o), ap(a), ap(s1), None, op0), [o], [a, s1], per=1)
         else:
-            rec("v", lambda e: e.tensor_scalar(ap(o), ap(a), ap(s1), ap(s2), op0, op1), [o], [a, s1, s2])
+            rec("v", lambda e: e.tensor_scalar(ap(o), ap(a), ap(s1), ap(s2), op0, op1), [o], [a, s1, s2], per=1)
 
     def cp(o, a, q="v", scale=None):
         if q == "s":
@@ -263,9 +284,8 @@ def rank_program(g, core, T, topo):
         else:
             ts(o, a, scale, Op.mult)
 
-    def af(o, a, scale=1.0, bias=0.0, func=None):
-        f = Act.Identity if func is None else func
-        rec("s", lambda e: e.activation(ap(o), ap(a), f, bias=ap(bias), scale=ap(scale)), [o], [a, scale, bias])
+    def af(o, a, scale=1.0, bias=0.0, func=Act.Identity):
+        rec("s", lambda e: e.activation(ap(o), ap(a), func, bias=ap(bias), scale=ap(scale)), [o], [a, scale, bias])
 
     def ms(o, c):
         rec("v", lambda e: e.memset(ap(o), c), [o], [])
@@ -276,11 +296,11 @@ def rank_program(g, core, T, topo):
     def tr(o, a):
         rec("v", lambda e: e.transpose(ap(o), ap(a)), [o], [a])
 
-    def iota(o, pat, base, cm):
+    def iota(o, pat, base, cm, hint=()):
         if SCRATCH[o[0]][2] == I32:
-            rec("g", lambda e: e.iota(ap(o), pat, base, cm), [o], [])
+            rec("g", lambda e: e.iota(ap(o), pat, base, cm), [o], [], hint=hint)
         else:
-            rec("g", lambda e: e.iota(ap(o), pat, base, cm, allow_small_or_imprecise_dtypes=True), [o], [])
+            rec("g", lambda e: e.iota(ap(o), pat, base, cm, allow_small_or_imprecise_dtypes=True), [o], [], hint=hint)
 
     def quant(q, s, lo, n, a):
         o1, o2 = A(q, lo, lo + n), A(s, lo, lo + n)
@@ -292,32 +312,41 @@ def rank_program(g, core, T, topo):
         rec("t", lambda e: e.matmul_mx(ap(o), ap(a[0]), ap(a[1]), ap(a[2]), ap(a[3]), True, True), [o], a)
 
     def load(q, o, src, codes=False):
-        rec(q, lambda e: e.dma_start(ap(o).bitcast(dt.uint8) if codes else ap(o), src), [o], [], dma=True)
+        loads[q] = [rec(q, lambda e: e.dma_start(ap(o).bitcast(dt.uint8) if codes else ap(o), src), [o], [], dma=True,
+                        hint=loads.get(q, []))]
 
-    stores = []
+    stores, loads = [], {}
 
     def store(q, dst, src, a):
         stores.append(rec(q, lambda e: e.dma_start(dst, src), [], [a], dma=True))
 
-    sent, last = [0], {}
+    sent, last = [0], []
 
     def send(peer, dst, src, sem, codes=False):
         rid, pid = topo.addr(peer)[0], topo.addr(peer)[1]
         m = topo.mask(core, peer)
         view = (lambda a: ap(a).bitcast(dt.uint8)) if codes else ap
-        last[sem] = rec("g", lambda e: e.remote_dma(view(dst), view(src), T.sem[sem], T.sem.sent, pid, rid, m), [], [src],
-                        hint=[last[sem]] if sem in last else [])
-        ops[-1]["lag"] = FAR
-        if sem == "base":
-            ops[-1]["busy"], ops[-1]["lag"] = EARLY, 0.0
-        if sem == "w0_":
-            ops[-1]["hint"].append(last["base"])
+        n = rec("g", lambda e: e.remote_dma(view(dst), view(src), T.sem[sem], T.sem.sent, pid, rid, m), [], [src], hint=last[-1:])
+        if not last:
+            ops[n]["busy"] = OPT["early"]
+        last.append(n)
         sent[0] += len(topo.engines(core, peer))
 
-    def arrive(peer, outs, sem, writes):
-        rec(None, None, outs, [], sem=(sem, writes * len(topo.engines(peer, core))), hint=[last[sem]])
+    def arrive(peer, outs, sem, writes, far):
+        rec(None, None, outs, [], sem=(sem, writes * len(topo.engines(peer, core))), hint=last[-1:], far=far)
 
     left = [rank < rank ^ s for s in STEPS]
+    peers = [T.cores[rank ^ s] for s in STEPS]
+    lr, kr = A("lr", 128, 256), A("kr", 128, 256)
+
+    def half(n, b, w=64):
+        return A(n, w * b, w * b + w)
+
+    def ends(n, b=None):
+        return A(n, 7, 128, 8) if b is None else A(n, 64 * b + 7, 64 * b + 64, 8)
+
+    def pairs(n, b):
+        return tab(n, 4 * b, 4 * b + 3)
 
     load("y", A("phi", 0, 16), T.p[:])
     load("s", A("phi", 16, 32), T.p[:])
@@ -330,357 +359,294 @@ def rank_program(g, core, T, topo):
     load("y", A("sw"), T.ws[:])
     load("y", A("vt"), T.v[:])
 
-    cols = [(0, 0, 15), (0, 0, 7), (0, 3, 1), (0, 0, 31), (2, 0, 255), (1, 0, 112), (2, 0, 48)]
-    nv, ng = OPT["vp"], OPT["gp"]
-    a8, a16, a64, j16 = A("rows", 0, 16, 2), A("rows", 16, 24), A("rows", 24, 32), A("jr", 0, 256, 16)
-    iota(A("pi", 0, 1), [[0, 1]], 0, 1)
-    iota(A("mi", 0, 16), [[1, 16]], 128, -1)
-    iota(A("pi", 2, 3), [[0, 1]], 0, 16)
-    iota(A("pi", 1, 2), [[0, 1]], 0, 8)
-    iota(A("rows", 0, 16), [[8, 2], [0, 8]], 0, 0)
-    iota(A("jr"), [[1, 256]], 0, 0)
-    iota(A("lr"), [[0, 16], [1, 8]], 0, 0)
-    if not left[0]:
-        iota(A("kr"), [[0, 2], [1, 8], [0, 8]], 0, 0)
-    for k in range(nv, nv + ng):
-        iota(one("pk", k), [[0, 1]], PACKS[k], 0)
-    ms(A("z1"), 0.0)
-    for k in range(nv):
-        ms(one("pk", k), float(PACKS[k]))
-    for k in range(nv + ng, NP):
-        af(one("pk", k), A("z1"), 0.0, float(PACKS[k]))
-    ts(A("mi", 16, 32), A("mi", 0, 16), 15, Op.bitwise_and)
-    for k, (src, sh, an) in enumerate(cols):
-        if sh:
-            ts(one("ci", k), one("pi", src), sh, Op.logical_shift_right, an, Op.bitwise_and)
+    a8, c8, c4, c2 = A("rows", 0, 8), A("jr", 0, 8), A("jr", 0, 4), A("jr", 0, 2)
+    iota(A("pi"), [[0, 1]], 0, 1)
+    iota(A("jr", 0, 32), [[1, 32]], 0, 0)
+    iota(A("q16"), [[0, 4], [1, 16]], 0, 0)
+    iota(a8, [[8, 2], [0, 4]], 0, 0)
+    iota(A("rows", 16, 32), [[8, 2], [0, 8]], 0, 0)
+    iota(A("lr", 0, 128), [[0, 16], [1, 8]], 0, 0)
+    iota(A("kr", 0, 128), [[0, 2], [1, 8], [0, 8]], 0, 0)
+    iota(A("jr", 32, 256), [[1, 224]], 32, 0)
+    ms(one("z1", 0), 0.0)
+    ms(one("z1", 1), 1.0)
+    for k in range(0, NP, 2):
+        if k < 2 * OPT["vp"]:
+            ts(A("pk", k, k + 2), A("z1"), float(PACKS[k + 1] - PACKS[k]), Op.mult, float(PACKS[k]), Op.add)
         else:
-            ts(one("ci", k), one("pi", src), an, Op.bitwise_and)
-    ts(A("c16", 16, 32), A("mi", 16, 32), 0.0, Op.is_equal, 32.0, Op.mult)
-    ts(A("c16", 32, 48), A("mi", 16, 32), 1.0, Op.is_equal, -16.0, Op.mult)
-    cp(A("col", 0, 7), A("ci", 0, 7))
-    ms(A("absb", 16, 32), 0.0)
-    tt(A("c16", 0, 16), A("c16", 16, 32), A("c16", 32, 48), Op.add)
-    ts(col(13), col(0), 15.0, Op.not_equal, 16.0, Op.mult)
-    ts(A("absb", 0, 16), A("rows", 0, 16), col(4), Op.add)
-    ts(tab("p32"), A("jr", 0, 64, 32), col(3), Op.add)
-    ts(tab("rep"), A("jr", 0, 8), 0.0, Op.mult, col(0), Op.add)
-    cp(tab("pu"), A("jr", 0, 128, 16))
-    ts(tab("p1"), a8, col(1), Op.add)
-    ts(tab("p3"), A("jr", 0, 16, 2), col(2), Op.add)
-    cp(A("phf"), A("phi"))
-    tt(col(10), col(3), col(0), Op.subtract)
-    tr(A("pht"), A("phf"))
-    af(a64, a8, 8.0)
-    af(col(15), col(13), -1.0)
-    af(A("r8"), A("lr"), func=Act.Sign)
-    af(A("ks", 0, 128, 2), A("lr", 0, 128, 2), 1.0, col(13))
-    af(A("ks", 1, 128, 2), A("lr", 1, 128, 2), 1.0, col(15))
-    cp(A("cr"), G(A("c16", 0, 16), tab("rep")), "s")
+            af(A("pk", k, k + 2), A("z1"), float(PACKS[k + 1] - PACKS[k]), float(PACKS[k]))
+    for k, an in enumerate((15, 7, 31, 14, 3)):
+        ts(one("ci", k), A("pi"), an, Op.bitwise_and)
+    cp(A("col", 0, 5), A("ci", 0, 5))
+    for k, src, scale, bias in ((5, 1, -1.0, col(0)), (6, 0, -1.0, col(2)), (7, 5, 0.125, 0.0), (8, 0, 16.0, 0.0), (9, 0, 16.0, 8.0),
+                                (10, 6, UNIT, 0.0), (11, 6, 1.0, -1.0), (12, 5, 1.0, 7.0), (13, 1, 8.0, 7.0), (14, 4, 16.0, 15.0),
+                                (15, 3, 8.0, 15.0), (16, 6, 1.0, col(1)), (17, 6, 1.0, 8.0)):
+        if (k != 14 or not all(left)) and k != (17 if left[0] else 16):
+            af(col(k), col(src), scale, bias)
 
-    def lists_of_pairs():
-        cp(A("uo"), A("hs", 16, 129, 16))
-        cp(A("ue"), A("hs", 8, 129, 16))
+    def fill(o, c):
+        af(o, A("lr", 0, len(range(o[1], o[2], o[3]))), 0.0, c)
+    af(lr, A("lr", 0, 128), UNIT)
+    af(kr, A("kr", 0, 128), UNIT)
+    af(A("absb"), A("rows", 16, 32), UNIT, col(0))
+    af(tf("p32"), c2, 0.0, col(2))
+    af(tf("rep"), c4, 0.0, col(0))
+    af(tf("pu"), c8, 16.0)
+    af(tf("p1"), a8, 1.0, col(1))
+    af(tf("p3"), c8, 2.0, col(7))
+    af(tf("pl"), c2, 0.0, col(15))
+    cp(A("tab", 0, TABS["pr"][0]), A("tf", 0, TABS["pr"][0]))
+    if not all(left):
+        ts(tab("pr"), A("rows", 0, 8, 2), 8.0, Op.mult, col(14), Op.add)
+    af(tf("p2"), c8, 16.0, col(12))
+    af(tf("p1e"), c4, 0.0, col(13))
+    ts(A("cr"), A("q16"), col(0), Op.not_equal, FARBELOW, Op.mult)
+    af(A("r8"), A("lr", 0, 128), func=Act.Sign)
+    for b in range(2):
+        af(half("r16", b), A("q16"), func=Act.Sign)
+        fill(A("kk", 64 * b + 48, 64 * b + 64), 1.0)
+    fill(A("dc"), -UNIT)
+    fill(ends("dc"), 7 * UNIT)
+    fill(A("frc"), 0.0)
+    fill(A("frc", 23, 32, 8), 2.0)
+    for lo, hi, st in ((32, 39, 3), (40, 47, 3), (39, 48, 8)):
+        fill(A("frc", lo, hi, st), -2.0)
+    af(A("cu"), A("jr", 0, 16), 1.0, col(8))
+    af(A("cu"), A("cu"), 1.0, 273.0)
+    ts(A("ma", 0, 32), A("jr", 0, 32), col(2), Op.is_gt)
+    ts(A("ma", 32, 64), A("jr", 0, 32), 15.5, Op.is_gt, col(10), Op.is_equal)
+    tt(A("m32"), A("ma", 0, 32), A("ma", 32, 64), Op.mult)
+    fill(A("er", 0, 112), 0.0)
+    af(A("sg"), A("jr", 0, 256, 16), 1.0, col(0))
+    fill(A("ft", 4 * NT, 512), 0.0)
+    ts(A("dg", 0, 64), A("q16"), col(0), Op.is_equal)
+    tt(A("dg", 64, 128), A("pk", 0, 64), A("dg", 0, 64), Op.mult)
+    cp(A("pki", 4, 22), A("pk", 64, NP))
+    scan(A("dg", 128, 192), A("r16", 0, 64), A("dg", 64, 128), Op.mult, Op.add)
+    cp(A("pki", 0, 4), A("dg", 143, 192, 16))
+    for t in range(5):
+        ts(A("rwi", t, 110, 5), A("pki"), SHIFTS[t][0], Op.logical_shift_right, SHIFTS[t][1], Op.bitwise_and)
+    cp(A("rw"), A("rwi"))
+    for n, c0 in (("rj", 2), ("ri", 1)):
+        f = A("rw", c0, 20, 5)
+        for b in range(2):
+            af(tf(n, 4 * b, 4 * b + 4), f, 1.0, 8.0 * b)
+            if left[0]:
+                af(tf(n + "0", 4 * b, 4 * b + 4), f, 8.0, 64.0 * b + 7.0)
+            else:
+                af(tf(n + "0", 4 * b, 4 * b + 4), f, 1.0, col(17 if b else 6))
+    cp(A("tab", TABS["rj"][0], TABS["ai"][0]), A("tf", TABS["rj"][0], TABS["ai"][0]))
+    af(col(18), one("rw", 3), 16.0)
+    af(col(19), one("rw", 13), 16.0)
+    af(col(20), one("rw", 16), 4.0)
+    for k in range(2):
+        af(tf("ai", 2 * k, 2 * k + 2), A("rw", 4, 10, 5))
+    af(tf("bg"), c4, 0.0, one("rw", 19))
+    af(tf("pp"), A("rw", 0, 20, 5))
+    af(tf("bi"), A("rw", 20, 24), 1.0, col(18))
+    af(tf("ag"), c4, one("rw", 14), col(20))
+    af(tf("pe", 0, 1), col(19), 1.0, col(6))
+    cp(A("tab", TABS["ai"][0], NTF), A("tf", TABS["ai"][0], NTF))
+    cp(A("ra"), G(A("rw", 24, 40), tab("rep")), "s")
+    af(A("pw"), A("rw", 40, 104), UNIT, -8 * UNIT)
 
-    def prepare(rd, lo, hi):
-        o = 32 * rd
-        tt(A("dx", lo, hi, 2), A("wh", lo + 1, hi, 2), A("wh", lo, hi, 2), Op.subtract)
-        tt(A("dx", lo + 1, hi, 2), A("wh", lo, hi, 2), A("wh", lo + 1, hi, 2), Op.subtract)
-        ts(A("ct", lo, hi), A("dx", lo, hi), col(13), Op.mult)
-        tt(A("bx", o + lo, o + hi), A("ct", lo, hi), A("wh", lo, hi), Op.add)
+    def places(n, s, word, where, letters):
+        tt(A(n), G(word, where), letters, Op.not_equal)
+        scan(A(s), A(n), A("dc"), Op.mult, Op.add)
 
-    def prepare_right():
-        tt(A("eq"), G(A("wh", 0, 16), tab("p1")), A("kr"), Op.is_equal)
-        tt(A("pr"), A("eq"), A("ks"), Op.mult)
-        tt(A("e4"), A("eq", 0, 128, 2), A("eq", 1, 128, 2), Op.subtract)
-        scan(A("bs", 1, 129), A("r8"), A("pr"), Op.mult, Op.add)
+    def prepare(rd):
+        w = A("wh", 16 * rd, 16 * rd + 16)
+        tt(A("n2"), G(w, tab("p3")) if rd == 0 else G(A("ls"), tab("p2")), lr, Op.not_equal)
+        scan(A("hs"), A("n2"), A("dt_"), Op.mult, Op.add)
+        cp(A("uo"), A("hs", 15, 128, 16))
+        cp(A("ue"), A("hs", 7, 128, 16))
+        lo = 16 * rd
+        tt(A("dx", 0, 16, 2), A("wh", lo + 1, lo + 16, 2), A("wh", lo, lo + 16, 2), Op.subtract)
+        tt(A("dx", 1, 16, 2), A("wh", lo, lo + 16, 2), A("wh", lo + 1, lo + 16, 2), Op.subtract)
+        base = w
+        if not left[rd]:
+            places("ni", "bs", w, tab("p1"), kr)
+            base = A("bv", lo, lo + 16)
+            cp(base, ends("bs"))
+            tt(A("e4", 64, 128), A("ni", 1, 128, 2), A("ni", 0, 128, 2), Op.subtract)
+            cp(A("e4", 0, 64), A("e4", 64, 128), "v", 1.5 * UNIT)
+            for b in range(2):
+                cp(half("go", b, 48), G(base, pairs("rj", b)), "s")
+        if rd:
+            send(peers[rd], A("bl", lo, lo + 16), base, "b%d_" % rd)
+            arrive(peers[rd], [A("bl", lo, lo + 16)], "b%d_" % rd, 1, OPT["late"])
 
-    peer0 = T.cores[rank ^ STEPS[0]]
-    tt(A("wh"), G(A("pht"), tab("p32")), A("absb"), Op.subtract)
-    tt(A("dd", 16, 31), A("wh", 16, 31), A("wh", 17, 32), Op.subtract)
-    if left[0]:
-        prepare(0, 0, 16)
-        send(peer0, A("w0", 0, 16), A("bx", 0, 16), "base")
-    else:
-        prepare_right()
-        cp(A("vb", 0, 16), A("bs", 8, 129, 8))
-        send(peer0, A("w0", 0, 16), A("vb", 0, 16), "base")
-    cp(A("dd", 23, 32, 8), A("wh", 23, 32, 8))
-    cp(A("dt_"), G(A("dd", 16, 32), tab("p1")), "s")
+    def differences(rd, win, j, i, add, out):
+        for b in range(2):
+            tt(half("tb", b, 48), G(win, pairs(j, b)), add(b), Op.add if left[rd] else Op.subtract)
+            tt(half(out, b, 48), G(win, pairs(i, b)), half("tb", b, 48), Op.subtract)
+
+    cp(A("pf"), A("phi", 0, 32), "v", UNIT)
+    tr(A("pt"), A("pf"))
+    send(peers[0], A("b0"), A("pt"), "b0_")
+    arrive(peers[0], [A("b0")], "b0_", 1, OPT["far"])
+    cp(A("hf"), A("phi", 32, 64))
+    tr(A("ht"), A("hf"))
+    tt(A("wh", 0, 16), G(A("pt"), tab("p32", 0, 1)), A("absb"), Op.subtract)
+    cp(A("hb", 0, 16), G(A("ht"), tab("p32", 0, 1)))
+    tt(A("hb", 16, 31), A("hb", 0, 15), A("hb", 1, 16), Op.subtract)
+    cp(A("hb", 23, 32, 8), A("hb", 7, 16, 8))
+    cp(A("dt_"), G(A("hb", 16, 32), tab("p1")), "s")
+    for b in range(4):
+        af(tf("hx", 16 * b, 16 * b + 16), A("hf", 0, 16), 4.0, float(b))
+    cp(tab("hx"), tf("hx"))
     quant("qu", "su", 0, 128, A("ut"))
     cp(A("su2"), G(A("su"), tab("pu")), "s")
     rec("v", lambda e: e.tensor_copy(T.qu2[:, 0:128].bitcast(dt.uint32), T.qu[:, 0:128].bitcast(dt.uint32).indirect(ap(tab("pu")))),
         [A("qu2")], [G(A("qu"), tab("pu"))])
     quant("qa", "sa", 3 * NT, 256, A("x0"))
-    tt(A("nq"), G(A("wh", 0, 16), tab("p3")), A("lr"), Op.not_equal)
+    prepare(0)
     if left[0]:
-        ts(tab("pl"), A("rows", 0, 2), col(5), Op.add, 16.0, Op.add)
-    else:
-        ts(tab("pr"), A("rows", 24, 32, 2), col(6), Op.add, 16.0, Op.add)
-    scan(A("hs", 1, 129), A("nq"), A("dt_"), Op.mult, Op.add)
-    lists_of_pairs()
-    af(A("dg", 0, 64), A("cr", 0, 64), 0.03125, func=Act.Relu)
-    af(A("frc"), A("jr", 0, 96), 0.0)
-    af(A("dg", 64, 128), A("dg", 0, 64), -1.0, 1.0)
-    af(A("frc", 39, 64, 8), A("jr", 0, 4), 0.0, 100.0)
-    af(a16, a8, 2.0)
-    af(A("rows", 40, 48), a64, 1.0, 8.0)
-    af(col(11), col(2), 8.0)
-    af(col(12), col(1), 8.0)
-    af(col(9), col(10), 0.0625)
-    af(col(14), col(10), 1.0, -1.0)
-    af(tf("p2"), A("jr", 8, 136, 16), 1.0, col(11))
-    af(tf("p1e"), A("rows", 40, 48), 1.0, col(12))
-    af(A("cu"), A("jr", 0, 16), 1.0, col(4))
+        ts(tab("p1o"), a8, col(16), Op.add)
+        af(half("ka", 0), A("kr", 128, 192), 1.0, col(0))
+        af(half("ka", 1), half("ka", 0), 1.0, 8 * UNIT)
+        places("np_", "bp", A("b0"), tab("p1o"), A("ka"))
+    mm("ps0", "qu2", "su2", 0, "qa", "sa", 3 * NT, 128)
+    mm("ps1", "qu2", "su2", 0, "qa", "sa", 3 * NT + 128, 128)
+    cp(A("ssb", 0, 128), A("ps0", 0, 128), "s")
+    cp(A("ssb", 128, 256), A("ps1", 0, 128))
+    frc = lambda b: A("frc")
 
-    def closure_tables():
-        tt(A("dg", 128, 192), A("pk", 0, 64), A("dg", 0, 64), Op.mult)
-        cp(A("pki", 4, 21), A("pk", 64, NP))
-        scan(A("dg", 192, 256), A("dg", 64, 128), A("dg", 128, 192), Op.mult, Op.add)
-        ms(A("kk", 32, 48), 1.0)
-        cp(A("pki", 0, 4), A("dg", 207, 256, 16))
-        for t in range(5):
-            ts(A("rwi", t, 105, 5), A("pki"), SHIFTS[t][0], Op.logical_shift_right, SHIFTS[t][1], Op.bitwise_and)
-        cp(A("rw"), A("rwi"))
-        for n, c0 in (("rj", 2), ("ri", 1)):
-            cp(tab(n, 0, 6, 2), A("rw", c0, 15, 5))
-            ts(tab(n, 1, 6, 2), A("rw", c0, 15, 5), 8.0, Op.add)
-        af(A("col", 16, 19), A("rw", 3, 15, 5), 16.0)
-        af(col(19), one("rw", 16), 4.0)
-        for k in range(2):
-            af(tf("ai", k, 8, 2), A("rows", 16, 24, 2), 1.0, one("rw", 4 + 5 * k))
-        af(tf("bg"), a16, 1.0, one("rw", 19))
-        af(tf("pp", 0, 4), A("rw", 0, 20, 5))
-        af(tf("bi", 0, 4), A("rw", 20, 24), 1.0, col(16))
-        af(tf("ag"), A("rows", 32, 40), one("rw", 14), col(19))
-        af(tf("pp", 4, 8), A("rw", 0, 20, 5), 1.0, col(17))
-        af(tf("pe", 0, 1), col(18), 1.0, col(10))
-        af(tf("bi", 4, 8), tf("bi", 0, 4), 1.0, 64.0)
-        cp(A("ra"), G(A("rw", 24, 40), tab("rep")), "s")
-        af(A("pw", 0, 64), A("rw", 40, 104), 1.0, -8.0)
-        af(A("pw", 64, 128), A("rw", 40, 104), 1.0, -8.0)
-
-    for rd, step in enumerate(STEPS):
-        peer = T.cores[rank ^ step]
-        xt_ = "x0" if rd == 0 else "xs"
-        if rd == 0:
-            mm("ps0", "qu2", "su2", 0, "qa", "sa", 3 * NT, 256)
-            cp(A("ssb"), A("ps0", 0, 256))
-            cp(A("g1"), G(A("ssb"), A("uo")))
-            if left[0]:
-                cp(A("wh", 16, 32), A("hs", 8, 129, 8))
-        else:
-            cp(A("g1", 64, 128), G(A("ssb"), A("uo", 4, 8)), "s")
-            cp(A("g1", 0, 64), G(A("ssb"), A("uo", 0, 4)))
-        tt(A("fr"), G(A("ssb"), A("ue")), A("g1"), Op.is_lt)
-        scan(A("fl", 1, 129), A("cr"), A("fr"), Op.add, Op.min)
-        lo = 32 * rd
-        nw = 32 if left[rd] else 16
-        word = A("wp", lo, lo + 16)
-        land = A("wl", 16 * rd, 16 * rd + 16) if rd else A("w0", 16, 32)
-        mine = word if left[rd] else A("vs", 16 * rd, 16 * rd + 16)
+    for rd in range(3):
+        peer, lo = peers[rd], 16 * rd
+        wh, land, change = A("wh", lo, lo + 16), A("wl", lo, lo + 16), A("vs", lo, lo + 16)
+        for b in range(2):
+            tt(half("g1", b), G(A("ssb"), half("uo", b, 4)), A("cr"), Op.add)
+        for b in range(2):
+            tt(half("fr", b), G(A("ssb"), half("ue", b, 4)), half("g1", b), Op.is_lt)
+        scan(A("fl"), A("r16"), A("fr"), Op.mult, Op.add)
+        px = change if left[rd] else A("px")
         if not left[rd]:
-            tt(A("p4"), G(A("fl"), tab("pr")), A("e4"), Op.mult)
+            tt(A("p4"), G(A("fl"), tab("pr")), A("e4", 0, 64), Op.mult)
             scan(A("s4"), A("r8", 0, 128, 2), A("p4"), Op.mult, Op.add)
-            if rd == 0:
-                cp(A("vb", 16, 32), A("s4", 3, 64, 4))
-                send(peer, land, A("vb", 16, 32), "w0_")
-            tt(mine, A("s4", 3, 64, 4), A("bs", 8, 129, 8), Op.add)
-            if rd:
-                send(peer, land, mine, "w%d_" % rd)
+            cp(change, A("s4", 3, 64, 4))
+        tt(px, G(A("fl"), tab("pl", 0, 1)), A("dx"), Op.mult)
+        send(peer, land, change, "w%d_" % rd)
         if rd == 0:
-            if left[0]:
-                tt(A("vb", 16, 32), G(A("fl"), tab("pl", 0, 1)), A("dx", 0, 16), Op.mult)
-                send(peer, land, A("vb", 16, 32), "w0_")
-                iota(A("rows", 32, 40), [[16, 2], [1, 4]], 0, 0)
-                iota(A("kr"), [[0, 2], [1, 8], [0, 8]], 0, 0)
-                closure_tables()
-                prepare(0, 16, 32)
-            else:
-                iota(A("rows", 32, 40), [[16, 2], [1, 4]], 0, 0)
-                closure_tables()
-                ts(tab("pl"), A("rows", 0, 2), col(5), Op.add, 16.0, Op.add)
-                prepare(0, 0, 16)
-            iota(A("k16"), [[0, 512]], 16, 0)
-            ops[-1]["hint"].append(last["w0_"])
+            iota(A("k16"), [[0, 512]], 16, 0, last[-1:])
             for b in range(4):
                 o = A("et", 512 * b, 512 * b + 512)
                 rec("g", lambda e, o=o, b=b: e.affine_select(ap(o), T.k16[:], [[-1, 512]], Op.is_equal, 0.0, b, 4), [o], [A("k16")])
-        tt(A("px", 0, nw), G(A("fl"), tab("pl", 0, nw // 16)), A("dx", 0, nw), Op.mult)
-        tt(A("wp", lo, lo + nw), A("px", 0, nw), A("bx", lo, lo + nw), Op.add)
-        if left[rd] and rd:
-            send(peer, land, mine, "w%d_" % rd)
+                quant("qe", "se", 128 * b, 128, o)
+        for b in range(4):
+            cp(half("xp", b, 256), G(A("xs" if rd else "x0"), tab("hx", 16 * b, 16 * b + 16)), "s")
+        tt(A("wp"), px, wh, Op.add)
+        if left[rd]:
+            tt(A("dd", 0, 15), A("wp", 0, 15), A("wp", 1, 16), Op.subtract)
+            cp(A("dd", 7, 16, 8), A("wp", 7, 16, 8))
+            cp(A("dw"), G(A("dd"), tab("p1")), "v")
+            for b in range(2):
+                cp(half("go", b, 48), G(A("wp"), pairs("rj", b)))
+                tt(half("ow", b, 48), G(A("wp"), pairs("ri", b)), half("go", b, 48), Op.is_gt)
+        else:
+            tt(A("vv"), A("s4", 3, 64, 4), A("bv", lo, lo + 16), Op.add)
+            for b in range(2):
+                tt(half("ow", b, 48), G(A("vv"), pairs("ri", b)), half("go", b, 48), Op.is_lt)
+                tt(half("eb", b), G(A("wp"), tab("p3", 4 * b, 4 * b + 4)), A("lr", 128, 192), Op.is_equal)
         if rd:
-            for b in range(4):
-                cp(A("xp", 256 * b, 256 * b + 256), A(xt_, b, 1024, 4), "s")
-        mode[0] = True
-        tt(A("go"), G(mine, tab("rj")), A("frc"), Op.subtract if left[rd] else Op.add)
-        if left[rd]:
-            tt(A("dd", 0, 31), A("wp", lo, lo + 31), A("wp", lo + 1, lo + 32), Op.subtract)
+            differences(rd, A("bl", lo, lo + 16), "rj", "ri", frc, "bd")
         else:
-            tt(A("eb"), G(word, tab("p3")), A("lr"), Op.is_equal)
-        tt(A("ow"), G(mine, tab("ri")), A("go"), Op.is_gt if left[rd] else Op.is_lt)
-        if left[rd]:
-            cp(A("dd", 7, 32, 8), A("wp", lo + 7, lo + 32, 8))
-        if rd == 0:
-            cp(A("tab", 12, NTF), A("tf", 12, NTF))
-        ts(A("ob"), A("ow"), 100.0, Op.mult)
-        if rd == 0:
-            arrive(peer, [A("w0", 0, 16)], "base", 1)
-            ts(A("ma", 0, 32), A("jr", 0, 32), col(3), Op.is_gt)
-            tt(A("oa"), G(A("w0", 0, 16), tab("ri" if left[0] else "rj")), A("ob"), Op.subtract)
-            ts(A("ma", 32, 64), A("jr", 0, 32), 15.5, Op.is_gt, col(9), Op.is_equal)
-            tt(A("ob"), G(A("w0", 0, 16), tab("rj" if left[0] else "ri")), A("oa"), Op.subtract)
-            tt(A("m32"), A("ma", 0, 32), A("ma", 32, 64), Op.mult)
-            free.append(len(ops))
-        mode[0] = False
-        arrive(peer, [land], "w%d_" % rd, 1)
-        cmp_ = Op.is_lt if left[rd] else Op.is_gt
-        tt(A("gp", 0, 32), G(land, tab("rj", 0, 2)), A("ob", 0, 32), Op.add if left[rd] else Op.subtract)
-        tt(A("gp", 32, 96), G(land, tab("rj", 2, 6)), A("ob", 32, 96), Op.add if left[rd] else Op.subtract)
-        tt(A("kk", 0, 32), G(land, tab("ri", 0, 2)), A("gp", 0, 32), cmp_)
-        tt(A("kk", 48, 112), G(land, tab("ri", 2, 6)), A("gp", 32, 96), cmp_)
-        cp(A("ga"), G(A("kk", 0, 48), tab("ag")), "s")
-        scan(A("cw", 0, 32), A("kk", 80, 112), A("kk", 48, 80), Op.min, Op.max)
-        cp(A("gb"), G(A("cw", 0, 32), tab("bg")), "s")
-        if rd == 0:
-            af(A("cu"), A("cu"), 1.0, 273.0)
-        if left[rd]:
-            cp(A("dh"), G(A("dd", 16, 32), tab("p1")), "s")
-        if rd == 0:
-            for b in range(4):
-                cp(A("xp", 256 * b, 256 * b + 256), A(xt_, b, 1024, 4), "s")
-            af(A("er", 0, 112), A("jr", 0, 112), 0.0)
-        tt(A("pa"), G(A("cw", 0, 32), tab("ai")), A("ga"), Op.min)
-        scan(A("cw", 32, 160), A("ra"), A("pa"), Op.mult, Op.max)
-        if rd == 0:
-            ms(A("ft", 4 * NT, 512), 0.0)
-        tt(A("pa"), G(A("cw", 32, 160), tab("bi")), A("gb"), Op.min)
-        scan(A("cw", 160, 288), A("ra"), A("pa"), Op.mult, Op.max)
-        tt(A("pa"), G(A("cw"), tab("pp")), A("pw"), Op.mult)
-        scan(A("pq", 1, 129), A("r8"), A("pa"), Op.mult, Op.add)
-        pos = A("pq", 8, 129, 8)
-        if left[rd]:
-            tt(A("nq"), G(A("pq"), tab("p1e")), A("kr"), Op.not_equal)
-            tt(A("mv"), pos, A("lr", 0, 16), Op.not_equal)
-            tt(A("um"), pos, A("lr", 0, 16), Op.is_equal)
-            scan(A("hs", 1, 129), A("nq"), A("dh"), Op.mult, Op.add)
-            scan(A("loc"), A("kk", 32, 48), A("mv"), Op.mult, Op.add)
-            tt(A("t1"), A("um"), A("cu"), Op.mult)
-            cp(A("uz"), A("hs", 8, 129, 8))
-            ts(A("cm"), A("m32"), A("loc", 15, 16), Op.mult)
-            tt(A("t2"), A("t1"), A("loc"), Op.add)
-            tr(A("ct"), A("cm"))
-        else:
-            tt(A("pr"), G(A("pq"), tab("p1e")), A("eb"), Op.mult)
-            tt(A("mv"), pos, A("lr", 0, 16), Op.not_equal)
-            tt(A("um"), pos, A("lr", 0, 16), Op.is_equal)
-            scan(A("ls", 1, 129), A("r8"), A("pr"), Op.mult, Op.add)
-            scan(A("loc"), A("kk", 32, 48), A("mv"), Op.mult, Op.add)
-            tt(A("t1"), A("um"), A("cu"), Op.mult)
-            tt(A("nq"), G(A("ls"), tab("p2")), A("lr"), Op.not_equal)
-            ts(A("cm"), A("m32"), A("loc", 15, 16), Op.mult)
-            tt(A("t2"), A("t1"), A("loc"), Op.add)
-            scan(A("hs", 1, 129), A("nq"), A("dt_"), Op.mult, Op.add)
-            tr(A("ct"), A("cm"))
-            cp(A("uz"), A("hs", 8, 129, 8))
-
-        def zpart(b, h, q):
-            cp(A("zt", 512 * h + b, 512 * h + 512, 4), G(A("xp", 256 * b, 256 * b + 256), A("uz", 8 * h, 8 * h + 8)), q)
-
-        def z32(b, h, q):
-            cp(A("z32", 256 * b + 128 * h, 256 * b + 128 * h + 128), A("zt", 512 * h + b, 512 * h + 512, 4), q, 32.0)
-
-        def ysum(b, h):
-            o = 128 * h
-            tt(A("yw", YS * b + o, YS * b + o + 128), A("ps%d" % (4 * h + b), 0, 128), A("z32", 256 * b + o, 256 * b + o + 128), Op.add)
-        for k in range(7):
-            zpart(k % 4, k // 4, "s")
+            differences(rd, A("bp") if left[0] else A("b0"), "rj0", "ri0", frc, "bd")
+        for b in range(2):
+            tt(half("ob", b, 48), half("ow", b, 48), half("bd", b, 48), Op.subtract if left[rd] else Op.add)
+        arrive(peer, [land], "w%d_" % rd, 1, OPT["far"])
+        for b in range(2):
+            c0, k0 = CW * b, 64 * b
+            if left[rd]:
+                tt(A("kk", k0, k0 + 48), G(land, pairs("ri", b)), half("ob", b, 48), Op.is_lt)
+            else:
+                tt(half("gp", b, 48), G(land, pairs("rj", b)), half("ob", b, 48), Op.subtract)
+                tt(A("kk", k0, k0 + 48), G(land, pairs("ri", b)), half("gp", b, 48), Op.is_gt)
+            cp(half("ga", b), G(half("kk", b), tab("ag")), "s")
+            scan(A("cw", c0, c0 + 16), A("kk", k0 + 32, k0 + 48), A("kk", k0 + 16, k0 + 32), Op.min, Op.max)
+            cp(half("gb", b), G(A("cw", c0, c0 + 16), tab("bg")), "s")
+            tt(half("pa", b), G(A("cw", c0, c0 + 16), tab("ai")), half("ga", b), Op.min)
+            scan(A("cw", c0 + 16, c0 + 80), A("ra"), half("pa", b), Op.mult, Op.max)
+            tt(half("pb", b), G(A("cw", c0 + 16, c0 + 80), tab("bi")), half("gb", b), Op.min)
+            scan(A("cw", c0 + 80, c0 + CW), A("ra"), half("pb", b), Op.mult, Op.max)
+            tt(half("pc", b), G(A("cw", c0, c0 + CW), tab("pp")), A("pw"), Op.mult)
+            scan(half("pq", b), A("r8", 0, 64), half("pc", b), Op.mult, Op.add)
+            if left[rd]:
+                tt(half("nq", b), G(half("pq", b), tab("p1e")), A("kr", 128, 192), Op.not_equal)
+                scan(half("ls", b), half("nq", b), half("dw", b), Op.mult, Op.add)
+            else:
+                tt(half("sl", b), G(half("pq", b), tab("p1e")), half("eb", b), Op.mult)
+                scan(half("ls", b), A("r8", 0, 64), half("sl", b), Op.mult, Op.add)
+            ts(half("uz", b, 8), ends("ls", b), 16.0, Op.mult, col(8 + b), Op.add)
+        tt(A("mv"), ends("pq"), A("lr", 128, 144), Op.not_equal)
+        tt(A("um"), ends("pq"), A("lr", 128, 144), Op.is_equal)
+        scan(A("loc"), A("kk", 48, 64), A("mv"), Op.mult, Op.add)
+        tt(A("t1"), A("um"), A("cu"), Op.mult)
+        ts(A("cm"), A("m32"), A("loc", 15, 16), Op.mult)
+        tt(A("t2"), A("t1"), A("loc"), Op.add)
+        tr(A("ct"), A("cm"))
         rec("v", lambda e: e.tensor_reduce(ap(A("pre")), ap(A("ct")), AxisListType.X, Op.add), [A("pre")], [A("ct")])
-        zpart(3, 1, "v")
-        ts(A("us"), A("t2"), A("pre"), Op.add, col(14), Op.add)
-        cp(G(A("er"), A("us")), A("jr"))
-        quant("qz", "sz", 0, 128, A("zt", 0, 512))
-        for b in range(4):
-            mm("ps%d" % b, "qw", "sw", 128 * b, "qz", "sz", 0, 128)
-        for b in range(4):
-            z32(b, 0, "v")
+        ts(A("us"), A("t2"), A("pre"), Op.add, col(11), Op.add)
+        for k in range(OPT["cut"]):
+            w = 16 // OPT["cut"]
+            cp(G(A("er"), half("us", k, w)), half("jr", k, 16 * w))
         tr(A("e2", 0, 96), A("er", 0, 96))
         tr(A("e2", 96, 192), A("er", 16, 112))
-        quant("qz", "sz", 128, 128, A("zt", 512, 1024))
-        for b in range(4):
-            mm("ps%d" % (4 + b), "qw", "sw", 128 * b, "qz", "sz", 128, 128)
-        for b in range(4):
-            z32(b, 1, "s")
         cp(A("uf"), G(A("e2"), tab("pe", 0, 1)))
         for h in range(2):
             for b in range(4):
-                ysum(b, h)
+                cp(A("zt", 512 * h + b, 512 * h + 512, 4), G(half("xp", b, 256), half("uz", h, 8)), OPT["z"][4 * h + b])
+            quant("qz", "sz", 128 * h, 128, half("zt", h, 512))
+            for b in range(4):
+                mm("ps%d" % (4 * h + b), "qw", "sw", 128 * b, "qz", "sz", 128 * h, 128)
+            for b in range(4):
+                cp(half("z32", 2 * b + h, 128), A("zt", 512 * h + b, 512 * h + 512, 4), OPT["z32"][4 * h + b], 32.0)
+            for b in range(4):
+                o = YS * b + 128 * h
+                tt(A("yw", o, o + 128), A("ps%d" % (4 * h + b), 0, 128), half("z32", 2 * b + h, 128), Op.add)
         for b in range(4):
-            cp(A("ft", b, 4 * NT, 4), G(A("yw", YS * b, YS * b + 256), A("uf", 0, 6)), "s" if b < 3 else "v", 0.03125)
+            cp(A("ft", b, 4 * NT, 4), G(A("yw", YS * b, YS * b + 256), A("uf", 0, 6)), OPT["f"][b], 0.03125)
         quant("qf", "sf", 128 * rd, 128, A("ft"))
         at_ = NT * (2 - rd)
         send(peer, A("qa", at_, at_ + NT), A("qf", 128 * rd, 128 * rd + NT), "f%d_" % rd, codes=True)
         send(peer, A("sa", at_, at_ + NT), A("sf", 128 * rd, 128 * rd + NT), "f%d_" % rd)
-        mode[0] = True
+        arrive(peer, [A("qa", at_, at_ + NT), A("sa", at_, at_ + NT)], "f%d_" % rd, 2, OPT["far"])
         for b in range(4):
-            cp(A("f16", NT * b, NT * b + NT), A("ft", b, 4 * NT, 4), "s", 16.0)
-        if left[rd]:
-            cp(A("dw"), G(A("dd", 0, 16), tab("p1")), "s")
-        ts(A("t1"), A("loc"), A("pre"), Op.add, NT + 0.5, Op.is_lt)
-        ts(A("t2"), A("loc"), A("pre"), Op.add, 255.0, Op.add)
-        if rd == 0:
-            ts(A("sg"), j16, col(0), Op.add)
-            quant("qe", "se", 0, 512, A("et"))
-            if left[0]:
-                ts(tab("pr"), A("rows", 24, 32, 2), col(6), Op.add, 16.0, Op.add)
-        tt(A("t1"), A("t1"), A("mv"), Op.mult)
-        tt(A("t2"), A("t2"), A("sg"), Op.subtract)
-        if rd < 2:
-            lists_of_pairs()
-        tt(A("t3"), A("t1"), A("t2"), Op.mult)
-        if left[rd]:
-            scan(A("ls", 1, 129), A("nq"), A("dw"), Op.mult, Op.add)
-        tt(A("xd", 0, 16), A("t3"), A("sg"), Op.add)
-        tt(A("xd", 16, 32), A("t3"), A("sg"), Op.add)
-        if rd < 2:
-            cp(A("wh", 16, 32), A("hs", 8, 129, 8))
-            cp(A("wh", 0, 16), A("ls", 8, 129, 8))
+            cp(half("f16", b, NT), A("ft", b, 4 * NT, 4), "s", 16.0)
+        ts(A("t3", 0, 16), A("t2"), A("pre"), Op.add, NT + 0.5, Op.is_lt)
+        tt(A("t3", 16, 32), A("loc"), A("sg"), Op.subtract)
+        ts(A("t3", 32, 48), A("t3", 16, 32), A("pre"), Op.add, 255.0, Op.add)
+        tt(A("t1"), A("t3", 0, 16), A("t3", 32, 48), Op.mult)
+        tt(A("xd", 0, 16), A("t1"), A("sg"), Op.add)
+        tt(A("xd", 16, 32), A("t1"), A("sg"), Op.add)
         tr(A("xt"), A("xd"))
-        if rd < 2 and not left[rd + 1]:
-            prepare_right()
         cp(A("ux"), G(A("xt"), tab("p32", 0, 1)))
         if rd < 2:
-            prepare(rd + 1, 0, 32 if left[rd + 1] else 16)
+            cp(A("wh", lo + 16, lo + 32), ends("ls"))
+            prepare(rd + 1)
         else:
-            tt(A("opf"), A("ls", 8, 129, 8), A("absb", 0, 16), Op.add)
+            cp(A("opf"), A("uz"))
             store("y", T.op[:], T.opf[:], A("opf"))
         if rd == 1:
             quant("qv", "sv", 0, 128, A("vt"))
-        mode[0] = False
-        arrive(peer, [A("qa", at_, at_ + NT), A("sa", at_, at_ + NT)], "f%d_" % rd, 2)
         for b in (0, 2, 1, 3):
             mm("ps%d" % (2 + b), "qe", "se", 128 * b, "qa", "sa", at_, 128)
         for b in (0, 2, 1, 3):
-            tt(A("yw", YS * b + 256, YS * b + YS), A("ps%d" % (2 + b), 0, NT), A("f16", NT * b, NT * b + NT), Op.add)
+            tt(A("yw", YS * b + 256, YS * b + YS), A("ps%d" % (2 + b), 0, NT), half("f16", b, NT), Op.add)
+        wq, wsc, res = ("qu2", "su2", "ssb") if rd < 2 else ("qv", "sv", "ysb")
         for h in range(2):
             for b in range(4):
-                cp(A("xs", 512 * h + b, 512 * h + 512, 4), G(A("yw", YS * b, YS * b + YS), A("ux", 8 * h, 8 * h + 8)),
-                   "s" if b < 2 else "v", 0.03125)
-        wq, wsc, res = ("qu2", "su2", "ssb") if rd < 2 else ("qv", "sv", "ysb")
-        quant("qx", "sx", 0, 128, A("xs", 0, 512))
-        mm("ps0", wq, wsc, 0, "qx", "sx", 0, 128)
-        if rd == 2:
-            store("y", T.oc[:, 0:512], T.qx[:, 0:128].bitcast(dt.uint8), A("qx", 0, 128))
-        cp(A(res, 0, 128), A("ps0", 0, 128), "s")
-        quant("qx", "sx", 128, 128, A("xs", 512, 1024))
-        mm("ps1", wq, wsc, 0, "qx", "sx", 128, 128)
-        cp(A(res, 128, 256), A("ps1", 0, 128))
+                cp(A("xs", 512 * h + b, 512 * h + 512, 4), G(half("yw", b, YS), half("ux", h, 8)), OPT["x"][4 * h + b], 0.03125)
+            quant("qx", "sx", 128 * h, 128, half("xs", h, 512))
+            mm("ps%d" % h, wq, wsc, 0, "qx", "sx", 128 * h, 128)
+            cp(half(res, h, 128), A("ps%d" % h, 0, 128), "sv"[h])
 
+    store("y", T.oc[:, 0:512], T.qx[:, 0:128].bitcast(dt.uint8), A("qx", 0, 128))
     store("s", T.y[:, 0:128], T.ysb[:, 0:128], A("ysb", 0, 128))
     store("y", T.oc[:, 512:1024], T.qx[:, 128:256].bitcast(dt.uint8), A("qx", 128, 256))
     for k in range(4):
         store("y" if k < 1 else "s", T.osc[4 * k:4 * k + 4, :], T.sx[32 * k:32 * k + 4, :], A("sx"))
     store("y", T.y[:, 128:256], T.ysb[:, 128:256], A("ysb", 128, 256))
     rec("y", None, [], [], after=stores)
-    emit(g, T, ops, free[0])
+    emit(g, T, ops)
     g.wait_ge(T.sem.sent, sent[0])

@@ -6,9 +6,9 @@ NT = 96
 YS = 256 + NT
 UNIT = 0.0625
 FARBELOW = -2.0 ** 90
-OPT = {"vp": 24, "wake": 170.0, "far": 1500.0, "issue": 300.0, "early": 2000.0, "late": 3500.0, "load": 1900.0,
-       "z": "ssssssss", "z32": "vvvvssss", "f": "sssv", "x": "ssvvssvv", "seed": 1, "tries": 2, "passes": 3,
-       "noise": 1.0, "cut": 1}
+OPT = {"vp": 17, "wake": 200.0, "same": 250.0, "far": 800.0, "issue": 150.0, "early": 2500.0, "late": 3500.0, "load": 1500.0,
+       "base": 300.0, "z": "sssvsssv", "z32": ("s", "s"), "f": "sssv", "x": "ssvvssvv", "keep": "zxy", "s": "sv", "dw": "v",
+       "go": "v", "wh": "v", "seed": 1, "passes": 3, "swaps": 2000, "heat": 50.0}
 
 D1 = [(2, 3), (1, 3), (0, 3), (1, 2), (0, 2), (0, 3), (0, 1), (0, 0)]
 D0 = [(0, 0), (1, 2), (0, 1), (0, 0), (0, 1), (2, 3), (0, 0), (0, 0)]
@@ -52,37 +52,39 @@ PACKS = tables()
 NP = len(PACKS)
 TABS = {}
 _at = [0]
-for _n, _w in (("p32", 2), ("pu", 8), ("p1", 8), ("p3", 8), ("pl", 2), ("rep", 4), ("pr", 4), ("p1o", 8), ("hx", 64), ("rj", 8),
-               ("ri", 8), ("rj0", 8), ("ri0", 8), ("ai", 4), ("ag", 4), ("bi", 4), ("bg", 4), ("pp", 4), ("p1e", 4), ("p2", 8), ("pe", 2)):
+for _n, _w in (("hx", 64), ("rep", 4), ("p3", 8), ("p2", 8), ("p1e", 4), ("ai", 4), ("ag", 4), ("bi", 4), ("bg", 4), ("pp", 4),
+               ("pe", 2), ("p32", 2), ("pu", 8), ("p1", 8), ("pl", 2), ("pr", 4), ("p1o", 8), ("rj", 8), ("ri", 8), ("rj0", 8),
+               ("ri0", 8), ("ri4", 8)):
     TABS[_n] = (_at[0], _w)
     _at[0] += _w
 NTF = TABS["pe"][0] + 1
 
 _B = {
     "x0": (1024, BF), "xs": (1024, BF), "xp": (1024, BF), "zt": (1024, BF), "z32": (1024, BF), "yw": (4 * YS, BF),
-    "ft": (512, BF), "f16": (4 * NT, BF), "ut": (512, BF), "vt": (512, BF), "et": (2048, BF), "k16": (512, BF),
+    "ft": (512, BF), "f16": (4 * NT, BF), "ut": (512, BF), "vt": (512, BF), "et": (516, BF),
     "qa": (3 * NT + 256, X4), "sa": (3 * NT + 256, U8), "qx": (256, X4), "sx": (256, U8), "qz": (256, X4), "sz": (256, U8),
     "qf": (384, X4), "sf": (384, U8), "qu": (128, X4), "su": (128, U8), "qu2": (128, X4), "su2": (128, U8),
     "qv": (128, X4), "sv": (128, U8), "qw": (512, X4), "sw": (512, U8), "qe": (512, X4), "se": (512, U8),
-    "ssb": (256, F32), "ysb": (256, F32), "g1": (128, F32), "fr": (128, BF), "fl": (128, BF),
-    "phi": (64, I32), "pf": (32, BF), "pt": (32, BF), "hf": (32, BF), "ht": (32, BF), "hb": (32, BF),
+    "ssb": (256, F32), "sl0": (256, F32), "ysb": (256, F32), "g1": (128, F32), "fr": (128, BF), "fl": (128, BF),
+    "phi": (32, I32), "pf": (32, BF), "pt": (32, BF), "hf": (32, BF), "ht": (32, BF), "hb": (32, BF), "wa": (16, BF),
     "wh": (48, BF), "absb": (16, BF), "dd": (16, BF), "dx": (16, BF), "px": (16, BF), "wp": (16, BF), "vs": (48, BF),
-    "wl": (48, BF), "b0": (32, BF), "bl": (48, BF), "bv": (48, BF), "vv": (16, BF), "dw": (128, BF), "dt_": (128, BF),
+    "wl": (48, BF), "wr": (128, BF), "b0": (32, BF), "bl": (48, BF), "bv": (48, BF), "dw": (128, BF), "dt_": (128, BF),
     "nq": (128, BF), "n2": (128, BF), "ni": (128, BF), "hs": (128, BF), "ls": (128, BF), "pq": (128, BF), "sl": (128, BF),
-    "eb": (128, BF), "e4": (128, BF), "p4": (64, BF), "s4": (64, BF), "bs": (128, BF), "bp": (128, BF), "np_": (128, BF),
-    "go": (96, BF), "ow": (96, BF), "ob": (96, F32), "tb": (96, F32), "bd": (96, F32), "gp": (96, F32), "kk": (128, BF),
-    "frc": (48, BF), "cw": (2 * CW, BF), "ga": (128, BF), "gb": (128, BF), "pa": (128, BF), "pb": (128, BF), "pc": (128, BF),
-    "pw": (64, BF), "ra": (64, BF), "r8": (128, BF), "r16": (128, BF), "dc": (128, BF), "cr": (64, BF), "ka": (128, BF),
-    "mv": (16, F32), "um": (16, F32), "loc": (16, F32), "t1": (16, F32), "t2": (16, F32), "t3": (48, F32),
+    "eb": (128, BF), "e4": (128, BF), "p4": (64, BF), "s4": (192, BF), "bs": (128, BF), "bp": (128, BF), "np_": (128, BF),
+    "go": (96, BF), "od": (96, BF), "ow": (96, BF), "ob": (96, F32), "tb": (96, F32), "bd": (96, F32), "gp": (96, F32),
+    "kk": (128, BF), "frc": (48, BF), "cw": (2 * CW, BF), "ga": (128, BF), "gb": (128, BF), "pa": (128, BF), "pb": (128, BF),
+    "pc": (128, BF), "pw": (64, BF), "ra": (64, BF), "r8": (128, BF), "r16": (128, BF), "dc": (128, BF), "cr": (64, BF),
+    "ka": (128, BF), "mv": (16, F32), "um": (16, F32), "loc": (16, F32), "t1": (16, F32), "t2": (16, F32), "t3": (32, F32),
     "cm": (32, F32), "ct": (32, F32), "pre": (1, F32), "m32": (32, F32), "ma": (64, F32), "cu": (16, F32),
     "sg": (16, F32), "xd": (32, F32), "xt": (32, F32), "er": (816, BF), "e2": (192, BF), "opf": (16, F32),
-    "uz": (16, U16), "ue": (8, U16), "uo": (8, U16), "us": (16, U16), "uf": (16, U16), "ux": (16, U16), "tab": (_at[0], U16),
+    "uz": (16, U16), "uu": (16, U16), "us": (16, U16), "uf": (16, U16), "ux": (16, U16), "hn": (16, U16), "tab": (_at[0], U16),
     "tf": (NTF, F32), "pi": (1, I32), "ci": (8, I32), "col": (24, F32), "rows": (32, F32), "jr": (256, BF), "kr": (256, BF),
-    "lr": (256, BF), "q16": (64, BF), "pk": (NP, F32), "pki": (22, I32), "rwi": (110, I32), "rw": (110, F32),
+    "lr": (256, BF), "q16": (64, BF), "pk": (NP, F32), "pki": (26, I32), "rwi": (130, I32), "rw": (130, F32),
     "dg": (192, F32), "z1": (2, F32),
 }
 PLACE = {n: (n, 0) for n in _B}
-for _h, _d, _l in (("slots", F32, "mv um loc t1 t2 t3 cm ct xd xt pre"), ("words", BF, "dd dx px wp vv")):
+for _h, _d, _l in (("slots", F32, "mv um loc t1 t2 t3 cm ct xd xt pre"), ("words", BF, "dd dx px wp"),
+                   ("steps", BF, "pa pb pc ga gb nq sl"), ("picks", BF, "n2 ni np_ hs bs bp")):
     _w = 0
     for _n in _l.split():
         PLACE[_n] = (_h, _w)
@@ -96,10 +98,105 @@ SEMAPHORES = ([k + str(i) for k, n in POOL.items() for i in range(n)] + ["sent"]
               + ["%s%d_" % (k, i) for k in "bwf" for i in range(3)])
 
 
+def arrange(ops, before):
+    N = len(ops)
+    busy, queue = [o["busy"] for o in ops], [o["q"] for o in ops]
+    up, down = [[] for o in ops], [[] for o in ops]
+    for n, o in enumerate(ops):
+        edges = list(o["since"])
+        for m in before[n] | set(o["hint"]):
+            wake = OPT["same" if queue[n] == queue[m] else "wake"]
+            edges.append((m, o["far"] + (ops[m]["lag"] + wake if m in before[n] or queue[n] is None else 0.0)))
+        for m, d in edges:
+            up[n].append((m, d))
+            down[m].append((n, d))
+
+    def lay(order, edges):
+        end, taken = {}, {k: [] for k in queue}
+        for n in order:
+            t = max([0.0] + [end[m] + d for m, d in edges[n]])
+            if queue[n] is not None:
+                l, i = taken[queue[n]], 0
+                while i < len(l) and t + busy[n] > l[i][0]:
+                    t = max(t, l[i][1])
+                    i += 1
+                l.insert(i, (t, t + busy[n]))
+            end[n] = t + busy[n]
+        return end
+    best, seed, rest = None, OPT["seed"], [0.0] * N
+    for n in range(N - 1, -1, -1):
+        rest[n] = busy[n] + max([0.0] + [rest[m] + d for m, d in down[n]])
+    for k in range(OPT["passes"]):
+        end = lay(sorted(range(N), key=lambda n: (-rest[n], n)), up)
+        if best is None or end[N - 1] < best[N - 1]:
+            best = end
+        rest = lay(sorted(range(N), key=lambda n: (-end[n], -n)), down)
+    order = sorted(range(N), key=lambda k: (best[k] - busy[k], k))
+    ups = [set(m for m, d in up[n]) for n in range(N)]
+
+    def timed(order, i, end, why):
+        end, why, last = list(end), list(why), {}
+        for n in order[i - 1::-1] if i else []:
+            if queue[n] not in last:
+                last[queue[n]] = n
+                if len(last) == 6:
+                    break
+        for n in order[i:]:
+            t, w = 0.0, -1
+            for m, d in up[n]:
+                if end[m] + d > t:
+                    t, w = end[m] + d, m
+            q = queue[n]
+            if q is not None:
+                m = last.get(q, -1)
+                if m >= 0 and end[m] > t:
+                    t, w = end[m], -2 - m
+                last[q] = n
+            end[n], why[n] = t + busy[n], w
+        return end, why
+    end, why = timed(order, 0, [0.0] * N, [-1] * N)
+    top, keep, held = end[N - 1], order, None
+    for trial in range(OPT["swaps"]):
+        if held is None:
+            held, n = [], N - 1
+            while why[n] != -1:
+                if why[n] < -1:
+                    held.append((n, -2 - why[n]))
+                n = why[n] if why[n] >= 0 else -2 - why[n]
+        if not held:
+            break
+        seed = (seed * 1103515245 + 12345) % 2147483648
+        n, m = held[(seed >> 8) % len(held)]
+        i, j = order.index(m), order.index(n)
+        for k in range((seed >> 20) % 3):
+            i2 = i - 1
+            while i2 >= 0 and queue[order[i2]] != queue[n]:
+                i2 -= 1
+            if i2 >= 0:
+                i = i2
+        move = {n}
+        for k in range(j - 1, i - 1, -1):
+            for x in move:
+                if order[k] in ups[x]:
+                    move.add(order[k])
+                    break
+        if order[i] in move:
+            continue
+        mid = order[i:j + 1]
+        new = order[:i] + [x for x in mid if x in move] + [x for x in mid if x not in move] + order[j + 1:]
+        e2, w2 = timed(new, i, end, why)
+        seed = (seed * 1103515245 + 12345) % 2147483648
+        if e2[N - 1] <= end[N - 1] + OPT["heat"] * (1.0 - trial / OPT["swaps"]) * seed / 2147483648.0:
+            order, end, why, held = new, e2, w2, None
+            if end[N - 1] < top:
+                top, keep = end[N - 1], order
+    OPT["span"] = OPT.get("span", []) + [int(top)]
+    return keep
+
+
 def emit(g, T, ops):
     qs = {"v": g.vector, "s": g.scalar, "t": g.tensor, "g": g, "y": g.sync}
     masks = {}
-    wake = OPT["wake"]
 
     def mask(a):
         if a not in masks:
@@ -117,42 +214,7 @@ def emit(g, T, ops):
         for a, wr in acc:
             seen.setdefault(a[0], []).append((n, mask(a), wr, o["q"]))
         before.append(deps)
-    N = len(ops)
-    up, down = [[] for o in ops], [[] for o in ops]
-    for n, o in enumerate(ops):
-        for m in before[n] | set(o["hint"]):
-            d = o["far"] + (ops[m]["lag"] + wake if m in before[n] or o["q"] is None else 0.0)
-            up[n].append((m, d))
-            down[m].append((n, d))
-
-    def lay(order, edges):
-        end, taken = {}, {k: [] for k in qs}
-        for n in order:
-            o = ops[n]
-            t = max([0.0] + [end[m] + d for m, d in edges[n]])
-            if o["q"] is not None:
-                l = taken[o["q"]]
-                i = 0
-                while i < len(l) and t + o["busy"] > l[i][0]:
-                    t = max(t, l[i][1])
-                    i += 1
-                l.insert(i, (t, t + o["busy"]))
-            end[n] = t + o["busy"]
-        return end
-    best, seed = None, OPT["seed"]
-    for trial in range(OPT["tries"]):
-        rest = [0.0] * N
-        for n in range(N - 1, -1, -1):
-            seed = (seed * 1103515245 + 12345) % 2147483648
-            more = OPT["noise"] * seed / 2147483648.0 if trial else 0.0
-            rest[n] = ops[n]["busy"] * (1.0 + more) + max([0.0] + [rest[m] + d for m, d in down[n]])
-        for k in range(OPT["passes"]):
-            end = lay(sorted(range(N), key=lambda n: (-rest[n], n)), up)
-            if best is None or end[N - 1] < best[N - 1]:
-                best = end
-            rest = lay(sorted(range(N), key=lambda n: (-end[n], -n)), down)
-    start = {n: best[n] - ops[n]["busy"] for n in range(N)}
-    order = sorted(range(len(ops)), key=lambda k: (start[k], k))
+    order = arrange(ops, before)
     place = {m: i for i, m in enumerate(order)}
     before = [[place[m] for m in before[n]] for n in order]
     ops = [ops[n] for n in order]
@@ -203,11 +265,11 @@ def rank_program(g, core, T, topo):
         buf, at = PLACE[n]
         return (buf, at + lo, at + (_B[n][0] if hi is None else hi), st)
 
-    def tab(n, a=0, b=None, st=1, buf="tab"):
-        return A(buf, TABS[n][0] + a, TABS[n][0] + (TABS[n][1] if b is None else b), st)
+    def tab(n, a=0, b=None, buf="tab"):
+        return A(buf, TABS[n][0] + a, TABS[n][0] + (TABS[n][1] if b is None else b))
 
-    def tf(n, a=0, b=None, st=1):
-        return tab(n, a, b, st, "tf")
+    def tf(n, a=0, b=None):
+        return tab(n, a, b, "tf")
 
     def G(win, off):
         return ("*", win, off)
@@ -218,6 +280,15 @@ def rank_program(g, core, T, topo):
     def one(n, k):
         return A(n, k, k + 1)
 
+    def half(n, b, w=64):
+        return A(n, w * b, w * b + w)
+
+    def ends(n, b=None):
+        return A(n, 7, 128, 8) if b is None else A(n, 64 * b + 7, 64 * b + 64, 8)
+
+    def pairs(n, b):
+        return tab(n, 4 * b, 4 * b + 3)
+
     def ap(a):
         if not isinstance(a, tuple):
             return a
@@ -225,7 +296,7 @@ def rank_program(g, core, T, topo):
             return ap(a[1]).indirect(ap(a[2]))
         return T[a[0]][:, a[1]:a[2]:a[3]] if a[3] != 1 else T[a[0]][:, a[1]:a[2]]
 
-    def rec(q, fn, outs, ins, dma=False, after=(), sem=None, hint=(), per=0, far=0.0):
+    def rec(q, fn, outs, ins, dma=False, after=(), sem=None, hint=(), per=0, far=0.0, since=()):
         r, w = [], []
         for a in ins:
             if isinstance(a, tuple):
@@ -245,7 +316,7 @@ def rank_program(g, core, T, topo):
         elif dma:
             busy, lag = 60.0, OPT["load"] + 1.0 * (n if outs else wide(ins[0]))
         elif q == "g":
-            busy = 140.0 + 1.7 * n if outs else OPT["issue"]
+            busy = 170.0 + 2.2 * n if outs else OPT["issue"]
         elif q == "t":
             busy = 0.6 * n + 10.0
         elif outs[0][0] == "*":
@@ -261,8 +332,16 @@ def rank_program(g, core, T, topo):
             both = len(full) == 2 and per == 0 and not [a for a in full if a[0][:2] == "ps"]
             busy = 0.83 * max(64.0, n * (2.0 if both else 0.5 if two else 1.0))
         ops.append({"q": q, "fn": fn, "r": r, "w": w, "dma": dma, "after": list(after), "sem": sem, "busy": busy, "lag": lag,
-                    "hint": list(hint), "far": far})
+                    "hint": list(hint), "far": far, "since": list(since)})
         return len(ops) - 1
+
+    runs = {}
+
+    def follow(name):
+        key = (name, ops[-1]["q"])
+        if name in OPT["keep"]:
+            ops[-1]["hint"] += runs.get(key, [])
+        runs[key] = [len(ops) - 1]
 
     def tt(o, a, b, op):
         rec("v", lambda e: e.tensor_tensor(ap(o), ap(a), ap(b), op), [o], [a, b])
@@ -287,11 +366,14 @@ def rank_program(g, core, T, topo):
     def af(o, a, scale=1.0, bias=0.0, func=Act.Identity):
         rec("s", lambda e: e.activation(ap(o), ap(a), func, bias=ap(bias), scale=ap(scale)), [o], [a, scale, bias])
 
+    def fill(o, c):
+        af(o, A("lr", 0, len(range(o[1], o[2], o[3]))), 0.0, c)
+
     def ms(o, c):
         rec("v", lambda e: e.memset(ap(o), c), [o], [])
 
     def scan(o, d0, d1, op0, op1):
-        rec("v", lambda e: e.tensor_tensor_scan(ap(o), ap(d0), ap(d1), 0.0, op0, op1), [o], [d0, d1], per=1)
+        return rec("v", lambda e: e.tensor_tensor_scan(ap(o), ap(d0), ap(d1), 0.0, op0, op1), [o], [d0, d1], per=1)
 
     def tr(o, a):
         rec("v", lambda e: e.transpose(ap(o), ap(a)), [o], [a])
@@ -311,11 +393,11 @@ def rank_program(g, core, T, topo):
         a = [A(wq, wlo, wlo + 128), A(ws_, wlo, wlo + 128), A(xq, xlo, xlo + n), A(xs_, xlo, xlo + n)]
         rec("t", lambda e: e.matmul_mx(ap(o), ap(a[0]), ap(a[1]), ap(a[2]), ap(a[3]), True, True), [o], a)
 
-    def load(q, o, src, codes=False):
-        loads[q] = [rec(q, lambda e: e.dma_start(ap(o).bitcast(dt.uint8) if codes else ap(o), src), [o], [], dma=True,
-                        hint=loads.get(q, []))]
-
     stores, loads = [], {}
+
+    def load(q, o, src, codes=False, after=()):
+        loads[q] = [rec(q, lambda e: e.dma_start(ap(o).bitcast(dt.uint8) if codes else ap(o), src), [o], [], dma=True,
+                        hint=loads.get(q, []), after=after)]
 
     def store(q, dst, src, a):
         stores.append(rec(q, lambda e: e.dma_start(dst, src), [], [a], dma=True))
@@ -332,74 +414,57 @@ def rank_program(g, core, T, topo):
         last.append(n)
         sent[0] += len(topo.engines(core, peer))
 
-    def arrive(peer, outs, sem, writes, far):
-        rec(None, None, outs, [], sem=(sem, writes * len(topo.engines(peer, core))), hint=last[-1:], far=far)
+    def arrive(peer, outs, sem, writes, far, since=(), own=None):
+        rec(None, None, outs, [], sem=(sem, writes * len(topo.engines(peer, core))), hint=own or last[-1:], far=far, since=since)
 
     left = [rank < rank ^ s for s in STEPS]
     peers = [T.cores[rank ^ s] for s in STEPS]
     lr, kr = A("lr", 128, 256), A("kr", 128, 256)
 
-    def half(n, b, w=64):
-        return A(n, w * b, w * b + w)
-
-    def ends(n, b=None):
-        return A(n, 7, 128, 8) if b is None else A(n, 64 * b + 7, 64 * b + 64, 8)
-
-    def pairs(n, b):
-        return tab(n, 4 * b, 4 * b + 3)
-
     load("y", A("phi", 0, 16), T.p[:])
-    load("s", A("phi", 16, 32), T.p[:])
-    load("y", A("phi", 32, 48), T.h[:])
-    load("s", A("phi", 48, 64), T.h[:])
-    load("y", A("ut"), T.u[:])
-    load("s", A("x0", 0, 512), T.x[:, 0:512])
-    load("y", A("x0", 512, 1024), T.x[:, 512:1024])
-    load("y", A("qw"), T.wc[:], codes=True)
-    load("y", A("sw"), T.ws[:])
-    load("y", A("vt"), T.v[:])
+    load("s", A("ut"), T.u[:])
+    load("y", A("x0", 0, 512), T.x[:, 0:512])
+    load("s", A("x0", 512, 1024), T.x[:, 512:1024])
+    load("y", A("phi", 16, 32), T.h[:])
 
-    a8, c8, c4, c2 = A("rows", 0, 8), A("jr", 0, 8), A("jr", 0, 4), A("jr", 0, 2)
+    a8, c8, c4 = A("rows", 0, 8), A("jr", 0, 8), A("jr", 0, 4)
     iota(A("pi"), [[0, 1]], 0, 1)
     iota(A("jr", 0, 32), [[1, 32]], 0, 0)
     iota(A("q16"), [[0, 4], [1, 16]], 0, 0)
     iota(a8, [[8, 2], [0, 4]], 0, 0)
     iota(A("rows", 16, 32), [[8, 2], [0, 8]], 0, 0)
     iota(A("lr", 0, 128), [[0, 16], [1, 8]], 0, 0)
-    iota(A("kr", 0, 128), [[0, 2], [1, 8], [0, 8]], 0, 0)
-    iota(A("jr", 32, 256), [[1, 224]], 32, 0)
+    iota(A("kr", 0, 64), [[1, 8], [0, 8]], 0, 0)
     ms(one("z1", 0), 0.0)
     ms(one("z1", 1), 1.0)
+    ms(A("et"), 0.0)
     for k in range(0, NP, 2):
         if k < 2 * OPT["vp"]:
             ts(A("pk", k, k + 2), A("z1"), float(PACKS[k + 1] - PACKS[k]), Op.mult, float(PACKS[k]), Op.add)
         else:
             af(A("pk", k, k + 2), A("z1"), float(PACKS[k + 1] - PACKS[k]), float(PACKS[k]))
-    for k, an in enumerate((15, 7, 31, 14, 3)):
+    for k, an in enumerate((15, 7, 31, 14, 3, 8, 16)):
         ts(one("ci", k), A("pi"), an, Op.bitwise_and)
-    cp(A("col", 0, 5), A("ci", 0, 5))
-    for k, src, scale, bias in ((5, 1, -1.0, col(0)), (6, 0, -1.0, col(2)), (7, 5, 0.125, 0.0), (8, 0, 16.0, 0.0), (9, 0, 16.0, 8.0),
-                                (10, 6, UNIT, 0.0), (11, 6, 1.0, -1.0), (12, 5, 1.0, 7.0), (13, 1, 8.0, 7.0), (14, 4, 16.0, 15.0),
-                                (15, 3, 8.0, 15.0), (16, 6, 1.0, col(1)), (17, 6, 1.0, 8.0)):
-        if (k != 14 or not all(left)) and k != (17 if left[0] else 16):
+    cp(A("col", 0, 7), A("ci", 0, 7))
+    for k, src, scale, bias in ((7, 5, 0.125, 0.0), (8, 0, 16.0, 0.0), (9, 0, 16.0, 8.0), (10, 6, UNIT, 0.0), (11, 6, 1.0, -1.0),
+                                (12, 5, 1.0, 7.0), (13, 1, 8.0, 7.0), (14, 4, 16.0, 15.0), (18, 0, 1.0, 4.0)):
+        if k != 14 or not all(left):
             af(col(k), col(src), scale, bias)
-
-    def fill(o, c):
-        af(o, A("lr", 0, len(range(o[1], o[2], o[3]))), 0.0, c)
     af(lr, A("lr", 0, 128), UNIT)
-    af(kr, A("kr", 0, 128), UNIT)
+    for b in range(2 - all(left)):
+        af(half("kr", 2 + b), A("kr", 0, 64), UNIT)
     af(A("absb"), A("rows", 16, 32), UNIT, col(0))
-    af(tf("p32"), c2, 0.0, col(2))
-    af(tf("rep"), c4, 0.0, col(0))
-    af(tf("pu"), c8, 16.0)
-    af(tf("p1"), a8, 1.0, col(1))
-    af(tf("p3"), c8, 2.0, col(7))
-    af(tf("pl"), c2, 0.0, col(15))
-    cp(A("tab", 0, TABS["pr"][0]), A("tf", 0, TABS["pr"][0]))
+    cp(tab("p32", 0, 1), col(2))
+    ts(tab("pu"), c8, 16.0, Op.mult)
+    ts(tab("p1"), a8, col(1), Op.add)
+    ts(tab("pl", 0, 1), col(3), 8.0, Op.mult, 15.0, Op.add)
     if not all(left):
         ts(tab("pr"), A("rows", 0, 8, 2), 8.0, Op.mult, col(14), Op.add)
+    af(tf("rep"), c4, 0.0, col(18))
+    af(tf("p3"), c8, 2.0, col(7))
     af(tf("p2"), c8, 16.0, col(12))
     af(tf("p1e"), c4, 0.0, col(13))
+    cp(A("tab", TABS["rep"][0], TABS["ai"][0]), A("tf", TABS["rep"][0], TABS["ai"][0]))
     ts(A("cr"), A("q16"), col(0), Op.not_equal, FARBELOW, Op.mult)
     af(A("r8"), A("lr", 0, 128), func=Act.Sign)
     for b in range(2):
@@ -417,75 +482,75 @@ def rank_program(g, core, T, topo):
     ts(A("ma", 32, 64), A("jr", 0, 32), 15.5, Op.is_gt, col(10), Op.is_equal)
     tt(A("m32"), A("ma", 0, 32), A("ma", 32, 64), Op.mult)
     fill(A("er", 0, 112), 0.0)
-    af(A("sg"), A("jr", 0, 256, 16), 1.0, col(0))
     fill(A("ft", 4 * NT, 512), 0.0)
     ts(A("dg", 0, 64), A("q16"), col(0), Op.is_equal)
     tt(A("dg", 64, 128), A("pk", 0, 64), A("dg", 0, 64), Op.mult)
-    cp(A("pki", 4, 22), A("pk", 64, NP))
+    cp(A("pki", 8, 26), A("pk", 64, NP))
     scan(A("dg", 128, 192), A("r16", 0, 64), A("dg", 64, 128), Op.mult, Op.add)
     cp(A("pki", 0, 4), A("dg", 143, 192, 16))
+    ts(A("pki", 4, 8), A("dg", 143, 192, 16), float((8 << SHIFTS[1][0]) + (8 << SHIFTS[2][0])), Op.add)
     for t in range(5):
-        ts(A("rwi", t, 110, 5), A("pki"), SHIFTS[t][0], Op.logical_shift_right, SHIFTS[t][1], Op.bitwise_and)
+        ts(A("rwi", t, 130, 5), A("pki"), SHIFTS[t][0], Op.logical_shift_right, SHIFTS[t][1], Op.bitwise_and)
     cp(A("rw"), A("rwi"))
     for n, c0 in (("rj", 2), ("ri", 1)):
-        f = A("rw", c0, 20, 5)
-        for b in range(2):
-            af(tf(n, 4 * b, 4 * b + 4), f, 1.0, 8.0 * b)
-            if left[0]:
-                af(tf(n + "0", 4 * b, 4 * b + 4), f, 8.0, 64.0 * b + 7.0)
-            else:
-                af(tf(n + "0", 4 * b, 4 * b + 4), f, 1.0, col(17 if b else 6))
-    cp(A("tab", TABS["rj"][0], TABS["ai"][0]), A("tf", TABS["rj"][0], TABS["ai"][0]))
-    af(col(18), one("rw", 3), 16.0)
-    af(col(19), one("rw", 13), 16.0)
-    af(col(20), one("rw", 16), 4.0)
+        f = A("rw", c0, 40, 5)
+        cp(tab(n), f)
+        if left[0]:
+            ts(tab(n + "0"), f, 8.0, Op.mult, 7.0, Op.add)
+        else:
+            ts(tab(n + "0"), f, col(6), Op.add)
+    ts(tab("ri4"), A("rw", 1, 40, 5), 4.0, Op.mult, 3.0, Op.add)
+    af(col(15), one("rw", 3), 16.0)
+    af(col(16), one("rw", 13), 16.0)
+    af(col(17), one("rw", 16), 4.0)
     for k in range(2):
         af(tf("ai", 2 * k, 2 * k + 2), A("rw", 4, 10, 5))
     af(tf("bg"), c4, 0.0, one("rw", 19))
     af(tf("pp"), A("rw", 0, 20, 5))
-    af(tf("bi"), A("rw", 20, 24), 1.0, col(18))
-    af(tf("ag"), c4, one("rw", 14), col(20))
-    af(tf("pe", 0, 1), col(19), 1.0, col(6))
+    af(tf("bi"), A("rw", 40, 44), 1.0, col(15))
+    af(tf("ag"), c4, one("rw", 14), col(17))
+    af(tf("pe", 0, 1), col(16), 1.0, col(6))
     cp(A("tab", TABS["ai"][0], NTF), A("tf", TABS["ai"][0], NTF))
-    cp(A("ra"), G(A("rw", 24, 40), tab("rep")), "s")
-    af(A("pw"), A("rw", 40, 104), UNIT, -8 * UNIT)
+    cp(A("ra"), G(A("rw", 40, 64), tab("rep")), "s")
+    af(A("pw"), A("rw", 60, 124), UNIT, -8 * UNIT)
 
     def places(n, s, word, where, letters):
         tt(A(n), G(word, where), letters, Op.not_equal)
         scan(A(s), A(n), A("dc"), Op.mult, Op.add)
 
     def prepare(rd):
-        w = A("wh", 16 * rd, 16 * rd + 16)
-        tt(A("n2"), G(w, tab("p3")) if rd == 0 else G(A("ls"), tab("p2")), lr, Op.not_equal)
-        scan(A("hs"), A("n2"), A("dt_"), Op.mult, Op.add)
-        cp(A("uo"), A("hs", 15, 128, 16))
-        cp(A("ue"), A("hs", 7, 128, 16))
         lo = 16 * rd
+        w = A("wh", lo, lo + 16)
+        if rd:
+            tt(A("n2"), G(A("ls"), tab("p2")), lr, Op.not_equal)
+            scan(A("hs"), A("n2"), A("dt_"), Op.mult, Op.add)
+            cp(A("uu", 8, 16), A("hs", 15, 128, 16))
+            cp(A("uu", 0, 8), A("hs", 7, 128, 16))
+        else:
+            cp(A("wa"), G(A("pt"), tab("p32", 0, 1)))
+            for k in range(2):
+                cp(half("uu", k, 8), A("wa", k, 16, 2), "v", 16.0)
         tt(A("dx", 0, 16, 2), A("wh", lo + 1, lo + 16, 2), A("wh", lo, lo + 16, 2), Op.subtract)
         tt(A("dx", 1, 16, 2), A("wh", lo, lo + 16, 2), A("wh", lo + 1, lo + 16, 2), Op.subtract)
         base = w
         if not left[rd]:
             places("ni", "bs", w, tab("p1"), kr)
             base = A("bv", lo, lo + 16)
-            cp(base, ends("bs"))
+            cp(base, ends("bs"), OPT["wh"])
             tt(A("e4", 64, 128), A("ni", 1, 128, 2), A("ni", 0, 128, 2), Op.subtract)
-            cp(A("e4", 0, 64), A("e4", 64, 128), "v", 1.5 * UNIT)
+            cp(A("e4", 0, 64), A("e4", 64, 128), "s", 1.5 * UNIT)
             for b in range(2):
-                cp(half("go", b, 48), G(base, pairs("rj", b)), "s")
+                cp(half("go", b, 48), G(base, pairs("ri", b)), "s")
+                tt(half("od", b, 48), G(base, pairs("rj", b)), half("go", b, 48), Op.subtract)
         if rd:
             send(peers[rd], A("bl", lo, lo + 16), base, "b%d_" % rd)
             arrive(peers[rd], [A("bl", lo, lo + 16)], "b%d_" % rd, 1, OPT["late"])
 
-    def differences(rd, win, j, i, add, out):
-        for b in range(2):
-            tt(half("tb", b, 48), G(win, pairs(j, b)), add(b), Op.add if left[rd] else Op.subtract)
-            tt(half(out, b, 48), G(win, pairs(i, b)), half("tb", b, 48), Op.subtract)
-
-    cp(A("pf"), A("phi", 0, 32), "v", UNIT)
+    for b in range(2):
+        cp(half("pf", b, 16), A("phi", 0, 16), "v", UNIT)
+        cp(half("hf", b, 16), A("phi", 16, 32))
     tr(A("pt"), A("pf"))
     send(peers[0], A("b0"), A("pt"), "b0_")
-    arrive(peers[0], [A("b0")], "b0_", 1, OPT["far"])
-    cp(A("hf"), A("phi", 32, 64))
     tr(A("ht"), A("hf"))
     tt(A("wh", 0, 16), G(A("pt"), tab("p32", 0, 1)), A("absb"), Op.subtract)
     cp(A("hb", 0, 16), G(A("ht"), tab("p32", 0, 1)))
@@ -499,69 +564,84 @@ def rank_program(g, core, T, topo):
     cp(A("su2"), G(A("su"), tab("pu")), "s")
     rec("v", lambda e: e.tensor_copy(T.qu2[:, 0:128].bitcast(dt.uint32), T.qu[:, 0:128].bitcast(dt.uint32).indirect(ap(tab("pu")))),
         [A("qu2")], [G(A("qu"), tab("pu"))])
-    quant("qa", "sa", 3 * NT, 256, A("x0"))
     prepare(0)
     if left[0]:
-        ts(tab("p1o"), a8, col(16), Op.add)
-        af(half("ka", 0), A("kr", 128, 192), 1.0, col(0))
+        ts(tab("p1o"), a8, col(1), Op.add, col(6), Op.add)
+        af(half("ka", 0), half("kr", 2), 1.0, col(0))
         af(half("ka", 1), half("ka", 0), 1.0, 8 * UNIT)
-        places("np_", "bp", A("b0"), tab("p1o"), A("ka"))
-    mm("ps0", "qu2", "su2", 0, "qa", "sa", 3 * NT, 128)
-    mm("ps1", "qu2", "su2", 0, "qa", "sa", 3 * NT + 128, 128)
-    cp(A("ssb", 0, 128), A("ps0", 0, 128), "s")
-    cp(A("ssb", 128, 256), A("ps1", 0, 128))
-    frc = lambda b: A("frc")
+    for h in range(2):
+        quant("qa", "sa", 3 * NT + 128 * h, 128, half("x0", h, 512))
+        mm("ps%d" % h, "qu2", "su2", 0, "qa", "sa", 3 * NT + 128 * h, 128)
+        cp(half("ssb", h, 128), A("ps%d" % h, 0, 128), "sv"[h])
+    cp(A("hn"), A("phi", 16, 32))
+    for b in range(2):
+        cp(half("sl0", b, 128), G(A("ssb"), half("hn", b, 8)), "vs"[b])
 
     for rd in range(3):
         peer, lo = peers[rd], 16 * rd
         wh, land, change = A("wh", lo, lo + 16), A("wl", lo, lo + 16), A("vs", lo, lo + 16)
+        scores = A("ssb" if rd else "sl0")
         for b in range(2):
-            tt(half("g1", b), G(A("ssb"), half("uo", b, 4)), A("cr"), Op.add)
+            tt(half("g1", b), G(scores, half("uu", 2 + b, 4)), A("cr"), Op.add)
         for b in range(2):
-            tt(half("fr", b), G(A("ssb"), half("ue", b, 4)), half("g1", b), Op.is_lt)
-        scan(A("fl"), A("r16"), A("fr"), Op.mult, Op.add)
+            tt(half("fr", b), G(scores, half("uu", b, 4)), half("g1", b), Op.is_lt)
+        flags = scan(A("fl"), A("r16"), A("fr"), Op.mult, Op.add)
         px = change if left[rd] else A("px")
         if not left[rd]:
             tt(A("p4"), G(A("fl"), tab("pr")), A("e4", 0, 64), Op.mult)
-            scan(A("s4"), A("r8", 0, 128, 2), A("p4"), Op.mult, Op.add)
-            cp(change, A("s4", 3, 64, 4))
+            scan(half("s4", rd), A("r8", 0, 128, 2), A("p4"), Op.mult, Op.add)
+            if rd:
+                change = half("s4", rd)
+            else:
+                cp(change, A("s4", 3, 64, 4))
         tt(px, G(A("fl"), tab("pl", 0, 1)), A("dx"), Op.mult)
-        send(peer, land, change, "w%d_" % rd)
+        send(peer, half("wr", rd - 1) if rd and not left[rd] else land, change, "w%d_" % rd)
+        if rd and left[rd]:
+            land = half("wr", rd - 1)
         if rd == 0:
-            iota(A("k16"), [[0, 512]], 16, 0, last[-1:])
+            iota(A("jr", 32, 256), [[1, 224]], 32, 0, last[-1:])
+            af(A("sg"), A("jr", 0, 256, 16), 1.0, col(0))
+            rec("g", lambda e: e.affine_select(T.et[:], T.et[:], [[-1, 516]], Op.not_equal, 16.0, 3, 4), [A("et")], [A("et")],
+                hint=last[-1:])
             for b in range(4):
-                o = A("et", 512 * b, 512 * b + 512)
-                rec("g", lambda e, o=o, b=b: e.affine_select(ap(o), T.k16[:], [[-1, 512]], Op.is_equal, 0.0, b, 4), [o], [A("k16")])
-                quant("qe", "se", 128 * b, 128, o)
+                quant("qe", "se", 128 * b, 128, A("et", 3 - b, 515 - b))
+            arrive(peer, [A("b0")], "b0_", 1, 0.0, [(flags, OPT["base"])], last[:1])
+            if left[0]:
+                places("np_", "bp", A("b0"), tab("p1o"), A("ka"))
         for b in range(4):
             cp(half("xp", b, 256), G(A("xs" if rd else "x0"), tab("hx", 16 * b, 16 * b + 16)), "s")
         tt(A("wp"), px, wh, Op.add)
         if left[rd]:
             tt(A("dd", 0, 15), A("wp", 0, 15), A("wp", 1, 16), Op.subtract)
             cp(A("dd", 7, 16, 8), A("wp", 7, 16, 8))
-            cp(A("dw"), G(A("dd"), tab("p1")), "v")
+            cp(A("dw"), G(A("dd"), tab("p1")), OPT["dw"])
             for b in range(2):
-                cp(half("go", b, 48), G(A("wp"), pairs("rj", b)))
+                cp(half("go", b, 48), G(A("wp"), pairs("rj", b)), OPT["go"])
                 tt(half("ow", b, 48), G(A("wp"), pairs("ri", b)), half("go", b, 48), Op.is_gt)
         else:
-            tt(A("vv"), A("s4", 3, 64, 4), A("bv", lo, lo + 16), Op.add)
             for b in range(2):
-                tt(half("ow", b, 48), G(A("vv"), pairs("ri", b)), half("go", b, 48), Op.is_lt)
-                tt(half("eb", b), G(A("wp"), tab("p3", 4 * b, 4 * b + 4)), A("lr", 128, 192), Op.is_equal)
-        if rd:
-            differences(rd, A("bl", lo, lo + 16), "rj", "ri", frc, "bd")
-        else:
-            differences(rd, A("bp") if left[0] else A("b0"), "rj0", "ri0", frc, "bd")
+                tt(half("ow", b, 48), G(half("s4", rd), pairs("ri4", b)), half("od", b, 48), Op.is_lt)
+                tt(half("eb", b), G(A("wp"), tab("p3", 4 * b, 4 * b + 4)), half("lr", 2), Op.is_equal)
+        base = A("bl", lo, lo + 16) if rd else A("bp") if left[0] else A("b0")
         for b in range(2):
+            tt(half("tb", b, 48), G(base, pairs("rj" if rd else "rj0", b)), A("frc"), Op.add if left[rd] else Op.subtract)
+            tt(half("bd", b, 48), G(base, pairs("ri" if rd else "ri0", b)), half("tb", b, 48), Op.subtract)
             tt(half("ob", b, 48), half("ow", b, 48), half("bd", b, 48), Op.subtract if left[rd] else Op.add)
-        arrive(peer, [land], "w%d_" % rd, 1, OPT["far"])
+        calls = 3 - min(rd, 1) if left[rd] else 1
+        arrive(peer, [land], "w%d_" % rd, 1, 0.0,
+               [(flags, OPT["far"] + OPT["issue"] + 2 * OPT["wake"] + calls * (OPT["same"] + 80.0))])
         for b in range(2):
             c0, k0 = CW * b, 64 * b
             if left[rd]:
-                tt(A("kk", k0, k0 + 48), G(land, pairs("ri", b)), half("ob", b, 48), Op.is_lt)
+                tt(A("kk", k0, k0 + 48), G(land, pairs("ri4" if rd else "ri", b)), half("ob", b, 48), Op.is_lt)
             else:
                 tt(half("gp", b, 48), G(land, pairs("rj", b)), half("ob", b, 48), Op.subtract)
                 tt(A("kk", k0, k0 + 48), G(land, pairs("ri", b)), half("gp", b, 48), Op.is_gt)
+            if rd == 0 and b == 0:
+                at = [len(ops) - 1]
+                load("y", A("qw"), T.wc[:], True, at)
+                load("y", A("sw"), T.ws[:], False, at)
+                load("y", A("vt"), T.v[:], False, at)
             cp(half("ga", b), G(half("kk", b), tab("ag")), "s")
             scan(A("cw", c0, c0 + 16), A("kk", k0 + 32, k0 + 48), A("kk", k0 + 16, k0 + 32), Op.min, Op.max)
             cp(half("gb", b), G(A("cw", c0, c0 + 16), tab("bg")), "s")
@@ -570,13 +650,13 @@ def rank_program(g, core, T, topo):
             tt(half("pb", b), G(A("cw", c0 + 16, c0 + 80), tab("bi")), half("gb", b), Op.min)
             scan(A("cw", c0 + 80, c0 + CW), A("ra"), half("pb", b), Op.mult, Op.max)
             tt(half("pc", b), G(A("cw", c0, c0 + CW), tab("pp")), A("pw"), Op.mult)
-            scan(half("pq", b), A("r8", 0, 64), half("pc", b), Op.mult, Op.add)
+            scan(half("pq", b), half("r8", 0), half("pc", b), Op.mult, Op.add)
             if left[rd]:
-                tt(half("nq", b), G(half("pq", b), tab("p1e")), A("kr", 128, 192), Op.not_equal)
+                tt(half("nq", b), G(half("pq", b), tab("p1e")), half("kr", 2), Op.not_equal)
                 scan(half("ls", b), half("nq", b), half("dw", b), Op.mult, Op.add)
             else:
                 tt(half("sl", b), G(half("pq", b), tab("p1e")), half("eb", b), Op.mult)
-                scan(half("ls", b), A("r8", 0, 64), half("sl", b), Op.mult, Op.add)
+                scan(half("ls", b), half("r8", 0), half("sl", b), Op.mult, Op.add)
             ts(half("uz", b, 8), ends("ls", b), 16.0, Op.mult, col(8 + b), Op.add)
         tt(A("mv"), ends("pq"), A("lr", 128, 144), Op.not_equal)
         tt(A("um"), ends("pq"), A("lr", 128, 144), Op.is_equal)
@@ -587,23 +667,25 @@ def rank_program(g, core, T, topo):
         tr(A("ct"), A("cm"))
         rec("v", lambda e: e.tensor_reduce(ap(A("pre")), ap(A("ct")), AxisListType.X, Op.add), [A("pre")], [A("ct")])
         ts(A("us"), A("t2"), A("pre"), Op.add, col(11), Op.add)
-        for k in range(OPT["cut"]):
-            w = 16 // OPT["cut"]
-            cp(G(A("er"), half("us", k, w)), half("jr", k, 16 * w))
+        cp(G(A("er"), A("us")), A("jr"))
         tr(A("e2", 0, 96), A("er", 0, 96))
         tr(A("e2", 96, 192), A("er", 16, 112))
         cp(A("uf"), G(A("e2"), tab("pe", 0, 1)))
         for h in range(2):
             for b in range(4):
                 cp(A("zt", 512 * h + b, 512 * h + 512, 4), G(half("xp", b, 256), half("uz", h, 8)), OPT["z"][4 * h + b])
+                follow("z")
             quant("qz", "sz", 128 * h, 128, half("zt", h, 512))
             for b in range(4):
                 mm("ps%d" % (4 * h + b), "qw", "sw", 128 * b, "qz", "sz", 128 * h, 128)
-            for b in range(4):
-                cp(half("z32", 2 * b + h, 128), A("zt", 512 * h + b, 512 * h + 512, 4), OPT["z32"][4 * h + b], 32.0)
+            for k in range(len(OPT["z32"][h])):
+                w = 512 // len(OPT["z32"][h])
+                o = 512 * h + w * k
+                cp(A("z32", o, o + w), A("zt", o, o + w), OPT["z32"][h][k], 32.0)
             for b in range(4):
                 o = YS * b + 128 * h
-                tt(A("yw", o, o + 128), A("ps%d" % (4 * h + b), 0, 128), half("z32", 2 * b + h, 128), Op.add)
+                tt(A("yw", o, o + 128), A("ps%d" % (4 * h + b), 0, 128), A("z32", 512 * h + b, 512 * h + 512, 4), Op.add)
+                follow("y")
         for b in range(4):
             cp(A("ft", b, 4 * NT, 4), G(A("yw", YS * b, YS * b + 256), A("uf", 0, 6)), OPT["f"][b], 0.03125)
         quant("qf", "sf", 128 * rd, 128, A("ft"))
@@ -614,15 +696,14 @@ def rank_program(g, core, T, topo):
         for b in range(4):
             cp(half("f16", b, NT), A("ft", b, 4 * NT, 4), "s", 16.0)
         ts(A("t3", 0, 16), A("t2"), A("pre"), Op.add, NT + 0.5, Op.is_lt)
-        tt(A("t3", 16, 32), A("loc"), A("sg"), Op.subtract)
-        ts(A("t3", 32, 48), A("t3", 16, 32), A("pre"), Op.add, 255.0, Op.add)
-        tt(A("t1"), A("t3", 0, 16), A("t3", 32, 48), Op.mult)
-        tt(A("xd", 0, 16), A("t1"), A("sg"), Op.add)
-        tt(A("xd", 16, 32), A("t1"), A("sg"), Op.add)
+        ts(A("t3", 16, 32), A("t2"), A("pre"), Op.add, 255.0, Op.add)
+        tt(A("t1"), A("t3", 0, 16), A("t3", 16, 32), Op.mult)
+        for k in range(2):
+            tt(half("xd", k, 16), A("t1"), A("sg"), Op.max)
         tr(A("xt"), A("xd"))
         cp(A("ux"), G(A("xt"), tab("p32", 0, 1)))
         if rd < 2:
-            cp(A("wh", lo + 16, lo + 32), ends("ls"))
+            cp(A("wh", lo + 16, lo + 32), ends("ls"), OPT["wh"])
             prepare(rd + 1)
         else:
             cp(A("opf"), A("uz"))
@@ -633,13 +714,15 @@ def rank_program(g, core, T, topo):
             mm("ps%d" % (2 + b), "qe", "se", 128 * b, "qa", "sa", at_, 128)
         for b in (0, 2, 1, 3):
             tt(A("yw", YS * b + 256, YS * b + YS), A("ps%d" % (2 + b), 0, NT), half("f16", b, NT), Op.add)
+            follow("m")
         wq, wsc, res = ("qu2", "su2", "ssb") if rd < 2 else ("qv", "sv", "ysb")
         for h in range(2):
             for b in range(4):
                 cp(A("xs", 512 * h + b, 512 * h + 512, 4), G(half("yw", b, YS), half("ux", h, 8)), OPT["x"][4 * h + b], 0.03125)
+                follow("x")
             quant("qx", "sx", 128 * h, 128, half("xs", h, 512))
             mm("ps%d" % h, wq, wsc, 0, "qx", "sx", 128 * h, 128)
-            cp(half(res, h, 128), A("ps%d" % h, 0, 128), "sv"[h])
+            cp(half(res, h, 128), A("ps%d" % h, 0, 128), OPT["s"][h])
 
     store("y", T.oc[:, 0:512], T.qx[:, 0:128].bitcast(dt.uint8), A("qx", 0, 128))
     store("s", T.y[:, 0:128], T.ysb[:, 0:128], A("ysb", 0, 128))

from concourse.mybir import dt, AluOpType, AxisListType, ActivationFunctionType

F32, BF, I32, U16, U8, X4 = "float32", "bfloat16", "int32", "uint16", "uint8", "float8_e4m3fn_x4"
STEPS = [1, 2, 4]
NT = 96
YS = 256 + NT
UNIT = 0.0625
FARBELOW = -2.0 ** 90
OPT = {"vp": 17, "wake": 200.0, "same": 250.0, "far": 800.0, "issue": 150.0, "early": 2500.0, "late": 3500.0, "load": 1500.0,
       "base": 300.0, "z": "sssvsssv", "z32": ("s", "s"), "f": "sssv", "x": "ssvvssvv", "keep": "zxy", "s": "sv", "dw": "v",
       "go": "v", "wh": "v", "seed": 1, "passes": 3, "swaps": 2000, "heat": 50.0}

D1 = [(2, 3), (1, 3), (0, 3), (1, 2), (0, 2), (0, 3), (0, 1), (0, 0)]
D0 = [(0, 0), (1, 2), (0, 1), (0, 0), (0, 1), (2, 3), (0, 0), (0, 0)]
A_SLOT = [7, 6, 4, 2, 5, 7, 3, 1, 7, 0, 7]
A_FROM = [0, 1, 2, 3, 3, 1, 2, 3, 2, 3, 3]
ENDS = [4, 7, 9, 10]
STARTS = [0, 5, 8, 10, 11, 13]
B_FROM = [3, 2, 1, 0, 0, 2, 1, 0, 1, 0, 0, 0, 0, 0, 0, 0]
B_SLOT = [7, 0, 1, 2, 5, 7, 3, 4, 7, 6, 7, 7, 7, 7, 7, 7]
INTRA = [[(6, -1), (4, -1), (12, -1)], [(6, 1), (1, -1), (13, -1)], [(4, 1), (0, -1), (13, 1)], [(1, 1), (0, 1), (12, 1)]]
SHIFTS = [(0, 255), (8, 15), (12, 15), (16, 15), (20, 15)]
CW = 144


def pos_term(e, t):
    h, x = e // 4, e % 4
    if t < 4:
        return (80 + 16 * x + ENDS[3 - t], -1) if h == 0 else (80 + 16 * t + ENDS[3 - x], 1)
    if t < 6:
        return (8 * h + INTRA[x][t - 4][0], INTRA[x][t - 4][1])
    if t == 6:
        return (16 + 16 * h + INTRA[x][2][0], INTRA[x][2][1])
    return (7, 7 - e)


def tables():
    R = range(16)
    pos = [[pos_term(2 * c + r // 8, r % 8)[0] for r in R] for c in range(4)]
    f = [[pos[0], [r // 4 for r in R], [4 + r % 4 for r in R], B_FROM, A_SLOT + [2, 5, 3, 7, 7]],
         [pos[1], [D1[r % 8][0] + 4 * (r // 8) for r in R], [D1[r % 8][1] + 4 * (r // 8) for r in R],
          [0] * 16, A_SLOT + [10, 13, 11, 7, 7]],
         [pos[2], [D0[r % 8][0] + 4 * (r // 8) for r in R], [D0[r % 8][1] + 4 * (r // 8) for r in R],
          [6 * (r % 2) + 2 * (r // 2) if r < 6 else 0 for r in R], [1] * 11 + [0] * 5],
         [pos[3], A_FROM + [12] * 5, [0] * 16, [0] * 16, [8 + s for s in B_SLOT]]]
    out = [sum(f[k][t][r] << SHIFTS[t][0] for t in range(5)) for k in range(4) for r in R]
    row = ENDS + [0 if r in STARTS else 1 for r in R] + [pos_term(j // 8, j % 8)[1] + 8 for j in range(64)] + [0] * 6
    return out + [sum(row[5 * k + t] << SHIFTS[t][0] for t in range(5)) for k in range(18)]


PACKS = tables()
NP = len(PACKS)
TABS = {}
_at = [0]
for _n, _w in (("hx", 64), ("rep", 4), ("p3", 8), ("p2", 8), ("p1e", 4), ("ai", 4), ("ag", 4), ("bi", 4), ("bg", 4), ("pp", 4),
               ("pe", 2), ("p32", 2), ("pu", 8), ("p1", 8), ("pl", 2), ("pr", 4), ("p1o", 8), ("rj", 8), ("ri", 8), ("rj0", 8),
               ("ri0", 8), ("ri4", 8)):
    TABS[_n] = (_at[0], _w)
    _at[0] += _w
NTF = TABS["pe"][0] + 1

_B = {
    "x0": (1024, BF), "xs": (1024, BF), "xp": (1024, BF), "zt": (1024, BF), "z32": (1024, BF), "yw": (4 * YS, BF),
    "ft": (512, BF), "f16": (4 * NT, BF), "ut": (512, BF), "vt": (512, BF), "et": (516, BF),
    "qa": (3 * NT + 256, X4), "sa": (3 * NT + 256, U8), "qx": (256, X4), "sx": (256, U8), "qz": (256, X4), "sz": (256, U8),
    "qf": (384, X4), "sf": (384, U8), "qu": (128, X4), "su": (128, U8), "qu2": (128, X4), "su2": (128, U8),
    "qv": (128, X4), "sv": (128, U8), "qw": (512, X4), "sw": (512, U8), "qe": (512, X4), "se": (512, U8),
    "ssb": (256, F32), "sl0": (256, F32), "ysb": (256, F32), "g1": (128, F32), "fr": (128, BF), "fl": (128, BF),
    "phi": (32, I32), "pf": (32, BF), "pt": (32, BF), "hf": (32, BF), "ht": (32, BF), "hb": (32, BF), "wa": (16, BF),
    "wh": (48, BF), "absb": (16, BF), "dd": (16, BF), "dx": (16, BF), "px": (16, BF), "wp": (16, BF), "vs": (48, BF),
    "wl": (48, BF), "wr": (128, BF), "b0": (32, BF), "bl": (48, BF), "bv": (48, BF), "dw": (128, BF), "dt_": (128, BF),
    "nq": (128, BF), "n2": (128, BF), "ni": (128, BF), "hs": (128, BF), "ls": (128, BF), "pq": (128, BF), "sl": (128, BF),
    "eb": (128, BF), "e4": (128, BF), "p4": (64, BF), "s4": (192, BF), "bs": (128, BF), "bp": (128, BF), "np_": (128, BF),
    "go": (96, BF), "od": (96, BF), "ow": (96, BF), "ob": (96, F32), "tb": (96, F32), "bd": (96, F32), "gp": (96, F32),
    "kk": (128, BF), "frc": (48, BF), "cw": (2 * CW, BF), "ga": (128, BF), "gb": (128, BF), "pa": (128, BF), "pb": (128, BF),
    "pc": (128, BF), "pw": (64, BF), "ra": (64, BF), "r8": (128, BF), "r16": (128, BF), "dc": (128, BF), "cr": (64, BF),
    "ka": (128, BF), "mv": (16, F32), "um": (16, F32), "loc": (16, F32), "t1": (16, F32), "t2": (16, F32), "t3": (32, F32),
    "cm": (32, F32), "ct": (32, F32), "pre": (1, F32), "m32": (32, F32), "ma": (64, F32), "cu": (16, F32),
    "sg": (16, F32), "xd": (32, F32), "xt": (32, F32), "er": (816, BF), "e2": (192, BF), "opf": (16, F32),
    "uz": (16, U16), "uu": (16, U16), "us": (16, U16), "uf": (16, U16), "ux": (16, U16), "hn": (16, U16), "tab": (_at[0], U16),
    "tf": (NTF, F32), "pi": (1, I32), "ci": (8, I32), "col": (24, F32), "rows": (32, F32), "jr": (256, BF), "kr": (256, BF),
    "lr": (256, BF), "q16": (64, BF), "pk": (NP, F32), "pki": (26, I32), "rwi": (130, I32), "rw": (130, F32),
    "dg": (192, F32), "z1": (2, F32),
}
PLACE = {n: (n, 0) for n in _B}
for _h, _d, _l in (("slots", F32, "mv um loc t1 t2 t3 cm ct xd xt pre"), ("words", BF, "dd dx px wp"),
                   ("steps", BF, "pa pb pc ga gb nq sl"), ("picks", BF, "n2 ni np_ hs bs bp")):
    _w = 0
    for _n in _l.split():
        PLACE[_n] = (_h, _w)
        _w += -(-_B[_n][0] // 16) * 16
    _B[_h], PLACE[_h] = (_w, _d), (_h, 0)
SCRATCH = {n: ("sbuf", [128, w], d) for n, (w, d) in _B.items() if PLACE[n][0] == n}
for _i in range(8):
    SCRATCH["ps%d" % _i] = ("psum", [128, 512], F32)
POOL = {"v": 56, "s": 34, "t": 16, "g": 12, "d": 22}
SEMAPHORES = ([k + str(i) for k, n in POOL.items() for i in range(n)] + ["sent"]
              + ["%s%d_" % (k, i) for k in "bwf" for i in range(3)])


def arrange(ops, before):
    N = len(ops)
    busy, queue = [o["busy"] for o in ops], [o["q"] for o in ops]
    up, down = [[] for o in ops], [[] for o in ops]
    for n, o in enumerate(ops):
        edges = list(o["since"])
        for m in before[n] | set(o["hint"]):
            wake = OPT["same" if queue[n] == queue[m] else "wake"]
            edges.append((m, o["far"] + (ops[m]["lag"] + wake if m in before[n] or queue[n] is None else 0.0)))
        for m, d in edges:
            up[n].append((m, d))
            down[m].append((n, d))

    def lay(order, edges):
        end, taken = {}, {k: [] for k in queue}
        for n in order:
            t = max([0.0] + [end[m] + d for m, d in edges[n]])
            if queue[n] is not None:
                l, i = taken[queue[n]], 0
                while i < len(l) and t + busy[n] > l[i][0]:
                    t = max(t, l[i][1])
                    i += 1
                l.insert(i, (t, t + busy[n]))
            end[n] = t + busy[n]
        return end
    best, seed, rest = None, OPT["seed"], [0.0] * N
    for n in range(N - 1, -1, -1):
        rest[n] = busy[n] + max([0.0] + [rest[m] + d for m, d in down[n]])
    for k in range(OPT["passes"]):
        end = lay(sorted(range(N), key=lambda n: (-rest[n], n)), up)
        if best is None or end[N - 1] < best[N - 1]:
            best = end
        rest = lay(sorted(range(N), key=lambda n: (-end[n], -n)), down)
    order = sorted(range(N), key=lambda k: (best[k] - busy[k], k))
    ups = [set(m for m, d in up[n]) for n in range(N)]

    def timed(order, i, end, why):
        end, why, last = list(end), list(why), {}
        for n in order[i - 1::-1] if i else []:
            if queue[n] not in last:
                last[queue[n]] = n
                if len(last) == 6:
                    break
        for n in order[i:]:
            t, w = 0.0, -1
            for m, d in up[n]:
                if end[m] + d > t:
                    t, w = end[m] + d, m
            q = queue[n]
            if q is not None:
                m = last.get(q, -1)
                if m >= 0 and end[m] > t:
                    t, w = end[m], -2 - m
                last[q] = n
            end[n], why[n] = t + busy[n], w
        return end, why
    end, why = timed(order, 0, [0.0] * N, [-1] * N)
    top, keep, held = end[N - 1], order, None
    for trial in range(OPT["swaps"]):
        if held is None:
            held, n = [], N - 1
            while why[n] != -1:
                if why[n] < -1:
                    held.append((n, -2 - why[n]))
                n = why[n] if why[n] >= 0 else -2 - why[n]
        if not held:
            break
        seed = (seed * 1103515245 + 12345) % 2147483648
        n, m = held[(seed >> 8) % len(held)]
        i, j = order.index(m), order.index(n)
        for k in range((seed >> 20) % 3):
            i2 = i - 1
            while i2 >= 0 and queue[order[i2]] != queue[n]:
                i2 -= 1
            if i2 >= 0:
                i = i2
        move = {n}
        for k in range(j - 1, i - 1, -1):
            for x in move:
                if order[k] in ups[x]:
                    move.add(order[k])
                    break
        if order[i] in move:
            continue
        mid = order[i:j + 1]
        new = order[:i] + [x for x in mid if x in move] + [x for x in mid if x not in move] + order[j + 1:]
        e2, w2 = timed(new, i, end, why)
        seed = (seed * 1103515245 + 12345) % 2147483648
        if e2[N - 1] <= end[N - 1] + OPT["heat"] * (1.0 - trial / OPT["swaps"]) * seed / 2147483648.0:
            order, end, why, held = new, e2, w2, None
            if end[N - 1] < top:
                top, keep = end[N - 1], order
    OPT["span"] = OPT.get("span", []) + [int(top)]
    return keep


def emit(g, T, ops):
    qs = {"v": g.vector, "s": g.scalar, "t": g.tensor, "g": g, "y": g.sync}
    masks = {}

    def mask(a):
        if a not in masks:
            masks[a] = sum(1 << c for c in range(a[1], a[2], a[3]))
        return masks[a]
    seen, before = {}, []
    for n, o in enumerate(ops):
        deps = set(o["after"])
        acc = [(a, False) for a in o["r"]] + [(a, True) for a in o["w"]]
        for a, wr in acc:
            ps = a[0][:2] == "ps"
            for m, mk, w2, q2 in seen.get(a[0], []):
                if (ps and (wr or w2 or q2 != o["q"])) or (not ps and (wr or w2) and mk & mask(a)):
                    deps.add(m)
        for a, wr in acc:
            seen.setdefault(a[0], []).append((n, mask(a), wr, o["q"]))
        before.append(deps)
    order = arrange(ops, before)
    place = {m: i for i, m in enumerate(order)}
    before = [[place[m] for m in before[n]] for n in order]
    ops = [ops[n] for n in order]
    known, at, waits, signals = {k: 0 for k in qs}, [], [], set()
    for n, o in enumerate(ops):
        ws = []
        if o["q"] is not None:
            for m in sorted(before[n], reverse=True):
                if not known[o["q"]] >> m & 1:
                    ws.append(m)
                    signals.add(m)
                    known[o["q"]] |= at[m] | 1 << m
        at.append(known[o["q"]] if o["q"] is not None else 0)
        waits.append(ws)
    used, holder, sem = {k: 0 for k in POOL}, {}, {}
    for n, o in enumerate(ops):
        if o["q"] is None:
            sem[n] = o["sem"]
            continue
        ws = list(waits[n])
        if n in signals:
            k = "d" if o["dma"] else o["q"]
            name = k + str(used[k] % POOL[k])
            step = 16 if o["dma"] else 1
            sem[n] = (name, step * (used[k] // POOL[k] + 1), step)
            used[k] += 1
            if name in holder and not at[n] >> holder[name] & 1:
                ws.append(holder[name])
            holder[name] = n
        for m in ws:
            qs[o["q"]].wait_ge(T.sem[sem[m][0]], sem[m][1])
        if o["fn"] is not None:
            i = o["fn"](qs[o["q"]])
            if n in signals:
                i.then_inc(T.sem[sem[n][0]], sem[n][2])


def rank_program(g, core, T, topo):
    rank = T.rank_of(core)
    if rank is None:
        return
    Op, Act = AluOpType, ActivationFunctionType
    ops = []

    def A(n, lo=0, hi=None, st=1):
        if n[:2] == "ps":
            return (n, lo, hi, st)
        buf, at = PLACE[n]
        return (buf, at + lo, at + (_B[n][0] if hi is None else hi), st)

    def tab(n, a=0, b=None, buf="tab"):
        return A(buf, TABS[n][0] + a, TABS[n][0] + (TABS[n][1] if b is None else b))

    def tf(n, a=0, b=None):
        return tab(n, a, b, "tf")

    def G(win, off):
        return ("*", win, off)

    def col(k):
        return A("col", k, k + 1)

    def one(n, k):
        return A(n, k, k + 1)

    def half(n, b, w=64):
        return A(n, w * b, w * b + w)

    def ends(n, b=None):
        return A(n, 7, 128, 8) if b is None else A(n, 64 * b + 7, 64 * b + 64, 8)

    def pairs(n, b):
        return tab(n, 4 * b, 4 * b + 3)

    def ap(a):
        if not isinstance(a, tuple):
            return a
        if a[0] == "*":
            return ap(a[1]).indirect(ap(a[2]))
        return T[a[0]][:, a[1]:a[2]:a[3]] if a[3] != 1 else T[a[0]][:, a[1]:a[2]]

    def rec(q, fn, outs, ins, dma=False, after=(), sem=None, hint=(), per=0, far=0.0, since=()):
        r, w = [], []
        for a in ins:
            if isinstance(a, tuple):
                r += [a[1], a[2]] if a[0] == "*" else [a]
        for a in outs:
            if a[0] == "*":
                w.append(a[1])
                r.append(a[2])
            else:
                w.append(a)
        wide = lambda a: 16 * (a[2][2] - a[2][1]) if a[0] == "*" else len(range(a[1], a[2], a[3]))
        n = wide(outs[0]) if outs else 0
        full = [a for a in ins if isinstance(a, tuple) and (a[0] == "*" or wide(a) == n)]
        lag = 0.0
        if q is None or fn is None:
            busy = 0.0
        elif dma:
            busy, lag = 60.0, OPT["load"] + 1.0 * (n if outs else wide(ins[0]))
        elif q == "g":
            busy = 170.0 + 2.2 * n if outs else OPT["issue"]
        elif q == "t":
            busy = 0.6 * n + 10.0
        elif outs[0][0] == "*":
            busy = 50.0 + 3.2 * n
        elif [a for a in full if a[0] == "*"]:
            busy = (65.0 if q == "s" else 50.0) + 1.3 * n
        elif len(outs) == 2:
            busy = 12.0 + 0.88 * n
        elif q == "s":
            busy = 50.0 + 0.83 * n
        else:
            two = not [a for a in full + outs if SCRATCH[a[0]][2] not in (BF, U16)]
            both = len(full) == 2 and per == 0 and not [a for a in full if a[0][:2] == "ps"]
            busy = 0.83 * max(64.0, n * (2.0 if both else 0.5 if two else 1.0))
        ops.append({"q": q, "fn": fn, "r": r, "w": w, "dma": dma, "after": list(after), "sem": sem, "busy": busy, "lag": lag,
                    "hint": list(hint), "far": far, "since": list(since)})
        return len(ops) - 1

    runs = {}

    def follow(name):
        key = (name, ops[-1]["q"])
        if name in OPT["keep"]:
            ops[-1]["hint"] += runs.get(key, [])
        runs[key] = [len(ops) - 1]

    def tt(o, a, b, op):
        rec("v", lambda e: e.tensor_tensor(ap(o), ap(a), ap(b), op), [o], [a, b])

    def ts(o, a, s1, op0, s2=None, op1=None):
        if op1 is None:
            rec("v", lambda e: e.tensor_scalar(ap(o), ap(a), ap(s1), None, op0), [o], [a, s1], per=1)
        else:
            rec("v", lambda e: e.tensor_scalar(ap(o), ap(a), ap(s1), ap(s2), op0, op1), [o], [a, s1, s2], per=1)

    def cp(o, a, q="v", scale=None):
        if q == "s":
            if scale is None:
                rec("s", lambda e: e.activation(ap(o), ap(a), Act.Copy), [o], [a])
            else:
                rec("s", lambda e: e.activation(ap(o), ap(a), Act.Copy, scale=scale), [o], [a])
        elif scale is None:
            rec("v", lambda e: e.tensor_copy(ap(o), ap(a)), [o], [a])
        else:
            ts(o, a, scale, Op.mult)

    def af(o, a, scale=1.0, bias=0.0, func=Act.Identity):
        rec("s", lambda e: e.activation(ap(o), ap(a), func, bias=ap(bias), scale=ap(scale)), [o], [a, scale, bias])

    def fill(o, c):
        af(o, A("lr", 0, len(range(o[1], o[2], o[3]))), 0.0, c)

    def ms(o, c):
        rec("v", lambda e: e.memset(ap(o), c), [o], [])

    def scan(o, d0, d1, op0, op1):
        return rec("v", lambda e: e.tensor_tensor_scan(ap(o), ap(d0), ap(d1), 0.0, op0, op1), [o], [d0, d1], per=1)

    def tr(o, a):
        rec("v", lambda e: e.transpose(ap(o), ap(a)), [o], [a])

    def iota(o, pat, base, cm, hint=()):
        if SCRATCH[o[0]][2] == I32:
            rec("g", lambda e: e.iota(ap(o), pat, base, cm), [o], [], hint=hint)
        else:
            rec("g", lambda e: e.iota(ap(o), pat, base, cm, allow_small_or_imprecise_dtypes=True), [o], [], hint=hint)

    def quant(q, s, lo, n, a):
        o1, o2 = A(q, lo, lo + n), A(s, lo, lo + n)
        rec("v", lambda e: e.quantize_mx(ap(o1), ap(o2), ap(a)), [o1, o2], [a])

    def mm(ps, wq, ws_, wlo, xq, xs_, xlo, n):
        o = A(ps, 0, n)
        a = [A(wq, wlo, wlo + 128), A(ws_, wlo, wlo + 128), A(xq, xlo, xlo + n), A(xs_, xlo, xlo + n)]
        rec("t", lambda e: e.matmul_mx(ap(o), ap(a[0]), ap(a[1]), ap(a[2]), ap(a[3]), True, True), [o], a)

    stores, loads = [], {}

    def load(q, o, src, codes=False, after=()):
        loads[q] = [rec(q, lambda e: e.dma_start(ap(o).bitcast(dt.uint8) if codes else ap(o), src), [o], [], dma=True,
                        hint=loads.get(q, []), after=after)]

    def store(q, dst, src, a):
        stores.append(rec(q, lambda e: e.dma_start(dst, src), [], [a], dma=True))

    sent, last = [0], []

    def send(peer, dst, src, sem, codes=False):
        rid, pid = topo.addr(peer)[0], topo.addr(peer)[1]
        m = topo.mask(core, peer)
        view = (lambda a: ap(a).bitcast(dt.uint8)) if codes else ap
        n = rec("g", lambda e: e.remote_dma(view(dst), view(src), T.sem[sem], T.sem.sent, pid, rid, m), [], [src], hint=last[-1:])
        if not last:
            ops[n]["busy"] = OPT["early"]
        last.append(n)
        sent[0] += len(topo.engines(core, peer))

    def arrive(peer, outs, sem, writes, far, since=(), own=None):
        rec(None, None, outs, [], sem=(sem, writes * len(topo.engines(peer, core))), hint=own or last[-1:], far=far, since=since)

    left = [rank < rank ^ s for s in STEPS]
    peers = [T.cores[rank ^ s] for s in STEPS]
    lr, kr = A("lr", 128, 256), A("kr", 128, 256)

    load("y", A("phi", 0, 16), T.p[:])
    load("s", A("ut"), T.u[:])
    load("y", A("x0", 0, 512), T.x[:, 0:512])
    load("s", A("x0", 512, 1024), T.x[:, 512:1024])
    load("y", A("phi", 16, 32), T.h[:])

    a8, c8, c4 = A("rows", 0, 8), A("jr", 0, 8), A("jr", 0, 4)
    iota(A("pi"), [[0, 1]], 0, 1)
    iota(A("jr", 0, 32), [[1, 32]], 0, 0)
    iota(A("q16"), [[0, 4], [1, 16]], 0, 0)
    iota(a8, [[8, 2], [0, 4]], 0, 0)
    iota(A("rows", 16, 32), [[8, 2], [0, 8]], 0, 0)
    iota(A("lr", 0, 128), [[0, 16], [1, 8]], 0, 0)
    iota(A("kr", 0, 64), [[1, 8], [0, 8]], 0, 0)
    ms(one("z1", 0), 0.0)
    ms(one("z1", 1), 1.0)
    ms(A("et"), 0.0)
    for k in range(0, NP, 2):
        if k < 2 * OPT["vp"]:
            ts(A("pk", k, k + 2), A("z1"), float(PACKS[k + 1] - PACKS[k]), Op.mult, float(PACKS[k]), Op.add)
        else:
            af(A("pk", k, k + 2), A("z1"), float(PACKS[k + 1] - PACKS[k]), float(PACKS[k]))
    for k, an in enumerate((15, 7, 31, 14, 3, 8, 16)):
        ts(one("ci", k), A("pi"), an, Op.bitwise_and)
    cp(A("col", 0, 7), A("ci", 0, 7))
    for k, src, scale, bias in ((7, 5, 0.125, 0.0), (8, 0, 16.0, 0.0), (9, 0, 16.0, 8.0), (10, 6, UNIT, 0.0), (11, 6, 1.0, -1.0),
                                (12, 5, 1.0, 7.0), (13, 1, 8.0, 7.0), (14, 4, 16.0, 15.0), (18, 0, 1.0, 4.0)):
        if k != 14 or not all(left):
            af(col(k), col(src), scale, bias)
    af(lr, A("lr", 0, 128), UNIT)
    for b in range(2 - all(left)):
        af(half("kr", 2 + b), A("kr", 0, 64), UNIT)
    af(A("absb"), A("rows", 16, 32), UNIT, col(0))
    cp(tab("p32", 0, 1), col(2))
    ts(tab("pu"), c8, 16.0, Op.mult)
    ts(tab("p1"), a8, col(1), Op.add)
    ts(tab("pl", 0, 1), col(3), 8.0, Op.mult, 15.0, Op.add)
    if not all(left):
        ts(tab("pr"), A("rows", 0, 8, 2), 8.0, Op.mult, col(14), Op.add)
    af(tf("rep"), c4, 0.0, col(18))
    af(tf("p3"), c8, 2.0, col(7))
    af(tf("p2"), c8, 16.0, col(12))
    af(tf("p1e"), c4, 0.0, col(13))
    cp(A("tab", TABS["rep"][0], TABS["ai"][0]), A("tf", TABS["rep"][0], TABS["ai"][0]))
    ts(A("cr"), A("q16"), col(0), Op.not_equal, FARBELOW, Op.mult)
    af(A("r8"), A("lr", 0, 128), func=Act.Sign)
    for b in range(2):
        af(half("r16", b), A("q16"), func=Act.Sign)
        fill(A("kk", 64 * b + 48, 64 * b + 64), 1.0)
    fill(A("dc"), -UNIT)
    fill(ends("dc"), 7 * UNIT)
    fill(A("frc"), 0.0)
    fill(A("frc", 23, 32, 8), 2.0)
    for lo, hi, st in ((32, 39, 3), (40, 47, 3), (39, 48, 8)):
        fill(A("frc", lo, hi, st), -2.0)
    af(A("cu"), A("jr", 0, 16), 1.0, col(8))
    af(A("cu"), A("cu"), 1.0, 273.0)
    ts(A("ma", 0, 32), A("jr", 0, 32), col(2), Op.is_gt)
    ts(A("ma", 32, 64), A("jr", 0, 32), 15.5, Op.is_gt, col(10), Op.is_equal)
    tt(A("m32"), A("ma", 0, 32), A("ma", 32, 64), Op.mult)
    fill(A("er", 0, 112), 0.0)
    fill(A("ft", 4 * NT, 512), 0.0)
    ts(A("dg", 0, 64), A("q16"), col(0), Op.is_equal)
    tt(A("dg", 64, 128), A("pk", 0, 64), A("dg", 0, 64), Op.mult)
    cp(A("pki", 8, 26), A("pk", 64, NP))
    scan(A("dg", 128, 192), A("r16", 0, 64), A("dg", 64, 128), Op.mult, Op.add)
    cp(A("pki", 0, 4), A("dg", 143, 192, 16))
    ts(A("pki", 4, 8), A("dg", 143, 192, 16), float((8 << SHIFTS[1][0]) + (8 << SHIFTS[2][0])), Op.add)
    for t in range(5):
        ts(A("rwi", t, 130, 5), A("pki"), SHIFTS[t][0], Op.logical_shift_right, SHIFTS[t][1], Op.bitwise_and)
    cp(A("rw"), A("rwi"))
    for n, c0 in (("rj", 2), ("ri", 1)):
        f = A("rw", c0, 40, 5)
        cp(tab(n), f)
        if left[0]:
            ts(tab(n + "0"), f, 8.0, Op.mult, 7.0, Op.add)
        else:
            ts(tab(n + "0"), f, col(6), Op.add)
    ts(tab("ri4"), A("rw", 1, 40, 5), 4.0, Op.mult, 3.0, Op.add)
    af(col(15), one("rw", 3), 16.0)
    af(col(16), one("rw", 13), 16.0)
    af(col(17), one("rw", 16), 4.0)
    for k in range(2):
        af(tf("ai", 2 * k, 2 * k + 2), A("rw", 4, 10, 5))
    af(tf("bg"), c4, 0.0, one("rw", 19))
    af(tf("pp"), A("rw", 0, 20, 5))
    af(tf("bi"), A("rw", 40, 44), 1.0, col(15))
    af(tf("ag"), c4, one("rw", 14), col(17))
    af(tf("pe", 0, 1), col(16), 1.0, col(6))
    cp(A("tab", TABS["ai"][0], NTF), A("tf", TABS["ai"][0], NTF))
    cp(A("ra"), G(A("rw", 40, 64), tab("rep")), "s")
    af(A("pw"), A("rw", 60, 124), UNIT, -8 * UNIT)

    def places(n, s, word, where, letters):
        tt(A(n), G(word, where), letters, Op.not_equal)
        scan(A(s), A(n), A("dc"), Op.mult, Op.add)

    def prepare(rd):
        lo = 16 * rd
        w = A("wh", lo, lo + 16)
        if rd:
            tt(A("n2"), G(A("ls"), tab("p2")), lr, Op.not_equal)
            scan(A("hs"), A("n2"), A("dt_"), Op.mult, Op.add)
            cp(A("uu", 8, 16), A("hs", 15, 128, 16))
            cp(A("uu", 0, 8), A("hs", 7, 128, 16))
        else:
            cp(A("wa"), G(A("pt"), tab("p32", 0, 1)))
            for k in range(2):
                cp(half("uu", k, 8), A("wa", k, 16, 2), "v", 16.0)
        tt(A("dx", 0, 16, 2), A("wh", lo + 1, lo + 16, 2), A("wh", lo, lo + 16, 2), Op.subtract)
        tt(A("dx", 1, 16, 2), A("wh", lo, lo + 16, 2), A("wh", lo + 1, lo + 16, 2), Op.subtract)
        base = w
        if not left[rd]:
            places("ni", "bs", w, tab("p1"), kr)
            base = A("bv", lo, lo + 16)
            cp(base, ends("bs"), OPT["wh"])
            tt(A("e4", 64, 128), A("ni", 1, 128, 2), A("ni", 0, 128, 2), Op.subtract)
            cp(A("e4", 0, 64), A("e4", 64, 128), "s", 1.5 * UNIT)
            for b in range(2):
                cp(half("go", b, 48), G(base, pairs("ri", b)), "s")
                tt(half("od", b, 48), G(base, pairs("rj", b)), half("go", b, 48), Op.subtract)
        if rd:
            send(peers[rd], A("bl", lo, lo + 16), base, "b%d_" % rd)
            arrive(peers[rd], [A("bl", lo, lo + 16)], "b%d_" % rd, 1, OPT["late"])

    for b in range(2):
        cp(half("pf", b, 16), A("phi", 0, 16), "v", UNIT)
        cp(half("hf", b, 16), A("phi", 16, 32))
    tr(A("pt"), A("pf"))
    send(peers[0], A("b0"), A("pt"), "b0_")
    tr(A("ht"), A("hf"))
    tt(A("wh", 0, 16), G(A("pt"), tab("p32", 0, 1)), A("absb"), Op.subtract)
    cp(A("hb", 0, 16), G(A("ht"), tab("p32", 0, 1)))
    tt(A("hb", 16, 31), A("hb", 0, 15), A("hb", 1, 16), Op.subtract)
    cp(A("hb", 23, 32, 8), A("hb", 7, 16, 8))
    cp(A("dt_"), G(A("hb", 16, 32), tab("p1")), "s")
    for b in range(4):
        af(tf("hx", 16 * b, 16 * b + 16), A("hf", 0, 16), 4.0, float(b))
    cp(tab("hx"), tf("hx"))
    quant("qu", "su", 0, 128, A("ut"))
    cp(A("su2"), G(A("su"), tab("pu")), "s")
    rec("v", lambda e: e.tensor_copy(T.qu2[:, 0:128].bitcast(dt.uint32), T.qu[:, 0:128].bitcast(dt.uint32).indirect(ap(tab("pu")))),
        [A("qu2")], [G(A("qu"), tab("pu"))])
    prepare(0)
    if left[0]:
        ts(tab("p1o"), a8, col(1), Op.add, col(6), Op.add)
        af(half("ka", 0), half("kr", 2), 1.0, col(0))
        af(half("ka", 1), half("ka", 0), 1.0, 8 * UNIT)
    for h in range(2):
        quant("qa", "sa", 3 * NT + 128 * h, 128, half("x0", h, 512))
        mm("ps%d" % h, "qu2", "su2", 0, "qa", "sa", 3 * NT + 128 * h, 128)
        cp(half("ssb", h, 128), A("ps%d" % h, 0, 128), "sv"[h])
    cp(A("hn"), A("phi", 16, 32))
    for b in range(2):
        cp(half("sl0", b, 128), G(A("ssb"), half("hn", b, 8)), "vs"[b])

    for rd in range(3):
        peer, lo = peers[rd], 16 * rd
        wh, land, change = A("wh", lo, lo + 16), A("wl", lo, lo + 16), A("vs", lo, lo + 16)
        scores = A("ssb" if rd else "sl0")
        for b in range(2):
            tt(half("g1", b), G(scores, half("uu", 2 + b, 4)), A("cr"), Op.add)
        for b in range(2):
            tt(half("fr", b), G(scores, half("uu", b, 4)), half("g1", b), Op.is_lt)
        flags = scan(A("fl"), A("r16"), A("fr"), Op.mult, Op.add)
        px = change if left[rd] else A("px")
        if not left[rd]:
            tt(A("p4"), G(A("fl"), tab("pr")), A("e4", 0, 64), Op.mult)
            scan(half("s4", rd), A("r8", 0, 128, 2), A("p4"), Op.mult, Op.add)
            if rd:
                change = half("s4", rd)
            else:
                cp(change, A("s4", 3, 64, 4))
        tt(px, G(A("fl"), tab("pl", 0, 1)), A("dx"), Op.mult)
        send(peer, half("wr", rd - 1) if rd and not left[rd] else land, change, "w%d_" % rd)
        if rd and left[rd]:
            land = half("wr", rd - 1)
        if rd == 0:
            iota(A("jr", 32, 256), [[1, 224]], 32, 0, last[-1:])
            af(A("sg"), A("jr", 0, 256, 16), 1.0, col(0))
            rec("g", lambda e: e.affine_select(T.et[:], T.et[:], [[-1, 516]], Op.not_equal, 16.0, 3, 4), [A("et")], [A("et")],
                hint=last[-1:])
            for b in range(4):
                quant("qe", "se", 128 * b, 128, A("et", 3 - b, 515 - b))
            arrive(peer, [A("b0")], "b0_", 1, 0.0, [(flags, OPT["base"])], last[:1])
            if left[0]:
                places("np_", "bp", A("b0"), tab("p1o"), A("ka"))
        for b in range(4):
            cp(half("xp", b, 256), G(A("xs" if rd else "x0"), tab("hx", 16 * b, 16 * b + 16)), "s")
        tt(A("wp"), px, wh, Op.add)
        if left[rd]:
            tt(A("dd", 0, 15), A("wp", 0, 15), A("wp", 1, 16), Op.subtract)
            cp(A("dd", 7, 16, 8), A("wp", 7, 16, 8))
            cp(A("dw"), G(A("dd"), tab("p1")), OPT["dw"])
            for b in range(2):
                cp(half("go", b, 48), G(A("wp"), pairs("rj", b)), OPT["go"])
                tt(half("ow", b, 48), G(A("wp"), pairs("ri", b)), half("go", b, 48), Op.is_gt)
        else:
            for b in range(2):
                tt(half("ow", b, 48), G(half("s4", rd), pairs("ri4", b)), half("od", b, 48), Op.is_lt)
                tt(half("eb", b), G(A("wp"), tab("p3", 4 * b, 4 * b + 4)), half("lr", 2), Op.is_equal)
        base = A("bl", lo, lo + 16) if rd else A("bp") if left[0] else A("b0")
        for b in range(2):
            tt(half("tb", b, 48), G(base, pairs("rj" if rd else "rj0", b)), A("frc"), Op.add if left[rd] else Op.subtract)
            tt(half("bd", b, 48), G(base, pairs("ri" if rd else "ri0", b)), half("tb", b, 48), Op.subtract)
            tt(half("ob", b, 48), half("ow", b, 48), half("bd", b, 48), Op.subtract if left[rd] else Op.add)
        calls = 3 - min(rd, 1) if left[rd] else 1
        arrive(peer, [land], "w%d_" % rd, 1, 0.0,
               [(flags, OPT["far"] + OPT["issue"] + 2 * OPT["wake"] + calls * (OPT["same"] + 80.0))])
        for b in range(2):
            c0, k0 = CW * b, 64 * b
            if left[rd]:
                tt(A("kk", k0, k0 + 48), G(land, pairs("ri4" if rd else "ri", b)), half("ob", b, 48), Op.is_lt)
            else:
                tt(half("gp", b, 48), G(land, pairs("rj", b)), half("ob", b, 48), Op.subtract)
                tt(A("kk", k0, k0 + 48), G(land, pairs("ri", b)), half("gp", b, 48), Op.is_gt)
            if rd == 0 and b == 0:
                at = [len(ops) - 1]
                load("y", A("qw"), T.wc[:], True, at)
                load("y", A("sw"), T.ws[:], False, at)
                load("y", A("vt"), T.v[:], False, at)
            cp(half("ga", b), G(half("kk", b), tab("ag")), "s")
            scan(A("cw", c0, c0 + 16), A("kk", k0 + 32, k0 + 48), A("kk", k0 + 16, k0 + 32), Op.min, Op.max)
            cp(half("gb", b), G(A("cw", c0, c0 + 16), tab("bg")), "s")
            tt(half("pa", b), G(A("cw", c0, c0 + 16), tab("ai")), half("ga", b), Op.min)
            scan(A("cw", c0 + 16, c0 + 80), A("ra"), half("pa", b), Op.mult, Op.max)
            tt(half("pb", b), G(A("cw", c0 + 16, c0 + 80), tab("bi")), half("gb", b), Op.min)
            scan(A("cw", c0 + 80, c0 + CW), A("ra"), half("pb", b), Op.mult, Op.max)
            tt(half("pc", b), G(A("cw", c0, c0 + CW), tab("pp")), A("pw"), Op.mult)
            scan(half("pq", b), half("r8", 0), half("pc", b), Op.mult, Op.add)
            if left[rd]:
                tt(half("nq", b), G(half("pq", b), tab("p1e")), half("kr", 2), Op.not_equal)
                scan(half("ls", b), half("nq", b), half("dw", b), Op.mult, Op.add)
            else:
                tt(half("sl", b), G(half("pq", b), tab("p1e")), half("eb", b), Op.mult)
                scan(half("ls", b), half("r8", 0), half("sl", b), Op.mult, Op.add)
            ts(half("uz", b, 8), ends("ls", b), 16.0, Op.mult, col(8 + b), Op.add)
        tt(A("mv"), ends("pq"), A("lr", 128, 144), Op.not_equal)
        tt(A("um"), ends("pq"), A("lr", 128, 144), Op.is_equal)
        scan(A("loc"), A("kk", 48, 64), A("mv"), Op.mult, Op.add)
        tt(A("t1"), A("um"), A("cu"), Op.mult)
        ts(A("cm"), A("m32"), A("loc", 15, 16), Op.mult)
        tt(A("t2"), A("t1"), A("loc"), Op.add)
        tr(A("ct"), A("cm"))
        rec("v", lambda e: e.tensor_reduce(ap(A("pre")), ap(A("ct")), AxisListType.X, Op.add), [A("pre")], [A("ct")])
        ts(A("us"), A("t2"), A("pre"), Op.add, col(11), Op.add)
        cp(G(A("er"), A("us")), A("jr"))
        tr(A("e2", 0, 96), A("er", 0, 96))
        tr(A("e2", 96, 192), A("er", 16, 112))
        cp(A("uf"), G(A("e2"), tab("pe", 0, 1)))
        for h in range(2):
            for b in range(4):
                cp(A("zt", 512 * h + b, 512 * h + 512, 4), G(half("xp", b, 256), half("uz", h, 8)), OPT["z"][4 * h + b])
                follow("z")
            quant("qz", "sz", 128 * h, 128, half("zt", h, 512))
            for b in range(4):
                mm("ps%d" % (4 * h + b), "qw", "sw", 128 * b, "qz", "sz", 128 * h, 128)
            for k in range(len(OPT["z32"][h])):
                w = 512 // len(OPT["z32"][h])
                o = 512 * h + w * k
                cp(A("z32", o, o + w), A("zt", o, o + w), OPT["z32"][h][k], 32.0)
            for b in range(4):
                o = YS * b + 128 * h
                tt(A("yw", o, o + 128), A("ps%d" % (4 * h + b), 0, 128), A("z32", 512 * h + b, 512 * h + 512, 4), Op.add)
                follow("y")
        for b in range(4):
            cp(A("ft", b, 4 * NT, 4), G(A("yw", YS * b, YS * b + 256), A("uf", 0, 6)), OPT["f"][b], 0.03125)
        quant("qf", "sf", 128 * rd, 128, A("ft"))
        at_ = NT * (2 - rd)
        send(peer, A("qa", at_, at_ + NT), A("qf", 128 * rd, 128 * rd + NT), "f%d_" % rd, codes=True)
        send(peer, A("sa", at_, at_ + NT), A("sf", 128 * rd, 128 * rd + NT), "f%d_" % rd)
        arrive(peer, [A("qa", at_, at_ + NT), A("sa", at_, at_ + NT)], "f%d_" % rd, 2, OPT["far"])
        for b in range(4):
            cp(half("f16", b, NT), A("ft", b, 4 * NT, 4), "s", 16.0)
        ts(A("t3", 0, 16), A("t2"), A("pre"), Op.add, NT + 0.5, Op.is_lt)
        ts(A("t3", 16, 32), A("t2"), A("pre"), Op.add, 255.0, Op.add)
        tt(A("t1"), A("t3", 0, 16), A("t3", 16, 32), Op.mult)
        for k in range(2):
            tt(half("xd", k, 16), A("t1"), A("sg"), Op.max)
        tr(A("xt"), A("xd"))
        cp(A("ux"), G(A("xt"), tab("p32", 0, 1)))
        if rd < 2:
            cp(A("wh", lo + 16, lo + 32), ends("ls"), OPT["wh"])
            prepare(rd + 1)
        else:
            cp(A("opf"), A("uz"))
            store("y", T.op[:], T.opf[:], A("opf"))
        if rd == 1:
            quant("qv", "sv", 0, 128, A("vt"))
        for b in (0, 2, 1, 3):
            mm("ps%d" % (2 + b), "qe", "se", 128 * b, "qa", "sa", at_, 128)
        for b in (0, 2, 1, 3):
            tt(A("yw", YS * b + 256, YS * b + YS), A("ps%d" % (2 + b), 0, NT), half("f16", b, NT), Op.add)
            follow("m")
        wq, wsc, res = ("qu2", "su2", "ssb") if rd < 2 else ("qv", "sv", "ysb")
        for h in range(2):
            for b in range(4):
                cp(A("xs", 512 * h + b, 512 * h + 512, 4), G(half("yw", b, YS), half("ux", h, 8)), OPT["x"][4 * h + b], 0.03125)
                follow("x")
            quant("qx", "sx", 128 * h, 128, half("xs", h, 512))
            mm("ps%d" % h, wq, wsc, 0, "qx", "sx", 128 * h, 128)
            cp(half(res, h, 128), A("ps%d" % h, 0, 128), OPT["s"][h])

    store("y", T.oc[:, 0:512], T.qx[:, 0:128].bitcast(dt.uint8), A("qx", 0, 128))
    store("s", T.y[:, 0:128], T.ysb[:, 0:128], A("ysb", 0, 128))
    store("y", T.oc[:, 512:1024], T.qx[:, 128:256].bitcast(dt.uint8), A("qx", 128, 256))
    for k in range(4):
        store("y" if k < 1 else "s", T.osc[4 * k:4 * k + 4, :], T.sx[32 * k:32 * k + 4, :], A("sx"))
    store("y", T.y[:, 128:256], T.ysb[:, 128:256], A("ysb", 128, 256))
    rec("y", None, [], [], after=stores)
    emit(g, T, ops)
    g.wait_ge(T.sem.sent, sent[0])
